import numpy as np
import ml_dtypes


def mxq(x, axis, fmt="e4m3"):
    dtype, down = {"e4m3": (ml_dtypes.float8_e4m3fn, 7), "e5m2": (ml_dtypes.float8_e5m2, 14)}[fmt]
    v = np.moveaxis(np.asarray(x, np.float32).astype(ml_dtypes.bfloat16).astype(np.float64), axis, -1)
    blocks = v.reshape(v.shape[:-1] + (-1, 32))
    amax = np.abs(blocks).max(-1, keepdims=True)
    byte = np.maximum(np.where(amax > 0, np.frexp(amax)[1] - 1 + 127, 0) - down, 1)
    scale = np.exp2(byte - 127.0)
    codes = (blocks / scale).astype(np.float32).astype(dtype).astype(np.float64)
    return np.moveaxis((codes * scale).reshape(v.shape), -1, axis)


WIDE = False


def mx_kscale(k):
    if not WIDE:
        return np.ones(k)
    levels = np.array([10, -10, 5, -5, 0])
    if k % 512:
        return np.exp2(np.random.permutation(np.resize(levels, k // 32))).repeat(32)
    a = np.empty((k // 512, 16))
    for p in range(k // 512):
        a[p, :8] = np.random.permutation(np.resize(levels, 8))
        for g in range(8):
            far = levels[np.abs(levels - a[p, g]) >= 10]
            a[p, g + 8] = far[np.random.randint(len(far))]
    return np.exp2(a.ravel()).repeat(32)


def f64(x):
    return np.asarray(x).astype(np.float64)


def striped(idx):
    return np.tile(idx.reshape(-1, 16).T, (8, 1)).astype(np.uint16)


def unstriped(offs):
    return offs[:16].T.reshape(-1).astype(np.int64)


E2M1 = np.array([0.0, 0.5, 1.0, 1.5, 2.0, 3.0, 4.0, 6.0, -0.0, -0.5, -1.0, -1.5, -2.0, -3.0, -4.0, -6.0])


def pack_weight(w, fmt):
    k, n = w.shape
    w = f64(np.asarray(w, np.float32).astype(ml_dtypes.bfloat16)).reshape(k // 32, 32, n)
    amax = np.abs(w).max(1)
    if fmt == "e4m3":
        byte = np.frexp(amax)[1] - 1 + 127 - 7
    else:
        mant, ex = np.frexp(amax / 6.0)
        byte = np.where(mant > 0.5, ex, ex - 1) + 127
    byte = np.clip(np.where(amax > 0, byte, 1), 1, 254)
    scaled = (w * np.exp2(127.0 - byte)[:, None, :]).reshape(k, n).astype(np.float32)
    by_word = np.ascontiguousarray(scaled.reshape(k // 512, 128, 4, n).transpose(0, 1, 3, 2))
    if fmt == "e4m3":
        words = by_word.astype(ml_dtypes.float8_e4m3fn).view(np.uint8)
    else:
        c = by_word.astype(ml_dtypes.float4_e2m1fn).view(np.uint8) & 0xF
        words = (c[..., 0::2] | (c[..., 1::2] << 4)).reshape(k // 512, 128, 2 * n)
    return np.ascontiguousarray(words), np.ascontiguousarray(byte.astype(np.uint8).reshape(k // 512, 16, n))


def unpack_weight(words, scales, fmt):
    g, _, n = scales.shape
    words = np.ascontiguousarray(words).reshape(g, 128, n, -1)
    if fmt == "e4m3":
        vals = words.view(ml_dtypes.float8_e4m3fn).astype(np.float64)
    else:
        nib = np.empty((g, 128, n, 4), np.uint8)
        nib[..., 0::2] = words & 0xF
        nib[..., 1::2] = words >> 4
        vals = E2M1[nib]
    vals = vals * np.repeat(np.exp2(scales.astype(np.float64) - 127.0), 8, axis=1)[..., None]
    return vals.transpose(0, 1, 3, 2).reshape(g * 512, n)


def silu(v):
    return v / (1.0 + np.exp(-np.maximum(v, -700.0)))


K, T, E, C, H, N = 1024, 512, 4, 128, 512, 256


def by_expert(wq, xq):
    return np.concatenate([wq[e].T @ xq[:, e * C:(e + 1) * C] for e in range(E)], axis=1)


def setup_inputs():
    n = np.random.standard_normal
    s = mx_kscale(K)
    u = mx_kscale(H)
    slot_token = np.random.permutation(T)[:E * C]
    partner = np.concatenate([np.random.permutation(T) for _ in range(-(-E * C // T))])[:E * C]
    x = pack_weight(n((K, T)) * s[:, None], "e4m3")
    wp = [pack_weight(m, "e2m1") for m in n((E, K, H)) / np.sqrt(K) / s[None, :, None] * u]
    return {
        "x_words": x[0],
        "x_scales": x[1],
        "w1": (n((E, K, H)) / np.sqrt(K) / s[None, :, None] * u).astype(np.float32),
        "wp_words": np.stack([m[0] for m in wp]),
        "wp_scales": np.stack([m[1] for m in wp]),
        "w2": (n((E, H, N)) / np.sqrt(H) / u[None, :, None]).astype(np.float32),
        "gate": np.tile(np.random.uniform(0.2, 1.0, E * C), (128, 1)).astype(np.float32),
        "offs": striped(slot_token),
        "offs2": striped(partner),
    }


def reference(x_words, x_scales, w1, wp_words, wp_scales, w2, gate, offs, offs2):
    w1q = mxq(f64(w1), 1, "e4m3")
    wp = np.stack([unpack_weight(wp_words[e], wp_scales[e], "e2m1") for e in range(E)])
    w2q = mxq(f64(w2), 1, "e4m3")
    idx, idx2 = unstriped(offs), unstriped(offs2)
    x = unpack_weight(x_words, x_scales, "e4m3")
    h = silu(by_expert(w1q, x[:, idx]) + by_expert(wp, x[:, idx2]))
    y = by_expert(w2q, mxq(h, 0, "e4m3"))
    out = np.zeros((N, T))
    out[:, idx] = f64(gate[:1]) * y
    return out

@@ -1,0 +1,257 @@
+from contextlib import ExitStack
+
+import concourse.mybir as mybir
+from concourse.masks import make_identity
+
+K, T, E, C, H, N = 1024, 512, 4, 128, 512, 256
+FLOPS = 2 * E * C * (2 * K * H + H * N)
+
+F32 = mybir.dt.float32
+BF16 = mybir.dt.bfloat16
+I32 = mybir.dt.int32
+U32 = mybir.dt.uint32
+U16 = mybir.dt.uint16
+U8 = mybir.dt.uint8
+FP8X4 = mybir.dt.float8_e4m3fn_x4
+FP4X4 = mybir.dt.float4_e2m1fn_x4
+SILU = mybir.ActivationFunctionType.Silu
+MULT = mybir.AluOpType.mult
+
+P = 128
+PACK = 4
+K_PASS = P * PACK
+PASSES = K // K_PASS
+GATHER = 256
+
+
+def cast_interleave(engine_copy, grouped, raw, c0, c1):
+    engine_copy(
+        out=grouped[:, c0 * PACK : c1 * PACK].rearrange("p (c i j) -> p c j i", i=4, j=PACK),
+        in_=raw[:, :, c0:c1].rearrange("p j (c i) -> p c j i", i=4),
+    )
+
+
+def tile_moe_duo_silu_kernel(
+    tc, x_words, x_scales, w1, wp_words, wp_scales, w2, gate, offs, offs2, out
+):
+    nc = tc.nc
+    with ExitStack() as ctx:
+        keep = ctx.enter_context(tc.tile_pool(name="keep", bufs=1))
+        psum = ctx.enter_context(tc.psum_pool(name="psum", bufs=2))
+
+        xs = keep.tile([P, PASSES * T], U8, name="xs", align_bytes=64)
+        wps = keep.tile([P, E * PASSES * H], U8, name="wps", align_bytes=64)
+        nc.vector.memset(xs[:].bitcast(I32), 0)
+        warm = keep.tile([P, 1], F32, name="warm")
+        nc.vector.memset(warm[:], 0.0)
+        nc.scalar.activation(out=warm[:], in_=warm[:], func=SILU)
+        nc.vector.memset(wps[:].bitcast(I32), 0)
+        ident = keep.tile([P, P], F32, name="ident")
+        make_identity(nc, ident[:])
+
+        tok_list = keep.tile([P, T // 16], U16, name="tok_list")
+        par_list = keep.tile([P, T // 16], U16, name="par_list")
+        xw = [keep.tile([P, T], U32, name="xw%d" % s, align_bytes=64) for s in range(PASSES)]
+        w1_raw = {}
+        w2_raw = {}
+        wpw = {}
+        gate_sb = keep.tile([P, E * C], F32, name="gate_sb")
+
+        def load_x(s):
+            nc.sync.dma_start(out=xw[s][:].bitcast(I32), in_=x_words[s].rearrange("p t d -> p (t d)").bitcast(I32))
+
+        def load_w1(e, s, c0, c1):
+            raw = keep.tile([P, PACK, c1 - c0], F32, name="w1raw%d_%d_%d" % (e, s, c0))
+            rows = w1[e, s * K_PASS : (s + 1) * K_PASS, c0:c1]
+            nc.sync.dma_start(out=raw[:], in_=rows.rearrange("(p j) w -> p j w", j=PACK))
+            w1_raw.setdefault((e, s), []).append((raw, c0, c1))
+
+        def load_w2(e):
+            raw = keep.tile([P, PACK, N], F32, name="w2raw%d" % e)
+            nc.sync.dma_start(out=raw[:], in_=w2[e].rearrange("(p j) w -> p j w", j=PACK))
+            w2_raw[e] = raw
+
+        def load_wp(e):
+            words = keep.tile([P, PASSES * 2 * H], U8, name="wpw%d" % e, align_bytes=64)
+            nc.sync.dma_start(
+                out=words[:].bitcast(I32).rearrange("p (s n) -> p s n", s=PASSES),
+                in_=wp_words[e].bitcast(I32).rearrange("s p n -> p s n"),
+            )
+            wpw[e] = words
+
+        nc.sync.dma_start(tok_list[:], offs)
+        load_x(0)
+        nc.sync.dma_start(par_list[:], offs2)
+        xs_rows = x_scales.bitcast(I32).rearrange("s (q r) n -> r q s n", r=4)
+        for r in range(4):
+            nc.sync.dma_start(
+                out=xs[r:P:32, :].bitcast(I32).rearrange("q (s n) -> q s n", s=PASSES), in_=xs_rows[r]
+            )
+        load_x(1)
+        load_w1(0, 0, 0, 512)
+        wps_rows = wp_scales.bitcast(I32).rearrange("e s (q r) n -> r q (e s) n", r=4)
+        for r in range(4):
+            nc.sync.dma_start(
+                out=wps[r:P:32, :].bitcast(I32).rearrange("q (g n) -> q g n", g=E * PASSES), in_=wps_rows[r]
+            )
+        load_wp(0)
+        load_w1(0, 1, 0, 512)
+        nc.sync.dma_start(out=gate_sb[:], in_=gate)
+        load_w1(1, 0, 0, 512)
+        load_w2(0)
+        load_wp(1)
+        load_w1(1, 1, 0, 512)
+        load_w1(2, 0, 0, 512)
+        load_w2(1)
+        load_wp(2)
+        load_w1(2, 1, 0, 512)
+        load_w1(3, 0, 0, 512)
+        load_w1(3, 1, 0, 256)
+        load_w1(3, 1, 256, 512)
+        load_wp(3)
+        load_w2(2)
+        load_w2(3)
+
+        tok_words = [keep.tile([P, E * C], U32, name="tokw%d" % s, align_bytes=64) for s in range(PASSES)]
+        par_words = [keep.tile([P, E * C], U32, name="parw%d" % s, align_bytes=64) for s in range(PASSES)]
+        tok_scales = [keep.tile([P, E * C], U8, name="toks%d" % s, align_bytes=64) for s in range(PASSES)]
+        par_scales = [keep.tile([P, E * C], U8, name="pars%d" % s, align_bytes=64) for s in range(PASSES)]
+
+        def gather(half):
+            slots = slice(half * GATHER, (half + 1) * GATHER)
+            cols = slice(half * GATHER // 16, (half + 1) * GATHER // 16)
+            for s in range(PASSES):
+                nc.vector.tensor_copy(tok_words[s][:, slots], xw[s][:].indirect(tok_list[:, cols]))
+                nc.vector.tensor_copy(par_words[s][:, slots], xw[s][:].indirect(par_list[:, cols]))
+            for s in range(PASSES):
+                nc.vector.tensor_copy(par_scales[s][:, slots], xs[:, s * T : (s + 1) * T].indirect(par_list[:, cols]))
+            for s in range(PASSES):
+                nc.vector.tensor_copy(tok_scales[s][:, slots], xs[:, s * T : (s + 1) * T].indirect(tok_list[:, cols]))
+
+        w1_codes = {}
+        w2_codes = {}
+        h_codes = {}
+
+        def quantize_w1(e, s, vector_share):
+            codes = keep.tile([P, H], U32, name="w1c%d_%d" % (e, s), align_bytes=64)
+            scales = keep.tile([P, H], U8, name="w1s%d_%d" % (e, s), align_bytes=64)
+            for raw, c0, c1 in w1_raw[(e, s)]:
+                width = c1 - c0
+                grouped = keep.tile([P, width * PACK], BF16, name="w1g%d_%d_%d" % (e, s, c0), align_bytes=64)
+                cut = width - int(width * vector_share) // 8 * 8
+                cast_interleave(nc.scalar.copy, grouped, raw, 0, cut)
+                if cut < width:
+                    cast_interleave(nc.vector.tensor_copy, grouped, raw, cut, width)
+                nc.vector.quantize_mx(out=codes[:, c0:c1].bitcast(FP8X4), scales=scales[:, c0:c1], in_=grouped[:])
+            w1_codes[(e, s)] = (codes, scales)
+
+        def quantize_w2(e, vector_share):
+            codes = keep.tile([P, N], U32, name="w2c%d" % e, align_bytes=64)
+            scales = keep.tile([P, N], U8, name="w2s%d" % e, align_bytes=64)
+            grouped = keep.tile([P, N * PACK], BF16, name="w2g%d" % e, align_bytes=64)
+            cut = N - int(N * vector_share) // 8 * 8
+            cast_interleave(nc.scalar.copy, grouped, w2_raw[e], 0, cut)
+            if cut < N:
+                cast_interleave(nc.vector.tensor_copy, grouped, w2_raw[e], cut, N)
+            nc.vector.quantize_mx(out=codes[:].bitcast(FP8X4), scales=scales[:], in_=grouped[:])
+            w2_codes[e] = (codes, scales)
+
+        def hidden(e, partner_last):
+            slots = slice(e * C, (e + 1) * C)
+            acc = psum.tile([P, H], F32, name="acc")
+            own = []
+            partner = []
+            for s in range(PASSES):
+                codes, scales = w1_codes[(e, s)]
+                own.append((tok_words[s][:, slots], tok_scales[s][:, slots], codes[:].bitcast(FP8X4), scales[:]))
+                g = e * PASSES + s
+                partner.append(
+                    (
+                        par_words[s][:, slots],
+                        par_scales[s][:, slots],
+                        wpw[e][:, s * 2 * H : (s + 1) * 2 * H].bitcast(FP4X4),
+                        wps[:, g * H : (g + 1) * H],
+                    )
+                )
+            passes = [own[0]] + partner + [own[1]] if partner_last else partner + own
+            for n, (words, word_scales, weights, weight_scales) in enumerate(passes):
+                nc.tensor.matmul_mx(
+                    out=acc[:],
+                    lhsT=words.bitcast(FP8X4),
+                    lhsT_scale=word_scales,
+                    rhs=weights,
+                    rhs_scale=weight_scales,
+                    start=(n == 0),
+                    stop=(n == len(passes) - 1),
+                )
+            h_rows = keep.tile([P, H], BF16, name="hrows%d" % e, align_bytes=64)
+            nc.scalar.activation(
+                out=h_rows[:].rearrange("c (u p d) -> c u p d", u=2, d=2),
+                in_=acc[:].rearrange("c (p u d) -> c u p d", u=2, d=2),
+                func=SILU,
+            )
+            turned = psum.tile([P, 2, C], F32, name="turned")
+            pairs = h_rows[:].bitcast(F32)
+            for u in range(2):
+                nc.tensor.transpose(turned[:, u, :], pairs[:, u * P : (u + 1) * P], ident[:])
+            grouped = keep.tile([P, C * PACK], BF16, name="hg%d" % e, align_bytes=64)
+            nc.scalar.copy(
+                out=grouped[:].bitcast(F32).rearrange("p (c u) -> p c u", u=2),
+                in_=turned[:].rearrange("p u c -> p c u"),
+            )
+            codes = keep.tile([P, C], U32, name="hc%d" % e, align_bytes=64)
+            scales = keep.tile([P, C], U8, name="hs%d" % e, align_bytes=64)
+            nc.vector.quantize_mx(out=codes[:].bitcast(FP8X4), scales=scales[:], in_=grouped[:])
+            h_codes[e] = (codes, scales)
+
+        result = [keep.tile([P, T], F32, name="result%d" % b) for b in range(N // P)]
+
+        def second(e):
+            slots = slice(e * C, (e + 1) * C)
+            y = psum.tile([P, N // P, C], F32, name="y")
+            w_codes, w_scales = w2_codes[e]
+            codes, scales = h_codes[e]
+            for b in range(N // P):
+                nc.tensor.matmul_mx(
+                    out=y[:, b, :],
+                    lhsT=w_codes[:, b * P : (b + 1) * P].bitcast(FP8X4),
+                    lhsT_scale=w_scales[:, b * P : (b + 1) * P],
+                    rhs=codes[:].bitcast(FP8X4),
+                    rhs_scale=scales[:],
+                    start=True,
+                    stop=True,
+                )
+            y_sb = keep.tile([P, N // P, C], F32, name="ysb%d" % e)
+            if e == E - 1:
+                for b in range(N // P):
+                    nc.scalar.copy(out=y_sb[:, b, :], in_=y[:, b, :])
+            else:
+                nc.scalar.copy(out=y_sb[:], in_=y[:])
+            cols = slice(e * C // 16, (e + 1) * C // 16)
+            for b in range(N // P):
+                nc.vector.tensor_tensor(result[b][:].indirect(tok_list[:, cols]), y_sb[:, b, :], gate_sb[:, slots], MULT)
+
+        gather(0)
+        quantize_w1(0, 0, 0.0)
+        quantize_w1(0, 1, 0.0)
+        gather(1)
+        hidden(0, False)
+        quantize_w1(1, 0, 0.0)
+        quantize_w2(0, 0.0)
+        second(0)
+        quantize_w1(1, 1, 0.375)
+        hidden(1, False)
+        quantize_w1(2, 0, 0.375)
+        quantize_w2(1, 0.375)
+        second(1)
+        quantize_w1(2, 1, 0.375)
+        hidden(2, False)
+        quantize_w1(3, 0, 0.375)
+        quantize_w1(3, 1, 0.5)
+        hidden(3, True)
+        quantize_w2(2, 0.5)
+        second(2)
+        quantize_w2(3, 0.25)
+        second(3)
+        for b in range(N // P):
+            nc.sync.dma_start(out=out[b * P : (b + 1) * P, :], in_=result[b][:])

@@ -21,7 +21,7 @@ P = 128
 PACK = 4
 K_PASS = P * PACK
 PASSES = K // K_PASS
-GATHER = 256
+WINDOW = 704
 
 
 def cast_interleave(engine_copy, grouped, raw, c0, c1):
@@ -38,8 +38,9 @@ def tile_moe_duo_silu_kernel(
     with ExitStack() as ctx:
         keep = ctx.enter_context(tc.tile_pool(name="keep", bufs=1))
         psum = ctx.enter_context(tc.psum_pool(name="psum", bufs=2))
+        psum_acc = ctx.enter_context(tc.psum_pool(name="psum_acc", bufs=2))
 
-        xs = keep.tile([P, PASSES * T], U8, name="xs", align_bytes=64)
+        xs = keep.tile([P, T + WINDOW], U8, name="xs", align_bytes=64)
         wps = keep.tile([P, E * PASSES * H], U8, name="wps", align_bytes=64)
         nc.vector.memset(xs[:].bitcast(I32), 0)
         warm = keep.tile([P, 1], F32, name="warm")
@@ -51,14 +52,16 @@ def tile_moe_duo_silu_kernel(
 
         tok_list = keep.tile([P, T // 16], U16, name="tok_list")
         par_list = keep.tile([P, T // 16], U16, name="par_list")
-        xw = [keep.tile([P, T], U32, name="xw%d" % s, align_bytes=64) for s in range(PASSES)]
+        xw = [keep.tile([P, WINDOW], I32, name="xw%d" % s, align_bytes=64) for s in range(PASSES)]
+        for s in range(PASSES):
+            nc.vector.memset(xw[s][:, T:WINDOW], 0)
         w1_raw = {}
         w2_raw = {}
         wpw = {}
-        gate_sb = keep.tile([P, E * C], F32, name="gate_sb")
+        gate_sb = [keep.tile([P, 2 * C], F32, name="gate_sb%d" % g) for g in range(2)]
 
         def load_x(s):
-            nc.sync.dma_start(out=xw[s][:].bitcast(I32), in_=x_words[s].rearrange("p t d -> p (t d)").bitcast(I32))
+            nc.sync.dma_start(out=xw[s][:, 0:T], in_=x_words[s].rearrange("p t d -> p (t d)").bitcast(I32))
 
         def load_w1(e, s, c0, c1):
             raw = keep.tile([P, PACK, c1 - c0], F32, name="w1raw%d_%d_%d" % (e, s, c0))
@@ -84,174 +87,223 @@ def tile_moe_duo_silu_kernel(
         nc.sync.dma_start(par_list[:], offs2)
         xs_rows = x_scales.bitcast(I32).rearrange("s (q r) n -> r q s n", r=4)
         for r in range(4):
-            nc.sync.dma_start(
-                out=xs[r:P:32, :].bitcast(I32).rearrange("q (s n) -> q s n", s=PASSES), in_=xs_rows[r]
-            )
+            nc.sync.dma_start(out=xs[r:P:32, 0 : PASSES * T].bitcast(I32).rearrange("q (s n) -> q s n", s=PASSES), in_=xs_rows[r])
         load_x(1)
         load_w1(0, 0, 0, 512)
+        load_w1(0, 1, 0, 512)
         wps_rows = wp_scales.bitcast(I32).rearrange("e s (q r) n -> r q (e s) n", r=4)
         for r in range(4):
-            nc.sync.dma_start(
-                out=wps[r:P:32, :].bitcast(I32).rearrange("q (g n) -> q g n", g=E * PASSES), in_=wps_rows[r]
-            )
-        load_wp(0)
-        load_w1(0, 1, 0, 512)
-        nc.sync.dma_start(out=gate_sb[:], in_=gate)
+            nc.sync.dma_start(out=wps[r:P:32, :].bitcast(I32).rearrange("q (g n) -> q g n", g=E * PASSES), in_=wps_rows[r])
         load_w1(1, 0, 0, 512)
+        load_wp(0)
+        load_w1(1, 1, 0, 512)
         load_w2(0)
         load_wp(1)
-        load_w1(1, 1, 0, 512)
+        nc.sync.dma_start(out=gate_sb[0][:], in_=gate[:, 0:256])
         load_w1(2, 0, 0, 512)
+        load_w1(2, 1, 0, 512)
         load_w2(1)
         load_wp(2)
-        load_w1(2, 1, 0, 512)
         load_w1(3, 0, 0, 512)
-        load_w1(3, 1, 0, 256)
-        load_w1(3, 1, 256, 512)
+        load_w1(3, 1, 0, 512)
         load_wp(3)
         load_w2(2)
         load_w2(3)
+        nc.sync.dma_start(out=gate_sb[1][:], in_=gate[:, 256:512])
 
         tok_words = [keep.tile([P, E * C], U32, name="tokw%d" % s, align_bytes=64) for s in range(PASSES)]
         par_words = [keep.tile([P, E * C], U32, name="parw%d" % s, align_bytes=64) for s in range(PASSES)]
-        tok_scales = [keep.tile([P, E * C], U8, name="toks%d" % s, align_bytes=64) for s in range(PASSES)]
+        tok_scales = [keep.tile([P, E * C], U8, name="toks%d" % s, align_bytes=64) for s in range(2)]
         par_scales = [keep.tile([P, E * C], U8, name="pars%d" % s, align_bytes=64) for s in range(PASSES)]
+        plan = {"A0":[["S",256],["S",256]],"B0":[["S",256],["S",256]],"A1":[["S",256],["S",256]],"B1":[["S",256],["V",256]],"A2":[["S",256],["S",256]],"B2":[["S",256],["V",256]],"A3":[["S",256],["V",256]],"B3":[["S",256],["V",256]],"C0":[["S",256]],"C1":[["S",256]],"C2":[["S",256]],"C3":[["S",256]]}
+        holds = {}
+        staged = {}
+        quantized = {}
+        accs = {}
+        turns = {}
+        hgs = {}
+        ys = {}
+        ysbs = {}
+        result = [keep.tile([P, T], F32, name="result%d" % b) for b in range(N // P)]
 
-        def gather(half):
-            slots = slice(half * GATHER, (half + 1) * GATHER)
-            cols = slice(half * GATHER // 16, (half + 1) * GATHER // 16)
+        def gath():
             for s in range(PASSES):
-                nc.vector.tensor_copy(tok_words[s][:, slots], xw[s][:].indirect(tok_list[:, cols]))
-                nc.vector.tensor_copy(par_words[s][:, slots], xw[s][:].indirect(par_list[:, cols]))
+                nc.vector.tensor_copy(tok_words[s][:], xw[s][:].bitcast(U32).indirect(tok_list[:]))
+                nc.vector.tensor_copy(par_words[s][:], xw[s][:].bitcast(U32).indirect(par_list[:]))
             for s in range(PASSES):
-                nc.vector.tensor_copy(par_scales[s][:, slots], xs[:, s * T : (s + 1) * T].indirect(par_list[:, cols]))
+                nc.vector.tensor_copy(par_scales[s][:], xs[:, s * T : s * T + WINDOW].indirect(par_list[:]))
             for s in range(PASSES):
-                nc.vector.tensor_copy(tok_scales[s][:, slots], xs[:, s * T : (s + 1) * T].indirect(tok_list[:, cols]))
+                nc.vector.tensor_copy(tok_scales[s][:], xs[:, s * T : s * T + WINDOW].indirect(tok_list[:]))
 
-        w1_codes = {}
-        w2_codes = {}
-        h_codes = {}
+        def source(name, c0):
+            e = int(name[1])
+            if name[0] == "C":
+                return w2_raw[e], c0
+            for raw, a, b in w1_raw[(e, 0 if name[0] == "A" else 1)]:
+                if a <= c0 < b:
+                    return raw, c0 - a
 
-        def quantize_w1(e, s, vector_share):
-            codes = keep.tile([P, H], U32, name="w1c%d_%d" % (e, s), align_bytes=64)
-            scales = keep.tile([P, H], U8, name="w1s%d_%d" % (e, s), align_bytes=64)
-            for raw, c0, c1 in w1_raw[(e, s)]:
-                width = c1 - c0
-                grouped = keep.tile([P, width * PACK], BF16, name="w1g%d_%d_%d" % (e, s, c0), align_bytes=64)
-                cut = width - int(width * vector_share) // 8 * 8
-                cast_interleave(nc.scalar.copy, grouped, raw, 0, cut)
-                if cut < width:
-                    cast_interleave(nc.vector.tensor_copy, grouped, raw, cut, width)
-                nc.vector.quantize_mx(out=codes[:, c0:c1].bitcast(FP8X4), scales=scales[:, c0:c1], in_=grouped[:])
-            w1_codes[(e, s)] = (codes, scales)
+        def c(name, i, group=None):
+            eng, cols = plan[name][i]
+            c0 = sum(x[1] for x in plan[name][:i])
+            first = i if group is None else group[0]
+            key = name + str(first)
+            if key not in staged:
+                width = cols if group is None else sum(plan[name][j][1] for j in group)
+                staged[key] = keep.tile([P, width * PACK], BF16, name="g" + key, tag=holds.get(key, "g" + key), align_bytes=64)
+            off = c0 - sum(x[1] for x in plan[name][:first])
+            raw, r0 = source(name, c0)
+            copy = nc.scalar.copy if eng == "S" else nc.vector.tensor_copy
+            copy(
+                out=staged[key][:, off * PACK : (off + cols) * PACK].rearrange("p (c i j) -> p c j i", i=4, j=PACK),
+                in_=raw[:, :, r0 : r0 + cols].rearrange("p j (c i) -> p c j i", i=4),
+            )
 
-        def quantize_w2(e, vector_share):
-            codes = keep.tile([P, N], U32, name="w2c%d" % e, align_bytes=64)
-            scales = keep.tile([P, N], U8, name="w2s%d" % e, align_bytes=64)
-            grouped = keep.tile([P, N * PACK], BF16, name="w2g%d" % e, align_bytes=64)
-            cut = N - int(N * vector_share) // 8 * 8
-            cast_interleave(nc.scalar.copy, grouped, w2_raw[e], 0, cut)
-            if cut < N:
-                cast_interleave(nc.vector.tensor_copy, grouped, w2_raw[e], cut, N)
-            nc.vector.quantize_mx(out=codes[:].bitcast(FP8X4), scales=scales[:], in_=grouped[:])
-            w2_codes[e] = (codes, scales)
+        def q(name, first):
+            if name not in quantized:
+                width = N if name[0] == "C" else H
+                codes = keep.tile([P, width], U32, name="codes" + name, tag="codes" + name, align_bytes=64)
+                scales = keep.tile([P, width], U8, name="scales" + name, align_bytes=64)
+                quantized[name] = (codes, scales)
+            codes, scales = quantized[name]
+            grouped = staged[name + str(first)]
+            c0 = sum(x[1] for x in plan[name][:first])
+            c1 = c0 + grouped.shape[1] // PACK
+            nc.vector.quantize_mx(out=codes[:, c0:c1].bitcast(FP8X4), scales=scales[:, c0:c1], in_=grouped[:])
 
-        def hidden(e, partner_last):
+        def mm1(e, partner_last=False):
             slots = slice(e * C, (e + 1) * C)
-            acc = psum.tile([P, H], F32, name="acc")
+            acc = psum_acc.tile([P, H], F32, name="acc")
             own = []
             partner = []
             for s in range(PASSES):
-                codes, scales = w1_codes[(e, s)]
+                codes, scales = quantized["AB"[s] + str(e)]
                 own.append((tok_words[s][:, slots], tok_scales[s][:, slots], codes[:].bitcast(FP8X4), scales[:]))
                 g = e * PASSES + s
-                partner.append(
-                    (
-                        par_words[s][:, slots],
-                        par_scales[s][:, slots],
-                        wpw[e][:, s * 2 * H : (s + 1) * 2 * H].bitcast(FP4X4),
-                        wps[:, g * H : (g + 1) * H],
-                    )
-                )
+                partner.append((par_words[s][:, slots], par_scales[s][:, slots], wpw[e][:, s * 2 * H : (s + 1) * 2 * H].bitcast(FP4X4), wps[:, g * H : (g + 1) * H]))
             passes = [own[0]] + partner + [own[1]] if partner_last else partner + own
             for n, (words, word_scales, weights, weight_scales) in enumerate(passes):
-                nc.tensor.matmul_mx(
-                    out=acc[:],
-                    lhsT=words.bitcast(FP8X4),
-                    lhsT_scale=word_scales,
-                    rhs=weights,
-                    rhs_scale=weight_scales,
-                    start=(n == 0),
-                    stop=(n == len(passes) - 1),
-                )
-            h_rows = keep.tile([P, H], BF16, name="hrows%d" % e, align_bytes=64)
+                nc.tensor.matmul_mx(out=acc[:], lhsT=words.bitcast(FP8X4), lhsT_scale=word_scales, rhs=weights, rhs_scale=weight_scales, start=(n == 0), stop=(n == len(passes) - 1))
+            accs[e] = acc
+
+        def silu(e):
+            h_rows = keep.tile([P, H], BF16, name="hrows%d" % e, tag="hrows%d" % e, align_bytes=64)
             nc.scalar.activation(
                 out=h_rows[:].rearrange("c (u p d) -> c u p d", u=2, d=2),
-                in_=acc[:].rearrange("c (p u d) -> c u p d", u=2, d=2),
+                in_=accs[e][:].rearrange("c (p u d) -> c u p d", u=2, d=2),
                 func=SILU,
             )
             turned = psum.tile([P, 2, C], F32, name="turned")
             pairs = h_rows[:].bitcast(F32)
             for u in range(2):
                 nc.tensor.transpose(turned[:, u, :], pairs[:, u * P : (u + 1) * P], ident[:])
-            grouped = keep.tile([P, C * PACK], BF16, name="hg%d" % e, align_bytes=64)
-            nc.scalar.copy(
-                out=grouped[:].bitcast(F32).rearrange("p (c u) -> p c u", u=2),
-                in_=turned[:].rearrange("p u c -> p c u"),
-            )
+            turns[e] = turned
+
+        def hc(e):
+            grouped = keep.tile([P, C * PACK], BF16, name="hg%d" % e, tag="hg%d" % e, align_bytes=64)
+            nc.scalar.copy(out=grouped[:].bitcast(F32).rearrange("p (c u) -> p c u", u=2), in_=turns[e][:].rearrange("p u c -> p c u"))
+            hgs[e] = grouped
+
+        def qh(e):
             codes = keep.tile([P, C], U32, name="hc%d" % e, align_bytes=64)
             scales = keep.tile([P, C], U8, name="hs%d" % e, align_bytes=64)
-            nc.vector.quantize_mx(out=codes[:].bitcast(FP8X4), scales=scales[:], in_=grouped[:])
-            h_codes[e] = (codes, scales)
+            nc.vector.quantize_mx(out=codes[:].bitcast(FP8X4), scales=scales[:], in_=hgs[e][:])
+            quantized["h%d" % e] = (codes, scales)
 
-        result = [keep.tile([P, T], F32, name="result%d" % b) for b in range(N // P)]
-
-        def second(e):
-            slots = slice(e * C, (e + 1) * C)
+        def mm2(e):
             y = psum.tile([P, N // P, C], F32, name="y")
-            w_codes, w_scales = w2_codes[e]
-            codes, scales = h_codes[e]
+            w_codes, w_scales = quantized["C%d" % e]
+            codes, scales = quantized["h%d" % e]
             for b in range(N // P):
-                nc.tensor.matmul_mx(
-                    out=y[:, b, :],
-                    lhsT=w_codes[:, b * P : (b + 1) * P].bitcast(FP8X4),
-                    lhsT_scale=w_scales[:, b * P : (b + 1) * P],
-                    rhs=codes[:].bitcast(FP8X4),
-                    rhs_scale=scales[:],
-                    start=True,
-                    stop=True,
-                )
-            y_sb = keep.tile([P, N // P, C], F32, name="ysb%d" % e)
-            if e == E - 1:
-                for b in range(N // P):
-                    nc.scalar.copy(out=y_sb[:, b, :], in_=y[:, b, :])
-            else:
-                nc.scalar.copy(out=y_sb[:], in_=y[:])
-            cols = slice(e * C // 16, (e + 1) * C // 16)
-            for b in range(N // P):
-                nc.vector.tensor_tensor(result[b][:].indirect(tok_list[:, cols]), y_sb[:, b, :], gate_sb[:, slots], MULT)
+                nc.tensor.matmul_mx(out=y[:, b, :], lhsT=w_codes[:, b * P : (b + 1) * P].bitcast(FP8X4), lhsT_scale=w_scales[:, b * P : (b + 1) * P], rhs=codes[:].bitcast(FP8X4), rhs_scale=scales[:], start=True, stop=True)
+            ys[e] = y
 
-        gather(0)
-        quantize_w1(0, 0, 0.0)
-        quantize_w1(0, 1, 0.0)
-        gather(1)
-        hidden(0, False)
-        quantize_w1(1, 0, 0.0)
-        quantize_w2(0, 0.0)
-        second(0)
-        quantize_w1(1, 1, 0.375)
-        hidden(1, False)
-        quantize_w1(2, 0, 0.375)
-        quantize_w2(1, 0.375)
-        second(1)
-        quantize_w1(2, 1, 0.375)
-        hidden(2, False)
-        quantize_w1(3, 0, 0.375)
-        quantize_w1(3, 1, 0.5)
-        hidden(3, True)
-        quantize_w2(2, 0.5)
-        second(2)
-        quantize_w2(3, 0.25)
-        second(3)
+        def yc(e, split=False):
+            y_sb = keep.tile([P, N // P, C], F32, name="ysb%d" % e, tag="ysb%d" % e, align_bytes=64)
+            if split:
+                for b in range(N // P):
+                    nc.scalar.copy(out=y_sb[:, b, :], in_=ys[e][:, b, :])
+            else:
+                nc.scalar.copy(out=y_sb[:], in_=ys[e][:])
+            ysbs[e] = y_sb
+
+        def sc(e, b):
+            cols = slice(e * C // 16, (e + 1) * C // 16)
+            weights = gate_sb[e // 2][:, (e % 2) * C : (e % 2 + 1) * C]
+            nc.vector.tensor_tensor(result[b][:].indirect(tok_list[:, cols]), ysbs[e][:, b, :], weights, MULT)
+
+        gath()
+        c('A0',0)
+        q('A0',0)
+        c('A0',1)
+        q('A0',1)
+        c('B0',0)
+        q('B0',0)
+        c('B0',1)
+        q('B0',1)
+        mm1(0)
+        silu(0)
+        hc(0)
+        qh(0)
+        c('A1',0)
+        q('A1',0)
+        c('A1',1)
+        q('A1',1)
+        c('B1',0)
+        q('B1',0)
+        c('B1',1)
+        q('B1',1)
+        mm1(1,False)
+        c('C0',0)
+        q('C0',0)
+        mm2(0)
+        yc(0)
+        sc(0,0)
+        sc(0,1)
+        silu(1)
+        hc(1)
+        qh(1)
+        c('A2',0)
+        q('A2',0)
+        c('A2',1)
+        q('A2',1)
+        c('B2',0)
+        q('B2',0)
+        c('B2',1)
+        q('B2',1)
+        mm1(2,False)
+        c('C1',0)
+        q('C1',0)
+        mm2(1)
+        yc(1)
+        sc(1,0)
+        sc(1,1)
+        silu(2)
+        hc(2)
+        qh(2)
+        c('A3',0)
+        q('A3',0)
+        c('A3',1)
+        q('A3',1)
+        c('B3',0)
+        q('B3',0)
+        c('B3',1)
+        q('B3',1)
+        mm1(3,True)
+        silu(3)
+        hc(3)
+        qh(3)
+        c('C2',0)
+        q('C2',0)
+        mm2(2)
+        yc(2)
+        c('C3',0)
+        q('C3',0)
+        sc(2,0)
+        sc(2,1)
+        mm2(3)
+        yc(3,True)
+        sc(3,0)
+        sc(3,1)
         for b in range(N // P):
             nc.sync.dma_start(out=out[b * P : (b + 1) * P, :], in_=result[b][:])

@@ -26,8 +26,8 @@ WINDOW = 704
 
 def cast_interleave(engine_copy, grouped, raw, c0, c1):
     engine_copy(
-        out=grouped[:, c0 * PACK : c1 * PACK].rearrange("p (c i j) -> p c j i", i=4, j=PACK),
-        in_=raw[:, :, c0:c1].rearrange("p j (c i) -> p c j i", i=4),
+        out=grouped[:, c0 * PACK : c1 * PACK].rearrange("p (c i j) -> p c j i", i=2, j=PACK),
+        in_=raw[:, :, c0:c1].rearrange("p j (c i) -> p c j i", i=2),
     )
 
 
@@ -155,8 +155,8 @@ def tile_moe_duo_silu_kernel(
             raw, r0 = source(name, c0)
             copy = nc.scalar.copy if eng == "S" else nc.vector.tensor_copy
             copy(
-                out=staged[key][:, off * PACK : (off + cols) * PACK].rearrange("p (c i j) -> p c j i", i=4, j=PACK),
-                in_=raw[:, :, r0 : r0 + cols].rearrange("p j (c i) -> p c j i", i=4),
+                out=staged[key][:, off * PACK : (off + cols) * PACK].rearrange("p (c i j) -> p c j i", i=2, j=PACK),
+                in_=raw[:, :, r0 : r0 + cols].rearrange("p j (c i) -> p c j i", i=2),
             )
 
         def q(name, first):

@@ -24,286 +24,259 @@ PASSES = K // K_PASS
 WINDOW = 704
 
 
-def cast_interleave(engine_copy, grouped, raw, c0, c1):
-    engine_copy(
-        out=grouped[:, c0 * PACK : c1 * PACK].rearrange("p (c i j) -> p c j i", i=2, j=PACK),
-        in_=raw[:, :, c0:c1].rearrange("p j (c i) -> p c j i", i=2),
-    )
-
-
 def tile_moe_duo_silu_kernel(
     tc, x_words, x_scales, w1, wp_words, wp_scales, w2, gate, offs, offs2, out
 ):
     nc = tc.nc
     with ExitStack() as ctx:
         keep = ctx.enter_context(tc.tile_pool(name="keep", bufs=1))
+        stage = ctx.enter_context(tc.tile_pool(name="stage", bufs=1))
         psum = ctx.enter_context(tc.psum_pool(name="psum", bufs=2))
-        psum_acc = ctx.enter_context(tc.psum_pool(name="psum_acc", bufs=2))
 
-        xs = keep.tile([P, T + WINDOW], U8, name="xs", align_bytes=64)
+        xs = stage.tile([P, PASSES * WINDOW], U8, name="xs", offset=0, align_bytes=64)
         wps = keep.tile([P, E * PASSES * H], U8, name="wps", align_bytes=64)
         nc.vector.memset(xs[:].bitcast(I32), 0)
         warm = keep.tile([P, 1], F32, name="warm")
         nc.vector.memset(warm[:], 0.0)
-        nc.scalar.activation(out=warm[:], in_=warm[:], func=SILU)
         nc.vector.memset(wps[:].bitcast(I32), 0)
         ident = keep.tile([P, P], F32, name="ident")
         make_identity(nc, ident[:])
 
         tok_list = keep.tile([P, T // 16], U16, name="tok_list")
         par_list = keep.tile([P, T // 16], U16, name="par_list")
-        xw = [keep.tile([P, WINDOW], I32, name="xw%d" % s, align_bytes=64) for s in range(PASSES)]
+        xw = [stage.tile([P, WINDOW], I32, name="xw%d" % s, offset=1536 + 2816 * s, align_bytes=64) for s in range(PASSES)]
         for s in range(PASSES):
             nc.vector.memset(xw[s][:, T:WINDOW], 0)
-        w1_raw = {}
-        w2_raw = {}
-        wpw = {}
-        gate_sb = [keep.tile([P, 2 * C], F32, name="gate_sb%d" % g) for g in range(2)]
+        w1_raw = [[keep.tile([P, PACK, H], F32, name="w1raw%d_%d" % (e, s)) for s in range(PASSES)] for e in range(E)]
+        w2_raw = [keep.tile([P, PACK, N], F32, name="w2raw%d" % e) for e in range(E)]
+        wpw = [keep.tile([P, PASSES * 2 * H], U8, name="wpw%d" % e, align_bytes=64) for e in range(E)]
+        gate_cut = [0, 1 * C, E * C]
+        gate_sb = [keep.tile([P, gate_cut[g + 1] - gate_cut[g]], F32, name="gate_sb%d" % g) for g in range(2)]
+        result = [keep.tile([P, T], F32, name="result%d" % b) for b in range(N // P)]
+        w1_codes = [[keep.tile([P, H], U32, name="w1c%d_%d" % (e, s), align_bytes=64) for s in range(PASSES)] for e in range(E)]
+        w1_scales = [[keep.tile([P, H], U8, name="w1s%d_%d" % (e, s), align_bytes=64) for s in range(PASSES)] for e in range(E)]
+        w1_codes[0][0] = stage.tile([P, H], U32, name="first_codes", offset=1536 + 2816, align_bytes=64)
+        w1_scales[0][1] = stage.tile([P, H], U8, name="second_scales", offset=0, align_bytes=64)
+        w1_scales[1][0] = stage.tile([P, H], U8, name="third_scales", offset=512, align_bytes=64)
+        w2_codes = [keep.tile([P, N], U32, name="w2c%d" % e, align_bytes=64) for e in range(E)]
+        w2_scales = [keep.tile([P, N], U8, name="w2s%d" % e, align_bytes=64) for e in range(E)]
+        h_codes = [keep.tile([P, C], U32, name="hc%d" % e, align_bytes=64) for e in range(E)]
+        h_scales = [keep.tile([P, C], U8, name="hs%d" % e, align_bytes=64) for e in range(E)]
+        xs_rows = x_scales.bitcast(I32).rearrange("s (q r) n -> q r s n", r=4)
+        wps_rows = wp_scales.bitcast(I32).rearrange("e s (q r) n -> q r (e s) n", r=4)
 
         def load_x(s):
             nc.sync.dma_start(out=xw[s][:, 0:T], in_=x_words[s].rearrange("p t d -> p (t d)").bitcast(I32))
 
-        def load_w1(e, s, c0, c1):
-            raw = keep.tile([P, PACK, c1 - c0], F32, name="w1raw%d_%d_%d" % (e, s, c0))
-            rows = w1[e, s * K_PASS : (s + 1) * K_PASS, c0:c1]
-            nc.sync.dma_start(out=raw[:], in_=rows.rearrange("(p j) w -> p j w", j=PACK))
-            w1_raw.setdefault((e, s), []).append((raw, c0, c1))
+        def load_token_scales(queue):
+            for q in range(4):
+                rows = xs[32 * q : 32 * q + 4, :].bitcast(I32).rearrange("r (s n) -> r s n", s=PASSES)
+                queue.dma_start(out=rows[:, :, 0 : T // 4], in_=xs_rows[q])
+
+        def load_packed_scales(queue):
+            for q in range(4):
+                queue.dma_start(out=xs[32 * q + 4 : 32 * q + 8, WINDOW : WINDOW + T].bitcast(I32), in_=xs_rows[q][:, 0, :])
+
+        def load_partner_scales(queue):
+            for q in range(4):
+                queue.dma_start(out=wps[32 * q : 32 * q + 4, :].bitcast(I32).rearrange("r (g n) -> r g n", g=E * PASSES), in_=wps_rows[q])
+
+        def load_w1(e, s):
+            rows = w1[e, s * K_PASS : (s + 1) * K_PASS, :]
+            nc.sync.dma_start(out=w1_raw[e][s][:], in_=rows.rearrange("(p j) w -> p j w", j=PACK))
 
         def load_w2(e):
-            raw = keep.tile([P, PACK, N], F32, name="w2raw%d" % e)
-            nc.sync.dma_start(out=raw[:], in_=w2[e].rearrange("(p j) w -> p j w", j=PACK))
-            w2_raw[e] = raw
+            nc.sync.dma_start(out=w2_raw[e][:], in_=w2[e].rearrange("(p j) w -> p j w", j=PACK))
 
         def load_wp(e):
-            words = keep.tile([P, PASSES * 2 * H], U8, name="wpw%d" % e, align_bytes=64)
             nc.sync.dma_start(
-                out=words[:].bitcast(I32).rearrange("p (s n) -> p s n", s=PASSES),
+                out=wpw[e][:].bitcast(I32).rearrange("p (s n) -> p s n", s=PASSES),
                 in_=wp_words[e].bitcast(I32).rearrange("s p n -> p s n"),
             )
-            wpw[e] = words
 
-        nc.sync.dma_start(tok_list[:], offs)
-        load_x(0)
-        nc.sync.dma_start(par_list[:], offs2)
-        xs_rows = x_scales.bitcast(I32).rearrange("s (q r) n -> r q s n", r=4)
-        for r in range(4):
-            nc.sync.dma_start(out=xs[r:P:32, 0 : PASSES * T].bitcast(I32).rearrange("q (s n) -> q s n", s=PASSES), in_=xs_rows[r])
-        load_x(1)
-        load_w1(0, 0, 0, 512)
-        load_w1(0, 1, 0, 512)
-        wps_rows = wp_scales.bitcast(I32).rearrange("e s (q r) n -> r q (e s) n", r=4)
-        for r in range(4):
-            nc.sync.dma_start(out=wps[r:P:32, :].bitcast(I32).rearrange("q (g n) -> q g n", g=E * PASSES), in_=wps_rows[r])
-        load_w1(1, 0, 0, 512)
-        load_wp(0)
-        load_w1(1, 1, 0, 512)
-        load_w2(0)
-        load_wp(1)
-        nc.sync.dma_start(out=gate_sb[0][:], in_=gate[:, 0:256])
-        load_w1(2, 0, 0, 512)
-        load_w1(2, 1, 0, 512)
-        load_w2(1)
-        load_wp(2)
-        load_w1(3, 0, 0, 512)
-        load_w1(3, 1, 0, 512)
-        load_wp(3)
-        load_w2(2)
-        load_w2(3)
-        nc.sync.dma_start(out=gate_sb[1][:], in_=gate[:, 256:512])
+        def load_gate(g):
+            nc.sync.dma_start(out=gate_sb[g][:], in_=gate[:, gate_cut[g] : gate_cut[g + 1]])
 
-        tok_words = [keep.tile([P, E * C], U32, name="tokw%d" % s, align_bytes=64) for s in range(PASSES)]
-        par_words = [keep.tile([P, E * C], U32, name="parw%d" % s, align_bytes=64) for s in range(PASSES)]
-        tok_scales = [keep.tile([P, E * C], U8, name="toks%d" % s, align_bytes=64) for s in range(2)]
-        par_scales = [keep.tile([P, E * C], U8, name="pars%d" % s, align_bytes=64) for s in range(PASSES)]
-        plan = {"A0":[["S",256],["S",256]],"B0":[["S",256],["S",256]],"A1":[["S",256],["S",256]],"B1":[["S",256],["V",256]],"A2":[["S",256],["S",256]],"B2":[["S",256],["V",256]],"A3":[["S",256],["V",256]],"B3":[["S",256],["V",256]],"C0":[["S",256]],"C1":[["S",256]],"C2":[["S",256]],"C3":[["S",256]]}
-        holds = {}
+        gathered = {}
         staged = {}
-        quantized = {}
         accs = {}
         turns = {}
-        hgs = {}
         ys = {}
-        ysbs = {}
-        result = [keep.tile([P, T], F32, name="result%d" % b) for b in range(N // P)]
+        y_sb = {}
 
-        def gath():
-            for s in range(PASSES):
-                nc.vector.tensor_copy(tok_words[s][:], xw[s][:].bitcast(U32).indirect(tok_list[:]))
-                nc.vector.tensor_copy(par_words[s][:], xw[s][:].bitcast(U32).indirect(par_list[:]))
-            for s in range(PASSES):
-                nc.vector.tensor_copy(par_scales[s][:], xs[:, s * T : s * T + WINDOW].indirect(par_list[:]))
-            for s in range(PASSES):
-                nc.vector.tensor_copy(tok_scales[s][:], xs[:, s * T : s * T + WINDOW].indirect(tok_list[:]))
+        def gather(kind, s):
+            dtype = U32 if kind[1] == "w" else U8
+            tile = keep.tile([P, E * C], dtype, name="%s%d" % (kind, s), align_bytes=64)
+            offsets = tok_list if kind[0] == "t" else par_list
+            window = xw[s][:].bitcast(U32) if kind[1] == "w" else xs[:, s * WINDOW : (s + 1) * WINDOW]
+            nc.vector.tensor_copy(tile[:], window.indirect(offsets[:]))
+            gathered[(kind, s)] = tile
 
-        def source(name, c0):
-            e = int(name[1])
-            if name[0] == "C":
-                return w2_raw[e], c0
-            for raw, a, b in w1_raw[(e, 0 if name[0] == "A" else 1)]:
-                if a <= c0 < b:
-                    return raw, c0 - a
-
-        def c(name, i, group=None):
-            eng, cols = plan[name][i]
-            c0 = sum(x[1] for x in plan[name][:i])
-            first = i if group is None else group[0]
-            key = name + str(first)
-            if key not in staged:
-                width = cols if group is None else sum(plan[name][j][1] for j in group)
-                staged[key] = keep.tile([P, width * PACK], BF16, name="g" + key, tag=holds.get(key, "g" + key), align_bytes=64)
-            off = c0 - sum(x[1] for x in plan[name][:first])
-            raw, r0 = source(name, c0)
-            copy = nc.scalar.copy if eng == "S" else nc.vector.tensor_copy
+        def cast(name, copy, raw, c0, c1, at):
+            tile = stage.tile([P, (c1 - c0) * PACK], BF16, name="st" + name, offset=at, align_bytes=64)
             copy(
-                out=staged[key][:, off * PACK : (off + cols) * PACK].rearrange("p (c i j) -> p c j i", i=2, j=PACK),
-                in_=raw[:, :, r0 : r0 + cols].rearrange("p j (c i) -> p c j i", i=2),
+                out=tile[:].rearrange("p (c i j) -> p c j i", i=2, j=PACK),
+                in_=raw[:, :, c0:c1].rearrange("p j (c i) -> p c j i", i=2),
             )
+            staged[name] = tile
 
-        def q(name, first):
-            if name not in quantized:
-                width = N if name[0] == "C" else H
-                codes = keep.tile([P, width], U32, name="codes" + name, tag="codes" + name, align_bytes=64)
-                scales = keep.tile([P, width], U8, name="scales" + name, align_bytes=64)
-                quantized[name] = (codes, scales)
-            codes, scales = quantized[name]
-            grouped = staged[name + str(first)]
-            c0 = sum(x[1] for x in plan[name][:first])
-            c1 = c0 + grouped.shape[1] // PACK
-            nc.vector.quantize_mx(out=codes[:, c0:c1].bitcast(FP8X4), scales=scales[:, c0:c1], in_=grouped[:])
+        def quant(codes, scales, c0, c1, tile):
+            nc.vector.quantize_mx(out=codes[:, c0:c1].bitcast(FP8X4), scales=scales[:, c0:c1], in_=tile[:])
 
-        def mm1(e, partner_last=False):
+        def first_product(e, order):
             slots = slice(e * C, (e + 1) * C)
-            acc = psum_acc.tile([P, H], F32, name="acc")
-            own = []
-            partner = []
+            acc = psum.tile([P, H], F32, name="acc")
+            passes = {}
             for s in range(PASSES):
-                codes, scales = quantized["AB"[s] + str(e)]
-                own.append((tok_words[s][:, slots], tok_scales[s][:, slots], codes[:].bitcast(FP8X4), scales[:]))
                 g = e * PASSES + s
-                partner.append((par_words[s][:, slots], par_scales[s][:, slots], wpw[e][:, s * 2 * H : (s + 1) * 2 * H].bitcast(FP4X4), wps[:, g * H : (g + 1) * H]))
-            passes = [own[0]] + partner + [own[1]] if partner_last else partner + own
-            for n, (words, word_scales, weights, weight_scales) in enumerate(passes):
-                nc.tensor.matmul_mx(out=acc[:], lhsT=words.bitcast(FP8X4), lhsT_scale=word_scales, rhs=weights, rhs_scale=weight_scales, start=(n == 0), stop=(n == len(passes) - 1))
+                first_row = 4 * (1 - s)
+                passes["o%d" % s] = (gathered[("tw", s)][:, slots], gathered[("tb", 1)][first_row:P, slots], w1_codes[e][s][:].bitcast(FP8X4), w1_scales[e][s][:])
+                passes["p%d" % s] = (gathered[("pw", s)][:, slots], gathered[("pb", s)][:, slots], wpw[e][:, s * 2 * H : (s + 1) * 2 * H].bitcast(FP4X4), wps[:, g * H : (g + 1) * H])
+            for n, key in enumerate(order.split()):
+                words, word_scales, weights, weight_scales = passes[key]
+                nc.tensor.matmul_mx(out=acc[:], lhsT=words.bitcast(FP8X4), lhsT_scale=word_scales, rhs=weights, rhs_scale=weight_scales, start=(n == 0), stop=(n == 3))
             accs[e] = acc
 
-        def silu(e):
-            h_rows = keep.tile([P, H], BF16, name="hrows%d" % e, tag="hrows%d" % e, align_bytes=64)
+        def silu(e, at):
+            rows = stage.tile([P, H], BF16, name="hrows%d" % e, offset=at, align_bytes=64)
             nc.scalar.activation(
-                out=h_rows[:].rearrange("c (u p d) -> c u p d", u=2, d=2),
+                out=rows[:].rearrange("c (u p d) -> c u p d", u=2, d=2),
                 in_=accs[e][:].rearrange("c (p u d) -> c u p d", u=2, d=2),
                 func=SILU,
             )
             turned = psum.tile([P, 2, C], F32, name="turned")
-            pairs = h_rows[:].bitcast(F32)
+            pairs = rows[:].bitcast(F32)
             for u in range(2):
                 nc.tensor.transpose(turned[:, u, :], pairs[:, u * P : (u + 1) * P], ident[:])
             turns[e] = turned
 
-        def hc(e):
-            grouped = keep.tile([P, C * PACK], BF16, name="hg%d" % e, tag="hg%d" % e, align_bytes=64)
+        def regroup(e, at):
+            grouped = stage.tile([P, C * PACK], BF16, name="hg%d" % e, offset=at, align_bytes=64)
             nc.scalar.copy(out=grouped[:].bitcast(F32).rearrange("p (c u) -> p c u", u=2), in_=turns[e][:].rearrange("p u c -> p c u"))
-            hgs[e] = grouped
+            quant(h_codes[e], h_scales[e], 0, C, grouped)
 
-        def qh(e):
-            codes = keep.tile([P, C], U32, name="hc%d" % e, align_bytes=64)
-            scales = keep.tile([P, C], U8, name="hs%d" % e, align_bytes=64)
-            nc.vector.quantize_mx(out=codes[:].bitcast(FP8X4), scales=scales[:], in_=hgs[e][:])
-            quantized["h%d" % e] = (codes, scales)
-
-        def mm2(e):
+        def second_product(e):
             y = psum.tile([P, N // P, C], F32, name="y")
-            w_codes, w_scales = quantized["C%d" % e]
-            codes, scales = quantized["h%d" % e]
             for b in range(N // P):
-                nc.tensor.matmul_mx(out=y[:, b, :], lhsT=w_codes[:, b * P : (b + 1) * P].bitcast(FP8X4), lhsT_scale=w_scales[:, b * P : (b + 1) * P], rhs=codes[:].bitcast(FP8X4), rhs_scale=scales[:], start=True, stop=True)
+                cols = slice(b * P, (b + 1) * P)
+                nc.tensor.matmul_mx(out=y[:, b, :], lhsT=w2_codes[e][:, cols].bitcast(FP8X4), lhsT_scale=w2_scales[e][:, cols], rhs=h_codes[e][:].bitcast(FP8X4), rhs_scale=h_scales[e][:], start=True, stop=True)
             ys[e] = y
 
-        def yc(e, split=False):
-            y_sb = keep.tile([P, N // P, C], F32, name="ysb%d" % e, tag="ysb%d" % e, align_bytes=64)
-            if split:
-                for b in range(N // P):
-                    nc.scalar.copy(out=y_sb[:, b, :], in_=ys[e][:, b, :])
+        def copy_y(e, b, at):
+            if b is None:
+                both = stage.tile([P, N // P, C], F32, name="ysb%d" % e, offset=at, align_bytes=64)
+                nc.scalar.copy(out=both[:], in_=ys[e][:])
+                y_sb[(e, 0)] = both[:, 0, :]
+                y_sb[(e, 1)] = both[:, 1, :]
             else:
-                nc.scalar.copy(out=y_sb[:], in_=ys[e][:])
-            ysbs[e] = y_sb
+                one = stage.tile([P, C], F32, name="ysb%d_%d" % (e, b), offset=at, align_bytes=64)
+                nc.scalar.copy(out=one[:], in_=ys[e][:, b, :])
+                y_sb[(e, b)] = one[:]
 
-        def sc(e, b):
+        def scatter(e, b):
             cols = slice(e * C // 16, (e + 1) * C // 16)
-            weights = gate_sb[e // 2][:, (e % 2) * C : (e % 2 + 1) * C]
-            nc.vector.tensor_tensor(result[b][:].indirect(tok_list[:, cols]), ysbs[e][:, b, :], weights, MULT)
+            g = 0 if e * C < gate_cut[1] else 1
+            first = e * C - gate_cut[g]
+            nc.vector.tensor_tensor(result[b][:].indirect(tok_list[:, cols]), y_sb[(e, b)], gate_sb[g][:, first : first + C], MULT)
 
-        gath()
-        c('A0',0)
-        q('A0',0)
-        c('A0',1)
-        q('A0',1)
-        c('B0',0)
-        q('B0',0)
-        c('B0',1)
-        q('B0',1)
-        mm1(0)
-        silu(0)
-        hc(0)
-        qh(0)
-        c('A1',0)
-        q('A1',0)
-        c('A1',1)
-        q('A1',1)
-        c('B1',0)
-        q('B1',0)
-        c('B1',1)
-        q('B1',1)
-        mm1(1,False)
-        c('C0',0)
-        q('C0',0)
-        mm2(0)
-        yc(0)
-        sc(0,0)
-        sc(0,1)
-        silu(1)
-        hc(1)
-        qh(1)
-        c('A2',0)
-        q('A2',0)
-        c('A2',1)
-        q('A2',1)
-        c('B2',0)
-        q('B2',0)
-        c('B2',1)
-        q('B2',1)
-        mm1(2,False)
-        c('C1',0)
-        q('C1',0)
-        mm2(1)
-        yc(1)
-        sc(1,0)
-        sc(1,1)
-        silu(2)
-        hc(2)
-        qh(2)
-        c('A3',0)
-        q('A3',0)
-        c('A3',1)
-        q('A3',1)
-        c('B3',0)
-        q('B3',0)
-        c('B3',1)
-        q('B3',1)
-        mm1(3,True)
-        silu(3)
-        hc(3)
-        qh(3)
-        c('C2',0)
-        q('C2',0)
-        mm2(2)
-        yc(2)
-        c('C3',0)
-        q('C3',0)
-        sc(2,0)
-        sc(2,1)
-        mm2(3)
-        yc(3,True)
-        sc(3,0)
-        sc(3,1)
+        nc.scalar.activation(out=warm[:], in_=warm[:], func=SILU)
+        nc.sync.dma_start(tok_list[:], offs)
+        load_x(0)
+        nc.sync.dma_start(par_list[:], offs2)
+        load_w1(0, 0)
+        load_token_scales(nc.sync)
+        load_x(1)
+        load_w1(0, 1)
+        load_packed_scales(nc.sync)
+        load_w1(1, 0)
+        load_partner_scales(nc.sync)
+        load_wp(0)
+        load_w2(0)
+        load_gate(0)
+        load_wp(1)
+        load_w1(1, 1)
+        load_w1(2, 0)
+        load_w2(1)
+        load_w1(2, 1)
+        load_w1(3, 0)
+        load_wp(2)
+        load_wp(3)
+        load_w1(3, 1)
+        load_gate(1)
+        load_w2(2)
+        load_w2(3)
+        gather("tw", 0)
+        gather("pw", 0)
+        gather("pb", 0)
+        gather("tw", 1)
+        gather("pw", 1)
+        gather("pb", 1)
+        gather("tb", 1)
+        cast("00a", nc.scalar.copy, w1_raw[0][0], 0, 512, 7168)
+        quant(w1_codes[0][0], w1_scales[0][0], 0, 512, staged["00a"])
+        cast("01a", nc.scalar.copy, w1_raw[0][1], 0, 512, 11264)
+        quant(w1_codes[0][1], w1_scales[0][1], 0, 512, staged["01a"])
+        first_product(0, "p0 p1 o0 o1")
+        cast("10a", nc.scalar.copy, w1_raw[1][0], 0, 512, 15360)
+        quant(w1_codes[1][0], w1_scales[1][0], 0, 512, staged["10a"])
+        cast("v0a", nc.scalar.copy, w2_raw[0], 0, 256, 19456)
+        quant(w2_codes[0], w2_scales[0], 0, 256, staged["v0a"])
+        silu(0, 19456)
+        cast("11a", nc.vector.tensor_copy, w1_raw[1][1], 0, 256, 15360)
+        cast("11b", nc.scalar.copy, w1_raw[1][1], 256, 512, 21504)
+        quant(w1_codes[1][1], w1_scales[1][1], 0, 256, staged["11a"])
+        quant(w1_codes[1][1], w1_scales[1][1], 256, 512, staged["11b"])
+        first_product(1, "p0 p1 o0 o1")
+        regroup(0, 15360)
+        second_product(0)
+        cast("20a", nc.vector.tensor_copy, w1_raw[2][0], 0, 256, 21504)
+        cast("20b", nc.scalar.copy, w1_raw[2][0], 256, 512, 23552)
+        quant(w1_codes[2][0], w1_scales[2][0], 0, 256, staged["20a"])
+        quant(w1_codes[2][0], w1_scales[2][0], 256, 512, staged["20b"])
+        copy_y(0, None, 21504)
+        scatter(0, 0)
+        scatter(0, 1)
+        cast("v1a", nc.scalar.copy, w2_raw[1], 0, 256, 25600)
+        quant(w2_codes[1], w2_scales[1], 0, 256, staged["v1a"])
+        silu(1, 23552)
+        cast("21a", nc.vector.tensor_copy, w1_raw[2][1], 0, 256, 25600)
+        cast("21b", nc.scalar.copy, w1_raw[2][1], 256, 512, 27648)
+        quant(w1_codes[2][1], w1_scales[2][1], 0, 256, staged["21a"])
+        quant(w1_codes[2][1], w1_scales[2][1], 256, 512, staged["21b"])
+        regroup(1, 25600)
+        second_product(1)
+        cast("30a", nc.vector.tensor_copy, w1_raw[3][0], 0, 256, 27648)
+        cast("30b", nc.scalar.copy, w1_raw[3][0], 256, 512, 29696)
+        quant(w1_codes[3][0], w1_scales[3][0], 0, 256, staged["30a"])
+        quant(w1_codes[3][0], w1_scales[3][0], 256, 512, staged["30b"])
+        copy_y(1, None, 28672)
+        first_product(2, "o0 o1 p0 p1")
+        silu(2, 31744)
+        cast("31a", nc.vector.tensor_copy, w1_raw[3][1], 0, 256, 29696)
+        cast("31c", nc.scalar.copy, w1_raw[3][1], 384, 512, 33792)
+        cast("31b", nc.vector.tensor_copy, w1_raw[3][1], 256, 384, 27648)
+        quant(w1_codes[3][1], w1_scales[3][1], 0, 256, staged["31a"])
+        quant(w1_codes[3][1], w1_scales[3][1], 256, 384, staged["31b"])
+        quant(w1_codes[3][1], w1_scales[3][1], 384, 512, staged["31c"])
+        regroup(2, 27648)
+        first_product(3, "o0 p0 p1 o1")
+        scatter(1, 0)
+        scatter(1, 1)
+        cast("v2a", nc.scalar.copy, w2_raw[2], 0, 256, 35840)
+        quant(w2_codes[2], w2_scales[2], 0, 256, staged["v2a"])
+        second_product(2)
+        cast("v3a", nc.vector.tensor_copy, w2_raw[3], 0, 256, 35840)
+        quant(w2_codes[3], w2_scales[3], 0, 256, staged["v3a"])
+        silu(3, 37888)
+        regroup(3, 39936)
+        copy_y(2, 0, 37888)
+        scatter(2, 0)
+        second_product(3)
+        copy_y(2, 1, 38400)
+        scatter(2, 1)
+        copy_y(3, 0, 41984)
+        scatter(3, 0)
+        copy_y(3, 1, 44032)
+        scatter(3, 1)
         for b in range(N // P):
             nc.sync.dma_start(out=out[b * P : (b + 1) * P, :], in_=result[b][:])

@@ -50,7 +50,7 @@ def tile_moe_duo_silu_kernel(
         w1_raw = [[keep.tile([P, PACK, H], F32, name="w1raw%d_%d" % (e, s)) for s in range(PASSES)] for e in range(E)]
         w2_raw = [keep.tile([P, PACK, N], F32, name="w2raw%d" % e) for e in range(E)]
         wpw = [keep.tile([P, PASSES * 2 * H], U8, name="wpw%d" % e, align_bytes=64) for e in range(E)]
-        gate_cut = [0, 1 * C, E * C]
+        gate_cut = [0, 2 * C, E * C]
         gate_sb = [keep.tile([P, gate_cut[g + 1] - gate_cut[g]], F32, name="gate_sb%d" % g) for g in range(2)]
         result = [keep.tile([P, T], F32, name="result%d" % b) for b in range(N // P)]
         w1_codes = [[keep.tile([P, H], U32, name="w1c%d_%d" % (e, s), align_bytes=64) for s in range(PASSES)] for e in range(E)]
@@ -62,24 +62,24 @@ def tile_moe_duo_silu_kernel(
         w2_scales = [keep.tile([P, N], U8, name="w2s%d" % e, align_bytes=64) for e in range(E)]
         h_codes = [keep.tile([P, C], U32, name="hc%d" % e, align_bytes=64) for e in range(E)]
         h_scales = [keep.tile([P, C], U8, name="hs%d" % e, align_bytes=64) for e in range(E)]
-        xs_rows = x_scales.bitcast(I32).rearrange("s (q r) n -> q r s n", r=4)
-        wps_rows = wp_scales.bitcast(I32).rearrange("e s (q r) n -> q r (e s) n", r=4)
+        xs_rows = x_scales.bitcast(I32).rearrange("s (q r) n -> r q s n", r=4)
+        wps_rows = wp_scales.bitcast(I32).rearrange("e s (q r) n -> r q (e s) n", r=4)
 
         def load_x(s):
             nc.sync.dma_start(out=xw[s][:, 0:T], in_=x_words[s].rearrange("p t d -> p (t d)").bitcast(I32))
 
         def load_token_scales(queue):
-            for q in range(4):
-                rows = xs[32 * q : 32 * q + 4, :].bitcast(I32).rearrange("r (s n) -> r s n", s=PASSES)
-                queue.dma_start(out=rows[:, :, 0 : T // 4], in_=xs_rows[q])
+            for r in range(4):
+                rows = xs[r:P:32, :].bitcast(I32).rearrange("q (s n) -> q s n", s=PASSES)
+                queue.dma_start(out=rows[:, :, 0 : T // 4], in_=xs_rows[r])
 
         def load_packed_scales(queue):
-            for q in range(4):
-                queue.dma_start(out=xs[32 * q + 4 : 32 * q + 8, WINDOW : WINDOW + T].bitcast(I32), in_=xs_rows[q][:, 0, :])
+            for r in range(4):
+                queue.dma_start(out=xs[4 + r : P : 32, WINDOW : WINDOW + T].bitcast(I32), in_=xs_rows[r][:, 0, :])
 
         def load_partner_scales(queue):
-            for q in range(4):
-                queue.dma_start(out=wps[32 * q : 32 * q + 4, :].bitcast(I32).rearrange("r (g n) -> r g n", g=E * PASSES), in_=wps_rows[q])
+            for r in range(4):
+                queue.dma_start(out=wps[r:P:32, :].bitcast(I32).rearrange("q (g n) -> q g n", g=E * PASSES), in_=wps_rows[r])
 
         def load_w1(e, s):
             rows = w1[e, s * K_PASS : (s + 1) * K_PASS, :]
@@ -200,11 +200,11 @@ def tile_moe_duo_silu_kernel(
         load_w1(2, 1)
         load_w1(3, 0)
         load_wp(2)
-        load_wp(3)
         load_w1(3, 1)
-        load_gate(1)
         load_w2(2)
+        load_wp(3)
         load_w2(3)
+        load_gate(1)
         gather("tw", 0)
         gather("pw", 0)
         gather("pb", 0)
@@ -233,50 +233,52 @@ def tile_moe_duo_silu_kernel(
         cast("20b", nc.scalar.copy, w1_raw[2][0], 256, 512, 23552)
         quant(w1_codes[2][0], w1_scales[2][0], 0, 256, staged["20a"])
         quant(w1_codes[2][0], w1_scales[2][0], 256, 512, staged["20b"])
-        copy_y(0, None, 21504)
+        copy_y(0, 0, 21504)
         scatter(0, 0)
-        scatter(0, 1)
         cast("v1a", nc.scalar.copy, w2_raw[1], 0, 256, 25600)
         quant(w2_codes[1], w2_scales[1], 0, 256, staged["v1a"])
         silu(1, 23552)
+        regroup(1, 27648)
+        second_product(1)
         cast("21a", nc.vector.tensor_copy, w1_raw[2][1], 0, 256, 25600)
-        cast("21b", nc.scalar.copy, w1_raw[2][1], 256, 512, 27648)
+        cast("21b", nc.scalar.copy, w1_raw[2][1], 256, 512, 29696)
         quant(w1_codes[2][1], w1_scales[2][1], 0, 256, staged["21a"])
         quant(w1_codes[2][1], w1_scales[2][1], 256, 512, staged["21b"])
-        regroup(1, 25600)
-        second_product(1)
-        cast("30a", nc.vector.tensor_copy, w1_raw[3][0], 0, 256, 27648)
-        cast("30b", nc.scalar.copy, w1_raw[3][0], 256, 512, 29696)
+        copy_y(0, 1, 25600)
+        scatter(0, 1)
+        copy_y(1, 0, 26112)
+        scatter(1, 0)
+        cast("30a", nc.scalar.copy, w1_raw[3][0], 0, 256, 31744)
+        cast("30b", nc.scalar.copy, w1_raw[3][0], 256, 512, 33792)
         quant(w1_codes[3][0], w1_scales[3][0], 0, 256, staged["30a"])
         quant(w1_codes[3][0], w1_scales[3][0], 256, 512, staged["30b"])
-        copy_y(1, None, 28672)
         first_product(2, "o0 o1 p0 p1")
-        silu(2, 31744)
-        cast("31a", nc.vector.tensor_copy, w1_raw[3][1], 0, 256, 29696)
-        cast("31c", nc.scalar.copy, w1_raw[3][1], 384, 512, 33792)
-        cast("31b", nc.vector.tensor_copy, w1_raw[3][1], 256, 384, 27648)
+        silu(2, 35840)
+        cast("31a", nc.vector.tensor_copy, w1_raw[3][1], 0, 256, 31744)
+        cast("31c", nc.scalar.copy, w1_raw[3][1], 384, 512, 37888)
+        cast("31b", nc.vector.tensor_copy, w1_raw[3][1], 256, 384, 33792)
         quant(w1_codes[3][1], w1_scales[3][1], 0, 256, staged["31a"])
         quant(w1_codes[3][1], w1_scales[3][1], 256, 384, staged["31b"])
         quant(w1_codes[3][1], w1_scales[3][1], 384, 512, staged["31c"])
-        regroup(2, 27648)
+        regroup(2, 31744)
+        copy_y(1, 1, 32768)
         first_product(3, "o0 p0 p1 o1")
-        scatter(1, 0)
-        scatter(1, 1)
-        cast("v2a", nc.scalar.copy, w2_raw[2], 0, 256, 35840)
+        cast("v2a", nc.scalar.copy, w2_raw[2], 0, 256, 39936)
         quant(w2_codes[2], w2_scales[2], 0, 256, staged["v2a"])
         second_product(2)
-        cast("v3a", nc.vector.tensor_copy, w2_raw[3], 0, 256, 35840)
+        scatter(1, 1)
+        cast("v3a", nc.vector.tensor_copy, w2_raw[3], 0, 256, 39936)
         quant(w2_codes[3], w2_scales[3], 0, 256, staged["v3a"])
-        silu(3, 37888)
-        regroup(3, 39936)
-        copy_y(2, 0, 37888)
+        silu(3, 41984)
+        regroup(3, 44032)
+        copy_y(2, 0, 41984)
         scatter(2, 0)
         second_product(3)
-        copy_y(2, 1, 38400)
+        copy_y(2, 1, 42496)
         scatter(2, 1)
-        copy_y(3, 0, 41984)
+        copy_y(3, 0, 46080)
         scatter(3, 0)
-        copy_y(3, 1, 44032)
+        copy_y(3, 1, 48128)
         scatter(3, 1)
         for b in range(N // P):
             nc.sync.dma_start(out=out[b * P : (b + 1) * P, :], in_=result[b][:])

@@ -180,6 +180,7 @@ def tile_moe_duo_silu_kernel(
             nc.vector.tensor_tensor(result[b][:].indirect(tok_list[:, cols]), y_sb[(e, b)], gate_sb[g][:, first : first + C], MULT)
 
         nc.scalar.activation(out=warm[:], in_=warm[:], func=SILU)
+        load_partner_scales(nc.gpsimd)
         nc.sync.dma_start(tok_list[:], offs)
         load_x(0)
         nc.sync.dma_start(par_list[:], offs2)
@@ -189,7 +190,6 @@ def tile_moe_duo_silu_kernel(
         load_w1(0, 1)
         load_packed_scales(nc.sync)
         load_w1(1, 0)
-        load_partner_scales(nc.sync)
         load_wp(0)
         load_w2(0)
         load_gate(0)

@@ -22,6 +22,7 @@ PACK = 4
 K_PASS = P * PACK
 PASSES = K // K_PASS
 WINDOW = 704
+BANK = 2048
 
 
 def tile_moe_duo_silu_kernel(
@@ -31,7 +32,7 @@ def tile_moe_duo_silu_kernel(
     with ExitStack() as ctx:
         keep = ctx.enter_context(tc.tile_pool(name="keep", bufs=1))
         stage = ctx.enter_context(tc.tile_pool(name="stage", bufs=1))
-        psum = ctx.enter_context(tc.psum_pool(name="psum", bufs=2))
+        psum = ctx.enter_context(tc.psum_pool(name="psum", bufs=1))
 
         xs = stage.tile([P, PASSES * WINDOW], U8, name="xs", offset=0, align_bytes=64)
         wps = keep.tile([P, E * PASSES * H], U8, name="wps", align_bytes=64)
@@ -50,8 +51,6 @@ def tile_moe_duo_silu_kernel(
         w1_raw = [[keep.tile([P, PACK, H], F32, name="w1raw%d_%d" % (e, s)) for s in range(PASSES)] for e in range(E)]
         w2_raw = [keep.tile([P, PACK, N], F32, name="w2raw%d" % e) for e in range(E)]
         wpw = [keep.tile([P, PASSES * 2 * H], U8, name="wpw%d" % e, align_bytes=64) for e in range(E)]
-        gate_cut = [0, 2 * C, E * C]
-        gate_sb = [keep.tile([P, gate_cut[g + 1] - gate_cut[g]], F32, name="gate_sb%d" % g) for g in range(2)]
         result = [keep.tile([P, T], F32, name="result%d" % b) for b in range(N // P)]
         w1_codes = [[keep.tile([P, H], U32, name="w1c%d_%d" % (e, s), align_bytes=64) for s in range(PASSES)] for e in range(E)]
         w1_scales = [[keep.tile([P, H], U8, name="w1s%d_%d" % (e, s), align_bytes=64) for s in range(PASSES)] for e in range(E)]
@@ -85,6 +84,12 @@ def tile_moe_duo_silu_kernel(
             rows = w1[e, s * K_PASS : (s + 1) * K_PASS, :]
             nc.sync.dma_start(out=w1_raw[e][s][:], in_=rows.rearrange("(p j) w -> p j w", j=PACK))
 
+        last_raw = [keep.tile([P, PACK, H // 2], F32, name="last_raw%d" % half) for half in range(2)]
+
+        def load_last(half):
+            rows = w1[E - 1, K_PASS : 2 * K_PASS, half * H // 2 : (half + 1) * H // 2]
+            nc.sync.dma_start(out=last_raw[half][:], in_=rows.rearrange("(p j) w -> p j w", j=PACK))
+
         def load_w2(e):
             nc.sync.dma_start(out=w2_raw[e][:], in_=w2[e].rearrange("(p j) w -> p j w", j=PACK))
 
@@ -94,8 +99,17 @@ def tile_moe_duo_silu_kernel(
                 in_=wp_words[e].bitcast(I32).rearrange("s p n -> p s n"),
             )
 
-        def load_gate(g):
-            nc.sync.dma_start(out=gate_sb[g][:], in_=gate[:, gate_cut[g] : gate_cut[g + 1]])
+        gate_cols = keep.tile([P, PACK], F32, name="gate_cols")
+        gate_all = keep.tile([P, E * C], F32, name="gate_all")
+
+        def load_gate_row():
+            nc.sync.dma_start(out=gate_cols[:], in_=gate[0].rearrange("(p j) -> p j", j=PACK))
+
+        def spread_gate(at):
+            spread = psum.tile([P, PACK, P], F32, name="spread", offset=BANK * 6)
+            for j in range(PACK):
+                nc.tensor.transpose(spread[:, j, :], gate_cols[:, j : j + 1].to_broadcast([P, P]), ident[:])
+            nc.scalar.copy(out=gate_all[:].rearrange("p (n j) -> p n j", j=PACK), in_=spread[:].rearrange("p j n -> p n j"))
 
         gathered = {}
         staged = {}
@@ -125,7 +139,7 @@ def tile_moe_duo_silu_kernel(
 
         def first_product(e, order):
             slots = slice(e * C, (e + 1) * C)
-            acc = psum.tile([P, H], F32, name="acc")
+            acc = psum.tile([P, H], F32, name="acc%d" % e, offset=BANK * (e % 2))
             passes = {}
             for s in range(PASSES):
                 g = e * PASSES + s
@@ -144,7 +158,7 @@ def tile_moe_duo_silu_kernel(
                 in_=accs[e][:].rearrange("c (p u d) -> c u p d", u=2, d=2),
                 func=SILU,
             )
-            turned = psum.tile([P, 2, C], F32, name="turned")
+            turned = psum.tile([P, 2, C], F32, name="turned%d" % e, offset=BANK * (2 + e % 2))
             pairs = rows[:].bitcast(F32)
             for u in range(2):
                 nc.tensor.transpose(turned[:, u, :], pairs[:, u * P : (u + 1) * P], ident[:])
@@ -155,8 +169,8 @@ def tile_moe_duo_silu_kernel(
             nc.scalar.copy(out=grouped[:].bitcast(F32).rearrange("p (c u) -> p c u", u=2), in_=turns[e][:].rearrange("p u c -> p c u"))
             quant(h_codes[e], h_scales[e], 0, C, grouped)
 
-        def second_product(e):
-            y = psum.tile([P, N // P, C], F32, name="y")
+        def second_product(e, bank):
+            y = psum.tile([P, N // P, C], F32, name="y%d" % e, offset=BANK * bank)
             for b in range(N // P):
                 cols = slice(b * P, (b + 1) * P)
                 nc.tensor.matmul_mx(out=y[:, b, :], lhsT=w2_codes[e][:, cols].bitcast(FP8X4), lhsT_scale=w2_scales[e][:, cols], rhs=h_codes[e][:].bitcast(FP8X4), rhs_scale=h_scales[e][:], start=True, stop=True)
@@ -175,15 +189,14 @@ def tile_moe_duo_silu_kernel(
 
         def scatter(e, b):
             cols = slice(e * C // 16, (e + 1) * C // 16)
-            g = 0 if e * C < gate_cut[1] else 1
-            first = e * C - gate_cut[g]
-            nc.vector.tensor_tensor(result[b][:].indirect(tok_list[:, cols]), y_sb[(e, b)], gate_sb[g][:, first : first + C], MULT)
+            nc.vector.tensor_tensor(result[b][:].indirect(tok_list[:, cols]), y_sb[(e, b)], gate_all[:, e * C : (e + 1) * C], MULT)
 
         nc.scalar.activation(out=warm[:], in_=warm[:], func=SILU)
         load_partner_scales(nc.gpsimd)
         nc.sync.dma_start(tok_list[:], offs)
         load_x(0)
         nc.sync.dma_start(par_list[:], offs2)
+        load_gate_row()
         load_w1(0, 0)
         load_token_scales(nc.sync)
         load_x(1)
@@ -192,19 +205,18 @@ def tile_moe_duo_silu_kernel(
         load_w1(1, 0)
         load_wp(0)
         load_w2(0)
-        load_gate(0)
         load_wp(1)
         load_w1(1, 1)
         load_w1(2, 0)
+        load_wp(2)
         load_w2(1)
         load_w1(2, 1)
         load_w1(3, 0)
-        load_wp(2)
         load_w1(3, 1)
-        load_w2(2)
         load_wp(3)
+        load_w2(2)
         load_w2(3)
-        load_gate(1)
+        spread_gate(0)
         gather("tw", 0)
         gather("pw", 0)
         gather("pb", 0)
@@ -228,57 +240,60 @@ def tile_moe_duo_silu_kernel(
         quant(w1_codes[1][1], w1_scales[1][1], 256, 512, staged["11b"])
         first_product(1, "p0 p1 o0 o1")
         regroup(0, 15360)
-        second_product(0)
+        second_product(0, 4)
         cast("20a", nc.vector.tensor_copy, w1_raw[2][0], 0, 256, 21504)
         cast("20b", nc.scalar.copy, w1_raw[2][0], 256, 512, 23552)
         quant(w1_codes[2][0], w1_scales[2][0], 0, 256, staged["20a"])
         quant(w1_codes[2][0], w1_scales[2][0], 256, 512, staged["20b"])
-        copy_y(0, 0, 21504)
+        copy_y(0, None, 21504)
         scatter(0, 0)
+        scatter(0, 1)
+        silu(1, 22528)
         cast("v1a", nc.scalar.copy, w2_raw[1], 0, 256, 25600)
         quant(w2_codes[1], w2_scales[1], 0, 256, staged["v1a"])
-        silu(1, 23552)
         regroup(1, 27648)
-        second_product(1)
+        second_product(1, 5)
         cast("21a", nc.vector.tensor_copy, w1_raw[2][1], 0, 256, 25600)
         cast("21b", nc.scalar.copy, w1_raw[2][1], 256, 512, 29696)
         quant(w1_codes[2][1], w1_scales[2][1], 0, 256, staged["21a"])
         quant(w1_codes[2][1], w1_scales[2][1], 256, 512, staged["21b"])
-        copy_y(0, 1, 25600)
-        scatter(0, 1)
-        copy_y(1, 0, 26112)
+        first_product(2, "p0 p1 o0 o1")
+        copy_y(1, 0, 25600)
         scatter(1, 0)
-        cast("30a", nc.scalar.copy, w1_raw[3][0], 0, 256, 31744)
-        cast("30b", nc.scalar.copy, w1_raw[3][0], 256, 512, 33792)
+        cast("30a", nc.vector.tensor_copy, w1_raw[3][0], 0, 256, 29696)
+        cast("30b", nc.scalar.copy, w1_raw[3][0], 256, 512, 31744)
         quant(w1_codes[3][0], w1_scales[3][0], 0, 256, staged["30a"])
         quant(w1_codes[3][0], w1_scales[3][0], 256, 512, staged["30b"])
-        first_product(2, "o0 o1 p0 p1")
-        silu(2, 35840)
+        silu(2, 29696)
         cast("31a", nc.vector.tensor_copy, w1_raw[3][1], 0, 256, 31744)
-        cast("31c", nc.scalar.copy, w1_raw[3][1], 384, 512, 37888)
-        cast("31b", nc.vector.tensor_copy, w1_raw[3][1], 256, 384, 33792)
+        cast("31c", nc.scalar.copy, w1_raw[3][1], 384, 512, 33792)
+        cast("31b", nc.vector.tensor_copy, w1_raw[3][1], 256, 384, 30720)
         quant(w1_codes[3][1], w1_scales[3][1], 0, 256, staged["31a"])
         quant(w1_codes[3][1], w1_scales[3][1], 256, 384, staged["31b"])
         quant(w1_codes[3][1], w1_scales[3][1], 384, 512, staged["31c"])
-        regroup(2, 31744)
-        copy_y(1, 1, 32768)
+        regroup(2, 30720)
         first_product(3, "o0 p0 p1 o1")
-        cast("v2a", nc.scalar.copy, w2_raw[2], 0, 256, 39936)
-        quant(w2_codes[2], w2_scales[2], 0, 256, staged["v2a"])
-        second_product(2)
+        copy_y(1, 1, 31744)
         scatter(1, 1)
-        cast("v3a", nc.vector.tensor_copy, w2_raw[3], 0, 256, 39936)
-        quant(w2_codes[3], w2_scales[3], 0, 256, staged["v3a"])
-        silu(3, 41984)
-        regroup(3, 44032)
-        copy_y(2, 0, 41984)
+        cast("v2a", nc.vector.tensor_copy, w2_raw[2], 0, 128, 32768)
+        cast("v2b", nc.scalar.copy, w2_raw[2], 128, 256, 35840)
+        quant(w2_codes[2], w2_scales[2], 0, 128, staged["v2a"])
+        quant(w2_codes[2], w2_scales[2], 128, 256, staged["v2b"])
+        silu(3, 37888)
+        second_product(2, 1)
+        cast("v3a", nc.vector.tensor_copy, w2_raw[3], 0, 128, 32768)
+        cast("v3b", nc.scalar.copy, w2_raw[3], 128, 256, 39936)
+        quant(w2_codes[3], w2_scales[3], 0, 128, staged["v3a"])
+        quant(w2_codes[3], w2_scales[3], 128, 256, staged["v3b"])
+        regroup(3, 41984)
+        copy_y(2, 0, 37888)
         scatter(2, 0)
-        second_product(3)
-        copy_y(2, 1, 42496)
+        second_product(3, 5)
+        copy_y(2, 1, 38400)
         scatter(2, 1)
-        copy_y(3, 0, 46080)
+        copy_y(3, 0, 44032)
         scatter(3, 0)
-        copy_y(3, 1, 48128)
+        copy_y(3, 1, 46080)
         scatter(3, 1)
         for b in range(N // P):
             nc.sync.dma_start(out=out[b * P : (b + 1) * P, :], in_=result[b][:])

@@ -126,11 +126,11 @@ def tile_moe_duo_silu_kernel(
             nc.vector.tensor_copy(tile[:], window.indirect(offsets[:]))
             gathered[(kind, s)] = tile
 
-        def cast(name, copy, raw, c0, c1, at):
+        def cast(name, copy, raw, c0, c1, at, walk=2):
             tile = stage.tile([P, (c1 - c0) * PACK], BF16, name="st" + name, offset=at, align_bytes=64)
             copy(
-                out=tile[:].rearrange("p (c i j) -> p c j i", i=2, j=PACK),
-                in_=raw[:, :, c0:c1].rearrange("p j (c i) -> p c j i", i=2),
+                out=tile[:].rearrange("p (c i j) -> p c j i", i=walk, j=PACK),
+                in_=raw[:, :, c0:c1].rearrange("p j (c i) -> p c j i", i=walk),
             )
             staged[name] = tile
 
@@ -234,14 +234,14 @@ def tile_moe_duo_silu_kernel(
         cast("v0a", nc.scalar.copy, w2_raw[0], 0, 256, 19456)
         quant(w2_codes[0], w2_scales[0], 0, 256, staged["v0a"])
         silu(0, 19456)
-        cast("11a", nc.vector.tensor_copy, w1_raw[1][1], 0, 256, 15360)
+        cast("11a", nc.vector.tensor_copy, w1_raw[1][1], 0, 256, 15360, 4)
         cast("11b", nc.scalar.copy, w1_raw[1][1], 256, 512, 21504)
         quant(w1_codes[1][1], w1_scales[1][1], 0, 256, staged["11a"])
         quant(w1_codes[1][1], w1_scales[1][1], 256, 512, staged["11b"])
         first_product(1, "p0 p1 o0 o1")
         regroup(0, 15360)
         second_product(0, 4)
-        cast("20a", nc.vector.tensor_copy, w1_raw[2][0], 0, 256, 21504)
+        cast("20a", nc.vector.tensor_copy, w1_raw[2][0], 0, 256, 21504, 4)
         cast("20b", nc.scalar.copy, w1_raw[2][0], 256, 512, 23552)
         quant(w1_codes[2][0], w1_scales[2][0], 0, 256, staged["20a"])
         quant(w1_codes[2][0], w1_scales[2][0], 256, 512, staged["20b"])
@@ -253,47 +253,51 @@ def tile_moe_duo_silu_kernel(
         quant(w2_codes[1], w2_scales[1], 0, 256, staged["v1a"])
         regroup(1, 27648)
         second_product(1, 5)
-        cast("21a", nc.vector.tensor_copy, w1_raw[2][1], 0, 256, 25600)
-        cast("21b", nc.scalar.copy, w1_raw[2][1], 256, 512, 29696)
-        quant(w1_codes[2][1], w1_scales[2][1], 0, 256, staged["21a"])
-        quant(w1_codes[2][1], w1_scales[2][1], 256, 512, staged["21b"])
+        cast("21a", nc.vector.tensor_copy, w1_raw[2][1], 0, 128, 25600, 4)
+        cast("21b", nc.scalar.copy, w1_raw[2][1], 128, 384, 29696)
+        cast("21c", nc.scalar.copy, w1_raw[2][1], 384, 512, 31744)
+        quant(w1_codes[2][1], w1_scales[2][1], 0, 128, staged["21a"])
+        quant(w1_codes[2][1], w1_scales[2][1], 128, 384, staged["21b"])
+        quant(w1_codes[2][1], w1_scales[2][1], 384, 512, staged["21c"])
         first_product(2, "p0 p1 o0 o1")
         copy_y(1, 0, 25600)
         scatter(1, 0)
-        cast("30a", nc.vector.tensor_copy, w1_raw[3][0], 0, 256, 29696)
-        cast("30b", nc.scalar.copy, w1_raw[3][0], 256, 512, 31744)
-        quant(w1_codes[3][0], w1_scales[3][0], 0, 256, staged["30a"])
-        quant(w1_codes[3][0], w1_scales[3][0], 256, 512, staged["30b"])
+        cast("30a", nc.vector.tensor_copy, w1_raw[3][0], 0, 128, 29696, 4)
+        cast("30b", nc.scalar.copy, w1_raw[3][0], 128, 384, 33792)
+        cast("30c", nc.scalar.copy, w1_raw[3][0], 384, 512, 35840)
+        quant(w1_codes[3][0], w1_scales[3][0], 0, 128, staged["30a"])
+        quant(w1_codes[3][0], w1_scales[3][0], 128, 384, staged["30b"])
+        quant(w1_codes[3][0], w1_scales[3][0], 384, 512, staged["30c"])
         silu(2, 29696)
-        cast("31a", nc.vector.tensor_copy, w1_raw[3][1], 0, 256, 31744)
-        cast("31c", nc.scalar.copy, w1_raw[3][1], 384, 512, 33792)
-        cast("31b", nc.vector.tensor_copy, w1_raw[3][1], 256, 384, 30720)
+        cast("31a", nc.vector.tensor_copy, w1_raw[3][1], 0, 256, 33792, 4)
+        cast("31c", nc.scalar.copy, w1_raw[3][1], 384, 512, 37888)
+        cast("31b", nc.vector.tensor_copy, w1_raw[3][1], 256, 384, 35840, 4)
         quant(w1_codes[3][1], w1_scales[3][1], 0, 256, staged["31a"])
         quant(w1_codes[3][1], w1_scales[3][1], 256, 384, staged["31b"])
         quant(w1_codes[3][1], w1_scales[3][1], 384, 512, staged["31c"])
-        regroup(2, 30720)
+        regroup(2, 35840)
         first_product(3, "o0 p0 p1 o1")
-        copy_y(1, 1, 31744)
+        copy_y(1, 1, 33792)
         scatter(1, 1)
-        cast("v2a", nc.vector.tensor_copy, w2_raw[2], 0, 128, 32768)
-        cast("v2b", nc.scalar.copy, w2_raw[2], 128, 256, 35840)
+        cast("v2a", nc.vector.tensor_copy, w2_raw[2], 0, 128, 34816, 4)
+        cast("v2b", nc.scalar.copy, w2_raw[2], 128, 256, 39936)
         quant(w2_codes[2], w2_scales[2], 0, 128, staged["v2a"])
         quant(w2_codes[2], w2_scales[2], 128, 256, staged["v2b"])
-        silu(3, 37888)
+        silu(3, 41984)
         second_product(2, 1)
-        cast("v3a", nc.vector.tensor_copy, w2_raw[3], 0, 128, 32768)
-        cast("v3b", nc.scalar.copy, w2_raw[3], 128, 256, 39936)
+        cast("v3a", nc.vector.tensor_copy, w2_raw[3], 0, 128, 34816, 4)
+        cast("v3b", nc.scalar.copy, w2_raw[3], 128, 256, 44032)
         quant(w2_codes[3], w2_scales[3], 0, 128, staged["v3a"])
         quant(w2_codes[3], w2_scales[3], 128, 256, staged["v3b"])
-        regroup(3, 41984)
-        copy_y(2, 0, 37888)
+        regroup(3, 46080)
+        copy_y(2, 0, 41984)
         scatter(2, 0)
         second_product(3, 5)
-        copy_y(2, 1, 38400)
+        copy_y(2, 1, 42496)
         scatter(2, 1)
-        copy_y(3, 0, 44032)
+        copy_y(3, 0, 48128)
         scatter(3, 0)
-        copy_y(3, 1, 46080)
+        copy_y(3, 1, 50176)
         scatter(3, 1)
         for b in range(N // P):
             nc.sync.dma_start(out=out[b * P : (b + 1) * P, :], in_=result[b][:])

@@ -34,270 +34,294 @@ def tile_moe_duo_silu_kernel(
         stage = ctx.enter_context(tc.tile_pool(name="stage", bufs=1))
         psum = ctx.enter_context(tc.psum_pool(name="psum", bufs=1))
 
-        xs = stage.tile([P, PASSES * WINDOW], U8, name="xs", offset=0, align_bytes=64)
+        places = {"top": (0, 0)}
+
+        def placed(name, columns, dtype, size, over=None, room=0):
+            if over is None:
+                at = places["top"][0]
+                room = max(room, (columns * size + 63) // 64 * 64)
+                places["top"] = (at + room, 0)
+            else:
+                tenant, skip = over if isinstance(over, tuple) else (over, 0)
+                at, room = places[tenant][0] + skip, places[tenant][1] - skip
+                assert columns * size <= room
+            places[name] = (at, room)
+            return stage.tile([P, columns], dtype, name=name, offset=at, align_bytes=64)
+
+        xs = placed("xs0", WINDOW, U8, 1)
+        moved = keep.tile([P, E * C], U8, name="moved", align_bytes=64)
         wps = keep.tile([P, E * PASSES * H], U8, name="wps", align_bytes=64)
         nc.vector.memset(xs[:].bitcast(I32), 0)
         warm = keep.tile([P, 1], F32, name="warm")
         nc.vector.memset(warm[:], 0.0)
         nc.vector.memset(wps[:].bitcast(I32), 0)
+        nc.vector.memset(moved[:].bitcast(I32), 0)
         ident = keep.tile([P, P], F32, name="ident")
         make_identity(nc, ident[:])
 
         tok_list = keep.tile([P, T // 16], U16, name="tok_list")
         par_list = keep.tile([P, T // 16], U16, name="par_list")
-        xw = [stage.tile([P, WINDOW], I32, name="xw%d" % s, offset=1536 + 2816 * s, align_bytes=64) for s in range(PASSES)]
+        xw = [placed("xw%d" % s, WINDOW, I32, 4) for s in range(PASSES)]
         for s in range(PASSES):
             nc.vector.memset(xw[s][:, T:WINDOW], 0)
-        w1_raw = [[keep.tile([P, PACK, H], F32, name="w1raw%d_%d" % (e, s)) for s in range(PASSES)] for e in range(E)]
-        w2_raw = [keep.tile([P, PACK, N], F32, name="w2raw%d" % e) for e in range(E)]
-        wpw = [keep.tile([P, PASSES * 2 * H], U8, name="wpw%d" % e, align_bytes=64) for e in range(E)]
         result = [keep.tile([P, T], F32, name="result%d" % b) for b in range(N // P)]
-        w1_codes = [[keep.tile([P, H], U32, name="w1c%d_%d" % (e, s), align_bytes=64) for s in range(PASSES)] for e in range(E)]
-        w1_scales = [[keep.tile([P, H], U8, name="w1s%d_%d" % (e, s), align_bytes=64) for s in range(PASSES)] for e in range(E)]
-        w1_codes[0][0] = stage.tile([P, H], U32, name="first_codes", offset=1536 + 2816, align_bytes=64)
-        w1_scales[0][1] = stage.tile([P, H], U8, name="second_scales", offset=0, align_bytes=64)
-        w1_scales[1][0] = stage.tile([P, H], U8, name="third_scales", offset=512, align_bytes=64)
-        w2_codes = [keep.tile([P, N], U32, name="w2c%d" % e, align_bytes=64) for e in range(E)]
-        w2_scales = [keep.tile([P, N], U8, name="w2s%d" % e, align_bytes=64) for e in range(E)]
-        h_codes = [keep.tile([P, C], U32, name="hc%d" % e, align_bytes=64) for e in range(E)]
-        h_scales = [keep.tile([P, C], U8, name="hs%d" % e, align_bytes=64) for e in range(E)]
-        xs_rows = x_scales.bitcast(I32).rearrange("s (q r) n -> r q s n", r=4)
         wps_rows = wp_scales.bitcast(I32).rearrange("e s (q r) n -> r q (e s) n", r=4)
+        gate_cols = keep.tile([P, PACK], F32, name="gate_cols")
+        gate_all = keep.tile([P, E * C], F32, name="gate_all")
+
+        raw = {}
+        wpw = {}
+        gathered = {}
+        staged = {}
+        codes = {}
+        scales = {}
+        accs = {}
+        hrows = {}
+        turns = {}
+        ys = {}
+        y_sb = {}
 
         def load_x(s):
             nc.sync.dma_start(out=xw[s][:, 0:T], in_=x_words[s].rearrange("p t d -> p (t d)").bitcast(I32))
 
         def load_token_scales(queue):
-            for r in range(4):
-                rows = xs[r:P:32, :].bitcast(I32).rearrange("q (s n) -> q s n", s=PASSES)
-                queue.dma_start(out=rows[:, :, 0 : T // 4], in_=xs_rows[r])
+            for q in range(4):
+                queue.dma_start(out=xs[32 * q : 32 * q + 8, 0:T].bitcast(I32), in_=x_scales[:, 4 * q : 4 * q + 4, :].bitcast(I32))
 
-        def load_packed_scales(queue):
-            for r in range(4):
-                queue.dma_start(out=xs[4 + r : P : 32, WINDOW : WINDOW + T].bitcast(I32), in_=xs_rows[r][:, 0, :])
+        def move_plane(queue):
+            for r0, r1 in ((0, 64), (64, 96), (96, 100)):
+                queue.dma_start(out=moved[r0:r1, :].bitcast(I32), in_=gathered[("pb", 0)][r0 + 4 : r1 + 4, :].bitcast(I32))
 
         def load_partner_scales(queue):
             for r in range(4):
                 queue.dma_start(out=wps[r:P:32, :].bitcast(I32).rearrange("q (g n) -> q g n", g=E * PASSES), in_=wps_rows[r])
 
-        def load_w1(e, s):
-            rows = w1[e, s * K_PASS : (s + 1) * K_PASS, :]
-            nc.sync.dma_start(out=w1_raw[e][s][:], in_=rows.rearrange("(p j) w -> p j w", j=PACK))
+        def load_rows(key, rows, c0, c1):
+            tile = placed("raw%s_%d" % (key, c0), PACK * (c1 - c0), F32, 4)[:].rearrange("p (j w) -> p j w", j=PACK)
+            nc.sync.dma_start(out=tile, in_=rows[:, c0:c1].rearrange("(p j) w -> p j w", j=PACK))
+            raw.setdefault(key, []).append((c0, c1, tile))
 
-        last_raw = [keep.tile([P, PACK, H // 2], F32, name="last_raw%d" % half) for half in range(2)]
+        def load_w1(e, s, c0=0, c1=H):
+            load_rows("%d%d" % (e, s), w1[e, s * K_PASS : (s + 1) * K_PASS, :], c0, c1)
 
-        def load_last(half):
-            rows = w1[E - 1, K_PASS : 2 * K_PASS, half * H // 2 : (half + 1) * H // 2]
-            nc.sync.dma_start(out=last_raw[half][:], in_=rows.rearrange("(p j) w -> p j w", j=PACK))
+        def load_w2(e, c0=0, c1=N):
+            load_rows("v%d" % e, w2[e], c0, c1)
 
-        def load_w2(e):
-            nc.sync.dma_start(out=w2_raw[e][:], in_=w2[e].rearrange("(p j) w -> p j w", j=PACK))
-
-        def load_wp(e):
+        def load_wp(e0, e1):
+            tile = placed("wpw%d" % e0, (e1 - e0) * PASSES * 2 * H, U8, 1)
             nc.sync.dma_start(
-                out=wpw[e][:].bitcast(I32).rearrange("p (s n) -> p s n", s=PASSES),
-                in_=wp_words[e].bitcast(I32).rearrange("s p n -> p s n"),
+                out=tile[:].bitcast(I32).rearrange("p (g n) -> p g n", g=(e1 - e0) * PASSES),
+                in_=wp_words[e0:e1].bitcast(I32).rearrange("e s p n -> p (e s) n"),
             )
+            for e in range(e0, e1):
+                for s in range(PASSES):
+                    g = (e - e0) * PASSES + s
+                    wpw[(e, s)] = tile[:, g * 2 * H : (g + 1) * 2 * H]
 
-        gate_cols = keep.tile([P, PACK], F32, name="gate_cols")
-        gate_all = keep.tile([P, E * C], F32, name="gate_all")
+        def load_gate_row(queue):
+            queue.dma_start(out=gate_cols[:], in_=gate[0].rearrange("(p j) -> p j", j=PACK))
 
-        def load_gate_row():
-            nc.sync.dma_start(out=gate_cols[:], in_=gate[0].rearrange("(p j) -> p j", j=PACK))
-
-        def spread_gate(at):
+        def spread_gate():
             spread = psum.tile([P, PACK, P], F32, name="spread", offset=BANK * 6)
             for j in range(PACK):
                 nc.tensor.transpose(spread[:, j, :], gate_cols[:, j : j + 1].to_broadcast([P, P]), ident[:])
             nc.scalar.copy(out=gate_all[:].rearrange("p (n j) -> p n j", j=PACK), in_=spread[:].rearrange("p j n -> p n j"))
 
-        gathered = {}
-        staged = {}
-        accs = {}
-        turns = {}
-        ys = {}
-        y_sb = {}
-
-        def gather(kind, s):
+        def gather(kind, s, over=None):
             dtype = U32 if kind[1] == "w" else U8
-            tile = keep.tile([P, E * C], dtype, name="%s%d" % (kind, s), align_bytes=64)
+            tile = placed("%s%d" % (kind, s), E * C, dtype, 4 if kind[1] == "w" else 1, over)
             offsets = tok_list if kind[0] == "t" else par_list
-            window = xw[s][:].bitcast(U32) if kind[1] == "w" else xs[:, s * WINDOW : (s + 1) * WINDOW]
+            window = xw[s][:].bitcast(U32) if kind[1] == "w" else xs[:]
             nc.vector.tensor_copy(tile[:], window.indirect(offsets[:]))
             gathered[(kind, s)] = tile
 
-        def cast(name, copy, raw, c0, c1, at, walk=2):
-            tile = stage.tile([P, (c1 - c0) * PACK], BF16, name="st" + name, offset=at, align_bytes=64)
+        def cast(key, engine, c0, c1, over=None, into=None):
+            r0, r1, source = [piece for piece in raw[key] if piece[0] <= c0 and c1 <= piece[1]][0]
+            if into is None:
+                into = (c0, c1)
+            if (key, into) not in staged:
+                staged[(key, into)] = placed("st%s_%d" % (key, into[0]), (into[1] - into[0]) * PACK, BF16, 2, over)
+            target = staged[(key, into)][:, (c0 - into[0]) * PACK : (c1 - into[0]) * PACK]
+            copy, walk = (nc.vector.tensor_copy, 4) if engine == "V" else (nc.scalar.copy, 2)
             copy(
-                out=tile[:].rearrange("p (c i j) -> p c j i", i=walk, j=PACK),
-                in_=raw[:, :, c0:c1].rearrange("p j (c i) -> p c j i", i=walk),
+                out=target.rearrange("p (c i j) -> p c j i", i=walk, j=PACK),
+                in_=source[:, :, c0 - r0 : c1 - r0].rearrange("p j (c i) -> p c j i", i=walk),
             )
-            staged[name] = tile
 
-        def quant(codes, scales, c0, c1, tile):
-            nc.vector.quantize_mx(out=codes[:, c0:c1].bitcast(FP8X4), scales=scales[:, c0:c1], in_=tile[:])
+        def quant(key, c0, c1, codes_over=None, scales_over=None, room=0, source=None):
+            width = C if key[0] == "h" else N if key[0] == "v" else H
+            if key not in codes:
+                codes[key] = placed("codes" + key, width, U32, 4, codes_over, room)
+                scales[key] = placed("scales" + key, width, U8, 1, scales_over)
+            nc.vector.quantize_mx(out=codes[key][:, c0:c1].bitcast(FP8X4), scales=scales[key][:, c0:c1], in_=staged[(key, source or (c0, c1))][:, (c0 - (source or (c0, c1))[0]) * PACK : (c1 - (source or (c0, c1))[0]) * PACK])
 
-        def first_product(e, order):
+        def first_passes(e, order, start=False, stop=False, bank=None):
             slots = slice(e * C, (e + 1) * C)
-            acc = psum.tile([P, H], F32, name="acc%d" % e, offset=BANK * (e % 2))
-            passes = {}
-            for s in range(PASSES):
-                g = e * PASSES + s
-                first_row = 4 * (1 - s)
-                passes["o%d" % s] = (gathered[("tw", s)][:, slots], gathered[("tb", 1)][first_row:P, slots], w1_codes[e][s][:].bitcast(FP8X4), w1_scales[e][s][:])
-                passes["p%d" % s] = (gathered[("pw", s)][:, slots], gathered[("pb", s)][:, slots], wpw[e][:, s * 2 * H : (s + 1) * 2 * H].bitcast(FP4X4), wps[:, g * H : (g + 1) * H])
-            for n, key in enumerate(order.split()):
-                words, word_scales, weights, weight_scales = passes[key]
-                nc.tensor.matmul_mx(out=acc[:], lhsT=words.bitcast(FP8X4), lhsT_scale=word_scales, rhs=weights, rhs_scale=weight_scales, start=(n == 0), stop=(n == 3))
-            accs[e] = acc
+            if start:
+                accs[e] = psum.tile([P, H], F32, name="acc%d" % e, offset=BANK * (e % 2 if bank is None else bank))
+            names = order.split()
+            for n, name in enumerate(names):
+                s = int(name[1])
+                if name[0] == "o":
+                    key = "%d%d" % (e, s)
+                    operands = (gathered[("tw", s)][:, slots], gathered[("tb", 0)][4 * s : P, slots], codes[key][:].bitcast(FP8X4), scales[key][:])
+                else:
+                    g = e * PASSES + s
+                    operands = (gathered[("pw", s)][:, slots], (moved if s else gathered[("pb", 0)])[:, slots], wpw[(e, s)].bitcast(FP4X4), wps[:, g * H : (g + 1) * H])
+                nc.tensor.matmul_mx(out=accs[e][:], lhsT=operands[0].bitcast(FP8X4), lhsT_scale=operands[1], rhs=operands[2], rhs_scale=operands[3], start=(start and n == 0), stop=(stop and n == len(names) - 1))
 
-        def silu(e, at):
-            rows = stage.tile([P, H], BF16, name="hrows%d" % e, offset=at, align_bytes=64)
-            nc.scalar.activation(
-                out=rows[:].rearrange("c (u p d) -> c u p d", u=2, d=2),
-                in_=accs[e][:].rearrange("c (p u d) -> c u p d", u=2, d=2),
-                func=SILU,
-            )
+        def silu(e, over=None, halves=False, room=0):
+            rows = placed("hrows%d" % e, H, BF16, 2, over, room)
             turned = psum.tile([P, 2, C], F32, name="turned%d" % e, offset=BANK * (2 + e % 2))
             pairs = rows[:].bitcast(F32)
+            target = rows[:].rearrange("c (u p d) -> c u p d", u=2, d=2)
+            source = accs[e][:].rearrange("c (p u d) -> c u p d", u=2, d=2)
+            if not halves:
+                nc.scalar.activation(out=target, in_=source, func=SILU)
             for u in range(2):
+                if halves:
+                    nc.scalar.activation(out=target[:, u, :, :], in_=source[:, u, :, :], func=SILU)
                 nc.tensor.transpose(turned[:, u, :], pairs[:, u * P : (u + 1) * P], ident[:])
             turns[e] = turned
 
-        def regroup(e, at):
-            grouped = stage.tile([P, C * PACK], BF16, name="hg%d" % e, offset=at, align_bytes=64)
+        def regroup(e, over=None, room=0):
+            grouped = placed("hg%d" % e, C * PACK, BF16, 2, over, room)
             nc.scalar.copy(out=grouped[:].bitcast(F32).rearrange("p (c u) -> p c u", u=2), in_=turns[e][:].rearrange("p u c -> p c u"))
-            quant(h_codes[e], h_scales[e], 0, C, grouped)
+            staged[("h%d" % e, (0, C))] = grouped
 
-        def second_product(e, bank):
-            y = psum.tile([P, N // P, C], F32, name="y%d" % e, offset=BANK * bank)
-            for b in range(N // P):
+        def second_product(e, bank, blocks=(0, 1)):
+            y = psum.tile([P, len(blocks), C], F32, name="y%d_%d" % (e, blocks[0]), offset=BANK * bank)
+            v, h = "v%d" % e, "h%d" % e
+            for n, b in enumerate(blocks):
                 cols = slice(b * P, (b + 1) * P)
-                nc.tensor.matmul_mx(out=y[:, b, :], lhsT=w2_codes[e][:, cols].bitcast(FP8X4), lhsT_scale=w2_scales[e][:, cols], rhs=h_codes[e][:].bitcast(FP8X4), rhs_scale=h_scales[e][:], start=True, stop=True)
+                nc.tensor.matmul_mx(out=y[:, n, :], lhsT=codes[v][:, cols].bitcast(FP8X4), lhsT_scale=scales[v][:, cols], rhs=codes[h][:].bitcast(FP8X4), rhs_scale=scales[h][:], start=True, stop=True)
+                ys[(e, b)] = y[:, n, :]
             ys[e] = y
 
-        def copy_y(e, b, at):
+        def copy_y(e, b=None, over=None, room=0):
             if b is None:
-                both = stage.tile([P, N // P, C], F32, name="ysb%d" % e, offset=at, align_bytes=64)
-                nc.scalar.copy(out=both[:], in_=ys[e][:])
-                y_sb[(e, 0)] = both[:, 0, :]
-                y_sb[(e, 1)] = both[:, 1, :]
+                both = placed("ysb%d" % e, N // P * C, F32, 4, over)
+                nc.scalar.copy(out=both[:].rearrange("p (b c) -> p b c", b=N // P), in_=ys[e][:])
+                y_sb[(e, 0)] = both[:, 0:C]
+                y_sb[(e, 1)] = both[:, C : 2 * C]
             else:
-                one = stage.tile([P, C], F32, name="ysb%d_%d" % (e, b), offset=at, align_bytes=64)
-                nc.scalar.copy(out=one[:], in_=ys[e][:, b, :])
+                one = placed("ysb%d_%d" % (e, b), C, F32, 4, over, room)
+                nc.scalar.copy(out=one[:], in_=ys[(e, b)])
                 y_sb[(e, b)] = one[:]
 
         def scatter(e, b):
             cols = slice(e * C // 16, (e + 1) * C // 16)
             nc.vector.tensor_tensor(result[b][:].indirect(tok_list[:, cols]), y_sb[(e, b)], gate_all[:, e * C : (e + 1) * C], MULT)
 
+        def store(b):
+            nc.sync.dma_start(out=out[b * P : (b + 1) * P, :], in_=result[b][:])
+
+        load_gate_row(nc.scalar)
         nc.scalar.activation(out=warm[:], in_=warm[:], func=SILU)
         load_partner_scales(nc.gpsimd)
         nc.sync.dma_start(tok_list[:], offs)
         load_x(0)
         nc.sync.dma_start(par_list[:], offs2)
-        load_gate_row()
         load_w1(0, 0)
         load_token_scales(nc.sync)
         load_x(1)
         load_w1(0, 1)
-        load_packed_scales(nc.sync)
+        load_wp(0, 1)
         load_w1(1, 0)
-        load_wp(0)
-        load_w2(0)
-        load_wp(1)
         load_w1(1, 1)
-        load_w1(2, 0)
-        load_wp(2)
+        load_wp(1, 2)
+        load_w2(0)
         load_w2(1)
+        load_w1(2, 0, 0, 256)
+        load_w1(2, 0, 256, 512)
         load_w1(2, 1)
+        load_wp(2, 3)
         load_w1(3, 0)
-        load_w1(3, 1)
-        load_wp(3)
+        load_wp(3, 4)
+        load_w1(3, 1, 0, 256)
+        load_w1(3, 1, 256, 512)
         load_w2(2)
         load_w2(3)
-        spread_gate(0)
+        spread_gate()
         gather("tw", 0)
         gather("pw", 0)
         gather("pb", 0)
+        gather("tb", 0)
         gather("tw", 1)
         gather("pw", 1)
-        gather("pb", 1)
-        gather("tb", 1)
-        cast("00a", nc.scalar.copy, w1_raw[0][0], 0, 512, 7168)
-        quant(w1_codes[0][0], w1_scales[0][0], 0, 512, staged["00a"])
-        cast("01a", nc.scalar.copy, w1_raw[0][1], 0, 512, 11264)
-        quant(w1_codes[0][1], w1_scales[0][1], 0, 512, staged["01a"])
-        first_product(0, "p0 p1 o0 o1")
-        cast("10a", nc.scalar.copy, w1_raw[1][0], 0, 512, 15360)
-        quant(w1_codes[1][0], w1_scales[1][0], 0, 512, staged["10a"])
-        cast("v0a", nc.scalar.copy, w2_raw[0], 0, 256, 19456)
-        quant(w2_codes[0], w2_scales[0], 0, 256, staged["v0a"])
-        silu(0, 19456)
-        cast("11a", nc.vector.tensor_copy, w1_raw[1][1], 0, 256, 15360, 4)
-        cast("11b", nc.scalar.copy, w1_raw[1][1], 256, 512, 21504)
-        quant(w1_codes[1][1], w1_scales[1][1], 0, 256, staged["11a"])
-        quant(w1_codes[1][1], w1_scales[1][1], 256, 512, staged["11b"])
-        first_product(1, "p0 p1 o0 o1")
-        regroup(0, 15360)
+        cast("00", "S", 0, 512)
+        move_plane(nc.scalar)
+        quant("00", 0, 512, codes_over="xw1")
+        cast("01", "S", 0, 512)
+        quant("01", 0, 512)
+        first_passes(0, "p0 p1 o0 o1", start=True, stop=True)
+        cast("10", "S", 256, 512, into=(0, 512))
+        cast("10", "V", 0, 256, into=(0, 512))
+        silu(0, over="raw10_0")
+        quant("10", 0, 512)
+        first_passes(1, "o0", start=True)
+        cast("11", "V", 0, 256)
+        cast("11", "S", 256, 512)
+        quant("11", 0, 256)
+        regroup(0, over="st11_0")
+        quant("11", 256, 512)
+        first_passes(1, "p0 p1 o1", stop=True)
+        quant("h0", 0, C)
+        cast("v0", "S", 0, 256)
+        silu(1, over="rawv0_0")
+        cast("v1", "V", 0, 256)
+        quant("v0", 0, 256)
         second_product(0, 4)
-        cast("20a", nc.vector.tensor_copy, w1_raw[2][0], 0, 256, 21504, 4)
-        cast("20b", nc.scalar.copy, w1_raw[2][0], 256, 512, 23552)
-        quant(w1_codes[2][0], w1_scales[2][0], 0, 256, staged["20a"])
-        quant(w1_codes[2][0], w1_scales[2][0], 256, 512, staged["20b"])
-        copy_y(0, None, 21504)
+        quant("v1", 0, 256)
+        cast("20", "V", 0, 256, into=(0, 512))
+        regroup(1)
+        copy_y(0, over="hrows1")
+        quant("h1", 0, C)
+        second_product(1, 5)
         scatter(0, 0)
         scatter(0, 1)
-        silu(1, 22528)
-        cast("v1a", nc.scalar.copy, w2_raw[1], 0, 256, 25600)
-        quant(w2_codes[1], w2_scales[1], 0, 256, staged["v1a"])
-        regroup(1, 27648)
-        second_product(1, 5)
-        cast("21a", nc.vector.tensor_copy, w1_raw[2][1], 0, 128, 25600, 4)
-        cast("21b", nc.scalar.copy, w1_raw[2][1], 128, 384, 29696)
-        cast("21c", nc.scalar.copy, w1_raw[2][1], 384, 512, 31744)
-        quant(w1_codes[2][1], w1_scales[2][1], 0, 128, staged["21a"])
-        quant(w1_codes[2][1], w1_scales[2][1], 128, 384, staged["21b"])
-        quant(w1_codes[2][1], w1_scales[2][1], 384, 512, staged["21c"])
-        first_product(2, "p0 p1 o0 o1")
-        copy_y(1, 0, 25600)
+        cast("20", "S", 256, 512, into=(0, 512))
+        copy_y(1, over="raw20_256")
+        quant("20", 0, 512)
         scatter(1, 0)
-        cast("30a", nc.vector.tensor_copy, w1_raw[3][0], 0, 128, 29696, 4)
-        cast("30b", nc.scalar.copy, w1_raw[3][0], 128, 384, 33792)
-        cast("30c", nc.scalar.copy, w1_raw[3][0], 384, 512, 35840)
-        quant(w1_codes[3][0], w1_scales[3][0], 0, 128, staged["30a"])
-        quant(w1_codes[3][0], w1_scales[3][0], 128, 384, staged["30b"])
-        quant(w1_codes[3][0], w1_scales[3][0], 384, 512, staged["30c"])
-        silu(2, 29696)
-        cast("31a", nc.vector.tensor_copy, w1_raw[3][1], 0, 256, 33792, 4)
-        cast("31c", nc.scalar.copy, w1_raw[3][1], 384, 512, 37888)
-        cast("31b", nc.vector.tensor_copy, w1_raw[3][1], 256, 384, 35840, 4)
-        quant(w1_codes[3][1], w1_scales[3][1], 0, 256, staged["31a"])
-        quant(w1_codes[3][1], w1_scales[3][1], 256, 384, staged["31b"])
-        quant(w1_codes[3][1], w1_scales[3][1], 384, 512, staged["31c"])
-        regroup(2, 35840)
-        first_product(3, "o0 p0 p1 o1")
-        copy_y(1, 1, 33792)
+        first_passes(2, "p0 p1 o0", start=True)
         scatter(1, 1)
-        cast("v2a", nc.vector.tensor_copy, w2_raw[2], 0, 128, 34816, 4)
-        cast("v2b", nc.scalar.copy, w2_raw[2], 128, 256, 39936)
-        quant(w2_codes[2], w2_scales[2], 0, 128, staged["v2a"])
-        quant(w2_codes[2], w2_scales[2], 128, 256, staged["v2b"])
-        silu(3, 41984)
-        second_product(2, 1)
-        cast("v3a", nc.vector.tensor_copy, w2_raw[3], 0, 128, 34816, 4)
-        cast("v3b", nc.scalar.copy, w2_raw[3], 128, 256, 44032)
-        quant(w2_codes[3], w2_scales[3], 0, 128, staged["v3a"])
-        quant(w2_codes[3], w2_scales[3], 128, 256, staged["v3b"])
-        regroup(3, 46080)
-        copy_y(2, 0, 41984)
+        cast("21", "S", 0, 512)
+        quant("21", 0, 512)
+        first_passes(2, "o1", stop=True)
+        cast("30", "S", 256, 512, into=(0, 512))
+        cast("30", "V", 0, 256, into=(0, 512), over=None)
+        silu(2, over="raw30_0")
+        quant("30", 0, 512)
+        first_passes(3, "p0 p1 o0", start=True)
+        cast("31", "V", 0, 256)
+        quant("31", 0, 256)
+        cast("31", "S", 384, 512, into=(256, 512))
+        cast("31", "V", 256, 384, into=(256, 512))
+        regroup(2, over="raw31_256")
+        quant("31", 256, 512)
+        first_passes(3, "o1", stop=True)
+        cast("v2", "S", 128, 256)
+        cast("v2", "V", 0, 128)
+        quant("h2", 0, C, codes_over=None)
+        quant("v2", 0, 128)
+        second_product(2, 4, (0,))
+        quant("v2", 128, 256)
+        silu(3)
+        second_product(2, 5, (1,))
+        copy_y(2, 0)
+        cast("v3", "V", 0, 256)
         scatter(2, 0)
-        second_product(3, 5)
-        copy_y(2, 1, 42496)
+        quant("v3", 0, 256)
+        regroup(3)
+        copy_y(2, 1, over="hrows3")
+        quant("h3", 0, C)
+        second_product(3, 6, (0,))
+        second_product(3, 7, (1,))
         scatter(2, 1)
-        copy_y(3, 0, 48128)
+        copy_y(3, 0)
+        copy_y(3, 1)
         scatter(3, 0)
-        copy_y(3, 1, 50176)
+        store(0)
         scatter(3, 1)
-        for b in range(N // P):
-            nc.sync.dma_start(out=out[b * P : (b + 1) * P, :], in_=result[b][:])
+        store(1)

@@ -89,8 +89,7 @@ def tile_moe_duo_silu_kernel(
                 queue.dma_start(out=xs[32 * q : 32 * q + 8, 0:T].bitcast(I32), in_=x_scales[:, 4 * q : 4 * q + 4, :].bitcast(I32))
 
         def move_plane(queue):
-            for r0, r1 in ((0, 64), (64, 96), (96, 100)):
-                queue.dma_start(out=moved[r0:r1, :].bitcast(I32), in_=gathered[("pb", 0)][r0 + 4 : r1 + 4, :].bitcast(I32))
+            queue.dma_start(out=moved[0:100, :].bitcast(I32), in_=gathered[("pb", 0)][4:104, :].bitcast(I32))
 
         def load_partner_scales(queue):
             for r in range(4):
@@ -218,7 +217,6 @@ def tile_moe_duo_silu_kernel(
 
         load_gate_row(nc.scalar)
         nc.scalar.activation(out=warm[:], in_=warm[:], func=SILU)
-        load_partner_scales(nc.gpsimd)
         nc.sync.dma_start(tok_list[:], offs)
         load_x(0)
         nc.sync.dma_start(par_list[:], offs2)
@@ -226,6 +224,7 @@ def tile_moe_duo_silu_kernel(
         load_token_scales(nc.sync)
         load_x(1)
         load_w1(0, 1)
+        load_partner_scales(nc.sync)
         load_wp(0, 1)
         load_w1(1, 0)
         load_w1(1, 1)
@@ -254,7 +253,7 @@ def tile_moe_duo_silu_kernel(
         quant("00", 0, 512, codes_over="xw1")
         cast("01", "S", 0, 512)
         quant("01", 0, 512)
-        first_passes(0, "p0 p1 o0 o1", start=True, stop=True)
+        first_passes(0, "p0 o0 o1 p1", start=True, stop=True)
         cast("10", "S", 256, 512, into=(0, 512))
         cast("10", "V", 0, 256, into=(0, 512))
         silu(0, over="raw10_0")
@@ -268,12 +267,12 @@ def tile_moe_duo_silu_kernel(
         first_passes(1, "p0 p1 o1", stop=True)
         quant("h0", 0, C)
         cast("v0", "S", 0, 256)
-        silu(1, over="rawv0_0")
-        cast("v1", "V", 0, 256)
+        silu(1)
+        cast("v1", "S", 0, 256)
         quant("v0", 0, 256)
         second_product(0, 4)
-        quant("v1", 0, 256)
         cast("20", "V", 0, 256, into=(0, 512))
+        quant("v1", 0, 256)
         regroup(1)
         copy_y(0, over="hrows1")
         quant("h1", 0, C)

@@ -236,9 +236,8 @@ def tile_moe_duo_silu_kernel(
         load_w1(2, 1)
         load_wp(2, 3)
         load_w1(3, 0)
+        load_w1(3, 1)
         load_wp(3, 4)
-        load_w1(3, 1, 0, 256)
-        load_w1(3, 1, 256, 512)
         load_w2(2)
         load_w2(3)
         spread_gate()
@@ -292,14 +291,15 @@ def tile_moe_duo_silu_kernel(
         cast("30", "V", 0, 256, into=(0, 512), over=None)
         silu(2, over="raw30_0")
         quant("30", 0, 512)
-        first_passes(3, "p0 p1 o0", start=True)
+        first_passes(3, "o0", start=True)
         cast("31", "V", 0, 256)
+        cast("31", "S", 384, 512)
+        cast("31", "V", 256, 384)
+        regroup(2, over="raw31_0")
         quant("31", 0, 256)
-        cast("31", "S", 384, 512, into=(256, 512))
-        cast("31", "V", 256, 384, into=(256, 512))
-        regroup(2, over="raw31_256")
-        quant("31", 256, 512)
-        first_passes(3, "o1", stop=True)
+        quant("31", 256, 384)
+        quant("31", 384, 512)
+        first_passes(3, "p0 p1 o1", stop=True)
         cast("v2", "S", 128, 256)
         cast("v2", "V", 0, 128)
         quant("h2", 0, C, codes_over=None)

@@ -21,7 +21,7 @@ P = 128
 PACK = 4
 K_PASS = P * PACK
 PASSES = K // K_PASS
-WINDOW = 704
+WAVE = 2 * C
 BANK = 2048
 
 
@@ -48,23 +48,20 @@ def tile_moe_duo_silu_kernel(
             places[name] = (at, room)
             return stage.tile([P, columns], dtype, name=name, offset=at, align_bytes=64)
 
-        xs = placed("xs0", WINDOW, U8, 1)
-        moved = keep.tile([P, E * C], U8, name="moved", align_bytes=64)
+        xs = placed("xs0", PASSES * T, U8, 1)
         wps = keep.tile([P, E * PASSES * H], U8, name="wps", align_bytes=64)
         nc.vector.memset(xs[:].bitcast(I32), 0)
         warm = keep.tile([P, 1], F32, name="warm")
         nc.vector.memset(warm[:], 0.0)
         nc.vector.memset(wps[:].bitcast(I32), 0)
-        nc.vector.memset(moved[:].bitcast(I32), 0)
         ident = keep.tile([P, P], F32, name="ident")
         make_identity(nc, ident[:])
 
         tok_list = keep.tile([P, T // 16], U16, name="tok_list")
         par_list = keep.tile([P, T // 16], U16, name="par_list")
-        xw = [placed("xw%d" % s, WINDOW, I32, 4) for s in range(PASSES)]
-        for s in range(PASSES):
-            nc.vector.memset(xw[s][:, T:WINDOW], 0)
+        xw = [placed("xw%d" % s, T, I32, 4) for s in range(PASSES)]
         result = [keep.tile([P, T], F32, name="result%d" % b) for b in range(N // P)]
+        xs_rows = x_scales.bitcast(I32).rearrange("s (q r) n -> r q s n", r=4)
         wps_rows = wp_scales.bitcast(I32).rearrange("e s (q r) n -> r q (e s) n", r=4)
         gate_cols = keep.tile([P, PACK], F32, name="gate_cols")
         gate_all = keep.tile([P, E * C], F32, name="gate_all")
@@ -82,14 +79,16 @@ def tile_moe_duo_silu_kernel(
         y_sb = {}
 
         def load_x(s):
-            nc.sync.dma_start(out=xw[s][:, 0:T], in_=x_words[s].rearrange("p t d -> p (t d)").bitcast(I32))
+            nc.sync.dma_start(out=xw[s][:], in_=x_words[s].rearrange("p t d -> p (t d)").bitcast(I32))
 
         def load_token_scales(queue):
-            for q in range(4):
-                queue.dma_start(out=xs[32 * q : 32 * q + 8, 0:T].bitcast(I32), in_=x_scales[:, 4 * q : 4 * q + 4, :].bitcast(I32))
+            for r in range(4):
+                rows = xs[r:P:32, :].bitcast(I32).rearrange("q (s n) -> q s n", s=PASSES)
+                queue.dma_start(out=rows, in_=xs_rows[r])
 
-        def move_plane(queue):
-            queue.dma_start(out=moved[0:100, :].bitcast(I32), in_=gathered[("pb", 0)][4:104, :].bitcast(I32))
+        def load_packed_scales(queue):
+            for r in range(4):
+                queue.dma_start(out=xs[4 + r : P : 32, T : 2 * T].bitcast(I32), in_=xs_rows[r][:, 0, :])
 
         def load_partner_scales(queue):
             for r in range(4):
@@ -126,13 +125,13 @@ def tile_moe_duo_silu_kernel(
                 nc.tensor.transpose(spread[:, j, :], gate_cols[:, j : j + 1].to_broadcast([P, P]), ident[:])
             nc.scalar.copy(out=gate_all[:].rearrange("p (n j) -> p n j", j=PACK), in_=spread[:].rearrange("p j n -> p n j"))
 
-        def gather(kind, s, over=None):
+        def gather(kind, s, wave, over=None):
             dtype = U32 if kind[1] == "w" else U8
-            tile = placed("%s%d" % (kind, s), E * C, dtype, 4 if kind[1] == "w" else 1, over)
-            offsets = tok_list if kind[0] == "t" else par_list
-            window = xw[s][:].bitcast(U32) if kind[1] == "w" else xs[:]
-            nc.vector.tensor_copy(tile[:], window.indirect(offsets[:]))
-            gathered[(kind, s)] = tile
+            tile = placed("%s%d_%d" % (kind, s, wave), WAVE, dtype, 4 if kind[1] == "w" else 1, over)
+            offsets = (tok_list if kind[0] == "t" else par_list)[:, wave * WAVE // 16 : (wave + 1) * WAVE // 16]
+            window = xw[s][:].bitcast(U32) if kind[1] == "w" else xs[:, s * T : (s + 1) * T]
+            nc.vector.tensor_copy(tile[:], window.indirect(offsets))
+            gathered[(kind, s, wave)] = tile
 
         def cast(key, engine, c0, c1, over=None, into=None):
             r0, r1, source = [piece for piece in raw[key] if piece[0] <= c0 and c1 <= piece[1]][0]
@@ -155,7 +154,8 @@ def tile_moe_duo_silu_kernel(
             nc.vector.quantize_mx(out=codes[key][:, c0:c1].bitcast(FP8X4), scales=scales[key][:, c0:c1], in_=staged[(key, source or (c0, c1))][:, (c0 - (source or (c0, c1))[0]) * PACK : (c1 - (source or (c0, c1))[0]) * PACK])
 
         def first_passes(e, order, start=False, stop=False, bank=None):
-            slots = slice(e * C, (e + 1) * C)
+            slots = slice(e % 2 * C, (e % 2 + 1) * C)
+            wave = e // 2
             if start:
                 accs[e] = psum.tile([P, H], F32, name="acc%d" % e, offset=BANK * (e % 2 if bank is None else bank))
             names = order.split()
@@ -163,10 +163,10 @@ def tile_moe_duo_silu_kernel(
                 s = int(name[1])
                 if name[0] == "o":
                     key = "%d%d" % (e, s)
-                    operands = (gathered[("tw", s)][:, slots], gathered[("tb", 0)][4 * s : P, slots], codes[key][:].bitcast(FP8X4), scales[key][:])
+                    operands = (gathered[("tw", s, wave)][:, slots], gathered[("tb", 1, wave)][4 * (1 - s) : P, slots], codes[key][:].bitcast(FP8X4), scales[key][:])
                 else:
                     g = e * PASSES + s
-                    operands = (gathered[("pw", s)][:, slots], (moved if s else gathered[("pb", 0)])[:, slots], wpw[(e, s)].bitcast(FP4X4), wps[:, g * H : (g + 1) * H])
+                    operands = (gathered[("pw", s, wave)][:, slots], gathered[("pb", s, wave)][:, slots], wpw[(e, s)].bitcast(FP4X4), wps[:, g * H : (g + 1) * H])
                 nc.tensor.matmul_mx(out=accs[e][:], lhsT=operands[0].bitcast(FP8X4), lhsT_scale=operands[1], rhs=operands[2], rhs_scale=operands[3], start=(start and n == 0), stop=(stop and n == len(names) - 1))
 
         def silu(e, over=None, halves=False, room=0):
@@ -215,16 +215,17 @@ def tile_moe_duo_silu_kernel(
         def store(b):
             nc.sync.dma_start(out=out[b * P : (b + 1) * P, :], in_=result[b][:])
 
-        load_gate_row(nc.scalar)
         nc.scalar.activation(out=warm[:], in_=warm[:], func=SILU)
+        load_partner_scales(nc.gpsimd)
         nc.sync.dma_start(tok_list[:], offs)
         load_x(0)
         nc.sync.dma_start(par_list[:], offs2)
-        load_w1(0, 0)
         load_token_scales(nc.sync)
+        load_w1(0, 0)
         load_x(1)
+        load_gate_row(nc.sync)
+        load_packed_scales(nc.sync)
         load_w1(0, 1)
-        load_partner_scales(nc.sync)
         load_wp(0, 1)
         load_w1(1, 0)
         load_w1(1, 1)
@@ -240,19 +241,24 @@ def tile_moe_duo_silu_kernel(
         load_wp(3, 4)
         load_w2(2)
         load_w2(3)
-        spread_gate()
-        gather("tw", 0)
-        gather("pw", 0)
-        gather("pb", 0)
-        gather("tb", 0)
-        gather("tw", 1)
-        gather("pw", 1)
+        gather("tw", 0, 0)
+        gather("tw", 0, 1)
+        gather("pw", 0, 0)
+        gather("pw", 0, 1)
+        gather("pb", 0, 0)
+        gather("pb", 0, 1)
+        gather("tw", 1, 0)
+        gather("pw", 1, 0)
         cast("00", "S", 0, 512)
-        move_plane(nc.scalar)
-        quant("00", 0, 512, codes_over="xw1")
-        cast("01", "S", 0, 512)
+        spread_gate()
+        quant("00", 0, 512)
+        gather("pb", 1, 0)
+        gather("tb", 1, 0)
+        cast("01", "V", 0, 128, into=(0, 512))
+        cast("01", "S", 128, 512, into=(0, 512))
         quant("01", 0, 512)
-        first_passes(0, "p0 o0 o1 p1", start=True, stop=True)
+        first_passes(0, "o0 p0 p1 o1", start=True, stop=True)
+        gather("tw", 1, 1, over="raw01_0")
         cast("10", "S", 256, 512, into=(0, 512))
         cast("10", "V", 0, 256, into=(0, 512))
         silu(0, over="raw10_0")
@@ -265,10 +271,13 @@ def tile_moe_duo_silu_kernel(
         quant("11", 256, 512)
         first_passes(1, "p0 p1 o1", stop=True)
         quant("h0", 0, C)
+        gather("pb", 1, 1, over="hg0")
+        gather("tb", 1, 1, over=("hg0", 256))
         cast("v0", "S", 0, 256)
         silu(1)
         cast("v1", "S", 0, 256)
         quant("v0", 0, 256)
+        gather("pw", 1, 1, over="stv0_0")
         second_product(0, 4)
         cast("20", "V", 0, 256, into=(0, 512))
         quant("v1", 0, 256)

@@ -216,7 +216,6 @@ def tile_moe_duo_silu_kernel(
             nc.sync.dma_start(out=out[b * P : (b + 1) * P, :], in_=result[b][:])
 
         nc.scalar.activation(out=warm[:], in_=warm[:], func=SILU)
-        load_partner_scales(nc.gpsimd)
         nc.sync.dma_start(tok_list[:], offs)
         load_x(0)
         nc.sync.dma_start(par_list[:], offs2)
@@ -226,6 +225,7 @@ def tile_moe_duo_silu_kernel(
         load_gate_row(nc.sync)
         load_packed_scales(nc.sync)
         load_w1(0, 1)
+        load_partner_scales(nc.sync)
         load_wp(0, 1)
         load_w1(1, 0)
         load_w1(1, 1)

@@ -22,6 +22,7 @@ PACK = 4
 K_PASS = P * PACK
 PASSES = K // K_PASS
 WAVE = 2 * C
+WINDOW = 704
 BANK = 2048
 
 
@@ -48,7 +49,7 @@ def tile_moe_duo_silu_kernel(
             places[name] = (at, room)
             return stage.tile([P, columns], dtype, name=name, offset=at, align_bytes=64)
 
-        xs = placed("xs0", PASSES * T, U8, 1)
+        xs = placed("xs0", PASSES * WINDOW, U8, 1)
         wps = keep.tile([P, E * PASSES * H], U8, name="wps", align_bytes=64)
         nc.vector.memset(xs[:].bitcast(I32), 0)
         warm = keep.tile([P, 1], F32, name="warm")
@@ -59,7 +60,8 @@ def tile_moe_duo_silu_kernel(
 
         tok_list = keep.tile([P, T // 16], U16, name="tok_list")
         par_list = keep.tile([P, T // 16], U16, name="par_list")
-        xw = [placed("xw%d" % s, T, I32, 4) for s in range(PASSES)]
+        xw = [placed("xw%d" % s, WINDOW, I32, 4) for s in range(PASSES)]
+        nc.vector.memset(xw[0][:, T:WINDOW], 0)
         result = [keep.tile([P, T], F32, name="result%d" % b) for b in range(N // P)]
         xs_rows = x_scales.bitcast(I32).rearrange("s (q r) n -> r q s n", r=4)
         wps_rows = wp_scales.bitcast(I32).rearrange("e s (q r) n -> r q (e s) n", r=4)
@@ -77,18 +79,19 @@ def tile_moe_duo_silu_kernel(
         turns = {}
         ys = {}
         y_sb = {}
+        dealt = {}
 
         def load_x(s):
-            nc.sync.dma_start(out=xw[s][:], in_=x_words[s].rearrange("p t d -> p (t d)").bitcast(I32))
+            nc.sync.dma_start(out=xw[s][:, 0:T], in_=x_words[s].rearrange("p t d -> p (t d)").bitcast(I32))
 
         def load_token_scales(queue):
             for r in range(4):
                 rows = xs[r:P:32, :].bitcast(I32).rearrange("q (s n) -> q s n", s=PASSES)
-                queue.dma_start(out=rows, in_=xs_rows[r])
+                queue.dma_start(out=rows[:, :, 0 : T // 4], in_=xs_rows[r])
 
         def load_packed_scales(queue):
             for r in range(4):
-                queue.dma_start(out=xs[4 + r : P : 32, T : 2 * T].bitcast(I32), in_=xs_rows[r][:, 0, :])
+                queue.dma_start(out=xs[4 + r : P : 32, WINDOW : WINDOW + T].bitcast(I32), in_=xs_rows[r][:, 0, :])
 
         def load_partner_scales(queue):
             for r in range(4):
@@ -105,6 +108,12 @@ def tile_moe_duo_silu_kernel(
         def load_w2(e, c0=0, c1=N):
             load_rows("v%d" % e, w2[e], c0, c1)
 
+        def load_w2_pair(e):
+            tile = placed("rawv%d_0" % e, 2 * PACK * N, F32, 4)[:].rearrange("p (e j w) -> p e j w", e=2, j=PACK)
+            nc.sync.dma_start(out=tile, in_=w2[e : e + 2].rearrange("e (p j) w -> p e j w", j=PACK))
+            for n in range(2):
+                raw["v%d" % (e + n)] = [(0, N, tile[:, n])]
+
         def load_wp(e0, e1):
             tile = placed("wpw%d" % e0, (e1 - e0) * PASSES * 2 * H, U8, 1)
             nc.sync.dma_start(
@@ -112,6 +121,7 @@ def tile_moe_duo_silu_kernel(
                 in_=wp_words[e0:e1].bitcast(I32).rearrange("e s p n -> p (e s) n"),
             )
             for e in range(e0, e1):
+                wpw[e] = tile[:, (e - e0) * PASSES * 2 * H : (e - e0 + 1) * PASSES * 2 * H]
                 for s in range(PASSES):
                     g = (e - e0) * PASSES + s
                     wpw[(e, s)] = tile[:, g * 2 * H : (g + 1) * 2 * H]
@@ -125,13 +135,16 @@ def tile_moe_duo_silu_kernel(
                 nc.tensor.transpose(spread[:, j, :], gate_cols[:, j : j + 1].to_broadcast([P, P]), ident[:])
             nc.scalar.copy(out=gate_all[:].rearrange("p (n j) -> p n j", j=PACK), in_=spread[:].rearrange("p j n -> p n j"))
 
-        def gather(kind, s, wave, over=None):
+        def gather(kind, s, wave=None, over=None):
             dtype = U32 if kind[1] == "w" else U8
-            tile = placed("%s%d_%d" % (kind, s, wave), WAVE, dtype, 4 if kind[1] == "w" else 1, over)
-            offsets = (tok_list if kind[0] == "t" else par_list)[:, wave * WAVE // 16 : (wave + 1) * WAVE // 16]
-            window = xw[s][:].bitcast(U32) if kind[1] == "w" else xs[:, s * T : (s + 1) * T]
+            count, width = (E * C, WINDOW) if wave is None else (WAVE, T)
+            tile = placed("%s%d_%s" % (kind, s, wave), count, dtype, 4 if kind[1] == "w" else 1, over)
+            first = 0 if wave is None else wave * WAVE // 16
+            offsets = (tok_list if kind[0] == "t" else par_list)[:, first : first + count // 16]
+            window = xw[s][:, 0:width].bitcast(U32) if kind[1] == "w" else xs[:, s * WINDOW : s * WINDOW + width]
             nc.vector.tensor_copy(tile[:], window.indirect(offsets))
-            gathered[(kind, s, wave)] = tile
+            for n in range(count // WAVE):
+                gathered[(kind, s, n if wave is None else wave)] = tile[:, n * WAVE : (n + 1) * WAVE]
 
         def cast(key, engine, c0, c1, over=None, into=None):
             r0, r1, source = [piece for piece in raw[key] if piece[0] <= c0 and c1 <= piece[1]][0]
@@ -163,11 +176,64 @@ def tile_moe_duo_silu_kernel(
                 s = int(name[1])
                 if name[0] == "o":
                     key = "%d%d" % (e, s)
-                    operands = (gathered[("tw", s, wave)][:, slots], gathered[("tb", 1, wave)][4 * (1 - s) : P, slots], codes[key][:].bitcast(FP8X4), scales[key][:])
+                    operands = (gathered[("tw", s, wave)][:, slots], gathered[("tb", s, wave)][:, slots], codes[key][:].bitcast(FP8X4), scales[key][:])
                 else:
                     g = e * PASSES + s
                     operands = (gathered[("pw", s, wave)][:, slots], gathered[("pb", s, wave)][:, slots], wpw[(e, s)].bitcast(FP4X4), wps[:, g * H : (g + 1) * H])
                 nc.tensor.matmul_mx(out=accs[e][:], lhsT=operands[0].bitcast(FP8X4), lhsT_scale=operands[1], rhs=operands[2], rhs_scale=operands[3], start=(start and n == 0), stop=(stop and n == len(names) - 1))
+
+        def keep_clock(key, wave, passes):
+            spare = psum.tile([P, H], F32, name="spare" + key, offset=BANK * 7)
+            for n in range(passes):
+                nc.tensor.matmul_mx(out=spare[:], lhsT=gathered[("tw", 1, wave)][:, 0:C].bitcast(FP8X4), lhsT_scale=gathered[("tb", 1, wave)][:, 0:C], rhs=codes[key][:].bitcast(FP8X4), rhs_scale=scales[key][:], start=True, stop=True)
+
+        def deal_partner_words(e, over=None):
+            tile = placed("wpd%d" % e, PASSES * H, U16, 2, over)
+            nc.vector.tensor_copy(
+                out=tile[:].rearrange("p (s t m) -> p s t m", s=PASSES, t=PACK),
+                in_=wpw[e].bitcast(U16).rearrange("p (s m t) -> p s t m", s=PASSES, t=PACK),
+            )
+            dealt["words"] = tile
+
+        def deal_partner_scales(e, over=None):
+            tile = placed("wsd%d" % e, PASSES * H, U8, 1, over)
+            nc.vector.tensor_copy(
+                out=tile[:].rearrange("p (s t m) -> p s t m", s=PASSES, t=PACK),
+                in_=wps[:, e * PASSES * H : (e + 1) * PASSES * H].rearrange("p (s m t) -> p s t m", s=PASSES, t=PACK),
+            )
+            dealt["scales"] = tile
+
+        def cast_dealt(key, engine, c0, c1, over=None):
+            source = raw[key][0][2]
+            if key not in staged:
+                staged[key] = placed("st" + key, H * PACK, BF16, 2, over)
+                staged[(key, (0, H))] = staged[key]
+            copy = nc.vector.tensor_copy if engine == "V" else nc.scalar.copy
+            copy(
+                out=staged[key][:].rearrange("p (t m j) -> p m j t", t=PACK, j=PACK)[:, c0 // PACK : c1 // PACK, :, :],
+                in_=source[:, :, c0:c1].rearrange("p j (m t) -> p m j t", t=PACK),
+            )
+
+        def turned_passes(e, name, blocks, start=False, stop=False):
+            slots = slice(e % 2 * C, (e % 2 + 1) * C)
+            wave = e // 2
+            s = int(name[1])
+            if start:
+                accs[e] = psum.tile([P, PACK, C], F32, name="acc%d" % e, offset=BANK * (e % 2))
+            for t in blocks:
+                if name[0] == "o":
+                    key = "%d%d" % (e, s)
+                    cols = slice(t * P, (t + 1) * P)
+                    operands = (codes[key][:, cols].bitcast(FP8X4), scales[key][:, cols], gathered[("tw", s, wave)][:, slots], gathered[("tb", 1, wave)][4 * (1 - s) : P, slots])
+                else:
+                    cols = slice(s * H + t * P, s * H + (t + 1) * P)
+                    operands = (dealt["words"][:, cols].bitcast(FP4X4), dealt["scales"][:, cols], gathered[("pw", s, wave)][:, slots], gathered[("pb", s, wave)][:, slots])
+                nc.tensor.matmul_mx(out=accs[e][:, t, :], lhsT=operands[0], lhsT_scale=operands[1], rhs=operands[2].bitcast(FP8X4), rhs_scale=operands[3], start=(start and t == blocks[0]), stop=(stop and t == blocks[-1]))
+
+        def silu_grouped(e):
+            grouped = placed("hg%d" % e, C * PACK, BF16, 2)
+            nc.scalar.activation(out=grouped[:].rearrange("p (c t) -> p c t", t=PACK), in_=accs[e][:].rearrange("p t c -> p c t"), func=SILU)
+            staged[("h%d" % e, (0, C))] = grouped
 
         def silu(e, over=None, halves=False, room=0):
             rows = placed("hrows%d" % e, H, BF16, 2, over, room)
@@ -216,20 +282,18 @@ def tile_moe_duo_silu_kernel(
             nc.sync.dma_start(out=out[b * P : (b + 1) * P, :], in_=result[b][:])
 
         nc.scalar.activation(out=warm[:], in_=warm[:], func=SILU)
+        load_partner_scales(nc.gpsimd)
         nc.sync.dma_start(tok_list[:], offs)
         load_x(0)
         nc.sync.dma_start(par_list[:], offs2)
-        load_token_scales(nc.sync)
         load_w1(0, 0)
+        load_token_scales(nc.sync)
         load_x(1)
         load_gate_row(nc.sync)
-        load_packed_scales(nc.sync)
         load_w1(0, 1)
-        load_partner_scales(nc.sync)
-        load_wp(0, 1)
+        load_wp(0, 2)
         load_w1(1, 0)
         load_w1(1, 1)
-        load_wp(1, 2)
         load_w2(0)
         load_w2(1)
         load_w1(2, 0, 0, 256)
@@ -241,60 +305,57 @@ def tile_moe_duo_silu_kernel(
         load_wp(3, 4)
         load_w2(2)
         load_w2(3)
-        gather("tw", 0, 0)
-        gather("tw", 0, 1)
-        gather("pw", 0, 0)
-        gather("pw", 0, 1)
-        gather("pb", 0, 0)
-        gather("pb", 0, 1)
+        gather("tw", 0)
+        gather("pw", 0)
+        gather("pb", 0)
+        gather("tb", 0)
+        gather("pb", 1)
+        gather("tb", 1)
         gather("tw", 1, 0)
         gather("pw", 1, 0)
         cast("00", "S", 0, 512)
         spread_gate()
-        quant("00", 0, 512)
-        gather("pb", 1, 0)
-        gather("tb", 1, 0)
-        cast("01", "V", 0, 128, into=(0, 512))
-        cast("01", "S", 128, 512, into=(0, 512))
+        quant("00", 0, 512, scales_over="xs0")
+        cast("01", "S", 0, 512)
         quant("01", 0, 512)
-        first_passes(0, "o0 p0 p1 o1", start=True, stop=True)
-        gather("tw", 1, 1, over="raw01_0")
+        first_passes(0, "p0 p1 o0 o1", start=True, stop=True)
         cast("10", "S", 256, 512, into=(0, 512))
         cast("10", "V", 0, 256, into=(0, 512))
         silu(0, over="raw10_0")
         quant("10", 0, 512)
         first_passes(1, "o0", start=True)
-        cast("11", "V", 0, 256)
-        cast("11", "S", 256, 512)
-        quant("11", 0, 256)
-        regroup(0, over="st11_0")
-        quant("11", 256, 512)
+        cast("11", "V", 0, 256, into=(0, 512))
+        cast("11", "S", 256, 512, into=(0, 512))
+        quant("11", 0, 512)
+        regroup(0, over="raw11_0")
         first_passes(1, "p0 p1 o1", stop=True)
         quant("h0", 0, C)
-        gather("pb", 1, 1, over="hg0")
-        gather("tb", 1, 1, over=("hg0", 256))
-        cast("v0", "S", 0, 256)
-        silu(1)
-        cast("v1", "S", 0, 256)
-        quant("v0", 0, 256)
-        gather("pw", 1, 1, over="stv0_0")
+        gather("pw", 1, 1, over="hg0")
+        gather("tw", 1, 1, over=("raw11_0", 4096))
+        cast("v0", "S", 0, 256, over=("raw11_0", 2048))
+        silu(1, room=4096)
+        cast("v1", "S", 0, 256, over="codes11")
+        quant("v0", 0, 256, room=2048)
         second_product(0, 4)
-        cast("20", "V", 0, 256, into=(0, 512))
-        quant("v1", 0, 256)
+        cast("20", "V", 0, 256)
+        quant("v1", 0, 256, room=4096)
         regroup(1)
-        copy_y(0, over="hrows1")
+        copy_y(0, 0, over="hrows1")
+        copy_y(0, 1, over=("hrows1", 2048))
         quant("h1", 0, C)
         second_product(1, 5)
         scatter(0, 0)
         scatter(0, 1)
-        cast("20", "S", 256, 512, into=(0, 512))
-        copy_y(1, over="raw20_256")
-        quant("20", 0, 512)
+        cast("20", "S", 256, 512, over="codesv0")
+        copy_y(1, 0, over="raw20_256")
+        copy_y(1, 1, over=("raw20_256", 2048))
+        quant("20", 0, 256, codes_over="ysb0_0")
+        quant("20", 256, 512)
         scatter(1, 0)
         first_passes(2, "p0 p1 o0", start=True)
         scatter(1, 1)
-        cast("21", "S", 0, 512)
-        quant("21", 0, 512)
+        cast("21", "S", 0, 512, over="codesv1")
+        quant("21", 0, 512, codes_over="ysb1_0")
         first_passes(2, "o1", stop=True)
         cast("30", "S", 256, 512, into=(0, 512))
         cast("30", "V", 0, 256, into=(0, 512), over=None)
@@ -309,23 +370,22 @@ def tile_moe_duo_silu_kernel(
         quant("31", 256, 384)
         quant("31", 384, 512)
         first_passes(3, "p0 p1 o1", stop=True)
-        cast("v2", "S", 128, 256)
-        cast("v2", "V", 0, 128)
-        quant("h2", 0, C, codes_over=None)
-        quant("v2", 0, 128)
-        second_product(2, 4, (0,))
-        quant("v2", 128, 256)
-        silu(3)
-        second_product(2, 5, (1,))
-        copy_y(2, 0)
+        cast("v2", "S", 128, 256, into=(0, 256))
+        cast("v2", "V", 0, 128, into=(0, 256))
+        quant("h2", 0, C)
+        silu(3, halves=True)
+        quant("v2", 0, 256)
         cast("v3", "V", 0, 256)
-        scatter(2, 0)
-        quant("v3", 0, 256)
         regroup(3)
-        copy_y(2, 1, over="hrows3")
+        second_product(2, 4, (0,))
+        second_product(2, 5, (1,))
+        quant("v3", 0, 256)
         quant("h3", 0, C)
+        copy_y(2, 0, over="hrows3")
+        copy_y(2, 1, over=("hrows3", 512))
         second_product(3, 6, (0,))
         second_product(3, 7, (1,))
+        scatter(2, 0)
         scatter(2, 1)
         copy_y(3, 0)
         copy_y(3, 1)

@@ -51,10 +51,10 @@ def tile_moe_duo_silu_kernel(
 
         xs = placed("xs0", PASSES * WINDOW, U8, 1)
         wps = keep.tile([P, E * PASSES * H], U8, name="wps", align_bytes=64)
+        nc.vector.memset(wps[:].bitcast(I32), 0)
         nc.vector.memset(xs[:].bitcast(I32), 0)
         warm = keep.tile([P, 1], F32, name="warm")
         nc.vector.memset(warm[:], 0.0)
-        nc.vector.memset(wps[:].bitcast(I32), 0)
         ident = keep.tile([P, P], F32, name="ident")
         make_identity(nc, ident[:])
 
@@ -93,8 +93,8 @@ def tile_moe_duo_silu_kernel(
             for r in range(4):
                 queue.dma_start(out=xs[4 + r : P : 32, WINDOW : WINDOW + T].bitcast(I32), in_=xs_rows[r][:, 0, :])
 
-        def load_partner_scales(queue):
-            for r in range(4):
+        def load_partner_scales(queue, rows):
+            for r in rows:
                 queue.dma_start(out=wps[r:P:32, :].bitcast(I32).rearrange("q (g n) -> q g n", g=E * PASSES), in_=wps_rows[r])
 
         def load_rows(key, rows, c0, c1):
@@ -282,7 +282,7 @@ def tile_moe_duo_silu_kernel(
             nc.sync.dma_start(out=out[b * P : (b + 1) * P, :], in_=result[b][:])
 
         nc.scalar.activation(out=warm[:], in_=warm[:], func=SILU)
-        load_partner_scales(nc.gpsimd)
+        load_partner_scales(nc.gpsimd, (0, 1))
         nc.sync.dma_start(tok_list[:], offs)
         load_x(0)
         nc.sync.dma_start(par_list[:], offs2)
@@ -291,6 +291,7 @@ def tile_moe_duo_silu_kernel(
         load_x(1)
         load_gate_row(nc.sync)
         load_w1(0, 1)
+        load_partner_scales(nc.sync, (2, 3))
         load_wp(0, 2)
         load_w1(1, 0)
         load_w1(1, 1)

@@ -358,6 +358,7 @@ def tile_moe_duo_silu_kernel(
         cast("21", "S", 0, 512, over="codesv1")
         quant("21", 0, 512, codes_over="ysb1_0")
         first_passes(2, "o1", stop=True)
+        keep_clock("21", 1, 2)
         cast("30", "S", 256, 512, into=(0, 512))
         cast("30", "V", 0, 256, into=(0, 512), over=None)
         silu(2, over="raw30_0")
@@ -371,6 +372,7 @@ def tile_moe_duo_silu_kernel(
         quant("31", 256, 384)
         quant("31", 384, 512)
         first_passes(3, "p0 p1 o1", stop=True)
+        keep_clock("31", 1, 1)
         cast("v2", "S", 128, 256, into=(0, 256))
         cast("v2", "V", 0, 128, into=(0, 256))
         quant("h2", 0, C)

@@ -14,6 +14,7 @@ U16 = mybir.dt.uint16
 U8 = mybir.dt.uint8
 FP8X4 = mybir.dt.float8_e4m3fn_x4
 FP4X4 = mybir.dt.float4_e2m1fn_x4
+COPY = mybir.ActivationFunctionType.Copy
 SILU = mybir.ActivationFunctionType.Silu
 MULT = mybir.AluOpType.mult
 
@@ -21,9 +22,9 @@ P = 128
 PACK = 4
 K_PASS = P * PACK
 PASSES = K // K_PASS
-WAVE = 2 * C
 WINDOW = 704
 BANK = 2048
+TAILS = 1
 
 
 def tile_moe_duo_silu_kernel(
@@ -49,7 +50,7 @@ def tile_moe_duo_silu_kernel(
             places[name] = (at, room)
             return stage.tile([P, columns], dtype, name=name, offset=at, align_bytes=64)
 
-        xs = placed("xs0", PASSES * WINDOW, U8, 1)
+        xs = placed("xs", PASSES * WINDOW, U8, 1)
         wps = keep.tile([P, E * PASSES * H], U8, name="wps", align_bytes=64)
         nc.vector.memset(wps[:].bitcast(I32), 0)
         nc.vector.memset(xs[:].bitcast(I32), 0)
@@ -61,15 +62,17 @@ def tile_moe_duo_silu_kernel(
         tok_list = keep.tile([P, T // 16], U16, name="tok_list")
         par_list = keep.tile([P, T // 16], U16, name="par_list")
         xw = [placed("xw%d" % s, WINDOW, I32, 4) for s in range(PASSES)]
-        nc.vector.memset(xw[0][:, T:WINDOW], 0)
+        for s in range(TAILS):
+            nc.vector.memset(xw[s][:, T:WINDOW], 0)
         result = [keep.tile([P, T], F32, name="result%d" % b) for b in range(N // P)]
         xs_rows = x_scales.bitcast(I32).rearrange("s (q r) n -> r q s n", r=4)
         wps_rows = wp_scales.bitcast(I32).rearrange("e s (q r) n -> r q (e s) n", r=4)
         gate_cols = keep.tile([P, PACK], F32, name="gate_cols")
-        gate_all = keep.tile([P, E * C], F32, name="gate_all")
 
         raw = {}
+        flat = {}
         wpw = {}
+        gates = {}
         gathered = {}
         staged = {}
         codes = {}
@@ -79,7 +82,6 @@ def tile_moe_duo_silu_kernel(
         turns = {}
         ys = {}
         y_sb = {}
-        dealt = {}
 
         def load_x(s):
             nc.sync.dma_start(out=xw[s][:, 0:T], in_=x_words[s].rearrange("p t d -> p (t d)").bitcast(I32))
@@ -89,30 +91,21 @@ def tile_moe_duo_silu_kernel(
                 rows = xs[r:P:32, :].bitcast(I32).rearrange("q (s n) -> q s n", s=PASSES)
                 queue.dma_start(out=rows[:, :, 0 : T // 4], in_=xs_rows[r])
 
-        def load_packed_scales(queue):
-            for r in range(4):
-                queue.dma_start(out=xs[4 + r : P : 32, WINDOW : WINDOW + T].bitcast(I32), in_=xs_rows[r][:, 0, :])
-
         def load_partner_scales(queue, rows):
             for r in rows:
                 queue.dma_start(out=wps[r:P:32, :].bitcast(I32).rearrange("q (g n) -> q g n", g=E * PASSES), in_=wps_rows[r])
 
-        def load_rows(key, rows, c0, c1):
-            tile = placed("raw%s_%d" % (key, c0), PACK * (c1 - c0), F32, 4)[:].rearrange("p (j w) -> p j w", j=PACK)
+        def load_rows(key, rows, c0, c1, room, pad):
+            flat[key] = placed("raw%s_%d" % (key, c0), PACK * (c1 - c0) + pad, F32, 4, None, room)
+            tile = flat[key][:, 0 : PACK * (c1 - c0)].rearrange("p (j w) -> p j w", j=PACK)
             nc.sync.dma_start(out=tile, in_=rows[:, c0:c1].rearrange("(p j) w -> p j w", j=PACK))
             raw.setdefault(key, []).append((c0, c1, tile))
 
-        def load_w1(e, s, c0=0, c1=H):
-            load_rows("%d%d" % (e, s), w1[e, s * K_PASS : (s + 1) * K_PASS, :], c0, c1)
+        def load_w1(e, s, c0=0, c1=H, room=0, pad=0):
+            load_rows("%d%d" % (e, s), w1[e, s * K_PASS : (s + 1) * K_PASS, :], c0, c1, room, pad)
 
-        def load_w2(e, c0=0, c1=N):
-            load_rows("v%d" % e, w2[e], c0, c1)
-
-        def load_w2_pair(e):
-            tile = placed("rawv%d_0" % e, 2 * PACK * N, F32, 4)[:].rearrange("p (e j w) -> p e j w", e=2, j=PACK)
-            nc.sync.dma_start(out=tile, in_=w2[e : e + 2].rearrange("e (p j) w -> p e j w", j=PACK))
-            for n in range(2):
-                raw["v%d" % (e + n)] = [(0, N, tile[:, n])]
+        def load_w2(e, c0=0, c1=N, room=0, pad=0):
+            load_rows("v%d" % e, w2[e], c0, c1, room, pad)
 
         def load_wp(e0, e1):
             tile = placed("wpw%d" % e0, (e1 - e0) * PASSES * 2 * H, U8, 1)
@@ -121,7 +114,6 @@ def tile_moe_duo_silu_kernel(
                 in_=wp_words[e0:e1].bitcast(I32).rearrange("e s p n -> p (e s) n"),
             )
             for e in range(e0, e1):
-                wpw[e] = tile[:, (e - e0) * PASSES * 2 * H : (e - e0 + 1) * PASSES * 2 * H]
                 for s in range(PASSES):
                     g = (e - e0) * PASSES + s
                     wpw[(e, s)] = tile[:, g * 2 * H : (g + 1) * 2 * H]
@@ -129,29 +121,37 @@ def tile_moe_duo_silu_kernel(
         def load_gate_row(queue):
             queue.dma_start(out=gate_cols[:], in_=gate[0].rearrange("(p j) -> p j", j=PACK))
 
-        def spread_gate():
+        def spread_gate(rooms):
             spread = psum.tile([P, PACK, P], F32, name="spread", offset=BANK * 6)
             for j in range(PACK):
                 nc.tensor.transpose(spread[:, j, :], gate_cols[:, j : j + 1].to_broadcast([P, P]), ident[:])
-            nc.scalar.copy(out=gate_all[:].rearrange("p (n j) -> p n j", j=PACK), in_=spread[:].rearrange("p j n -> p n j"))
+            if rooms is None:
+                whole = placed("gate_all", E * C, F32, 4)
+                nc.scalar.copy(out=whole[:].rearrange("p (n j) -> p n j", j=PACK), in_=spread[:].rearrange("p j n -> p n j"))
+                for e in range(E):
+                    gates[e] = whole[:, e * C : (e + 1) * C]
+                return
+            for e in range(E):
+                gates[e] = placed("gate%d" % e, C, F32, 4, None, rooms[e])
+                quarter = slice(e * C // PACK, (e + 1) * C // PACK)
+                nc.scalar.copy(out=gates[e][:].rearrange("p (n j) -> p n j", j=PACK), in_=spread[:, :, quarter].rearrange("p j n -> p n j"))
 
-        def gather(kind, s, wave=None, over=None):
+        def gather(kind, s, first=0, count=E * C, over=None):
             dtype = U32 if kind[1] == "w" else U8
-            count, width = (E * C, WINDOW) if wave is None else (WAVE, T)
-            tile = placed("%s%d_%s" % (kind, s, wave), count, dtype, 4 if kind[1] == "w" else 1, over)
-            first = 0 if wave is None else wave * WAVE // 16
-            offsets = (tok_list if kind[0] == "t" else par_list)[:, first : first + count // 16]
+            width = WINDOW if count == E * C else T
+            tile = placed("%s%d_%d" % (kind, s, first), count, dtype, 4 if kind[1] == "w" else 1, over)
+            offsets = (tok_list if kind[0] == "t" else par_list)[:, first // 16 : (first + count) // 16]
             window = xw[s][:, 0:width].bitcast(U32) if kind[1] == "w" else xs[:, s * WINDOW : s * WINDOW + width]
             nc.vector.tensor_copy(tile[:], window.indirect(offsets))
-            for n in range(count // WAVE):
-                gathered[(kind, s, n if wave is None else wave)] = tile[:, n * WAVE : (n + 1) * WAVE]
+            for n in range(count // C):
+                gathered[(kind, s, first // C + n)] = tile[:, n * C : (n + 1) * C]
 
-        def cast(key, engine, c0, c1, over=None, into=None):
+        def cast(key, engine, c0, c1, over=None, into=None, room=0):
             r0, r1, source = [piece for piece in raw[key] if piece[0] <= c0 and c1 <= piece[1]][0]
             if into is None:
                 into = (c0, c1)
             if (key, into) not in staged:
-                staged[(key, into)] = placed("st%s_%d" % (key, into[0]), (into[1] - into[0]) * PACK, BF16, 2, over)
+                staged[(key, into)] = placed("st%s_%d" % (key, into[0]), (into[1] - into[0]) * PACK, BF16, 2, over, room)
             target = staged[(key, into)][:, (c0 - into[0]) * PACK : (c1 - into[0]) * PACK]
             copy, walk = (nc.vector.tensor_copy, 4) if engine == "V" else (nc.scalar.copy, 2)
             copy(
@@ -164,94 +164,56 @@ def tile_moe_duo_silu_kernel(
             if key not in codes:
                 codes[key] = placed("codes" + key, width, U32, 4, codes_over, room)
                 scales[key] = placed("scales" + key, width, U8, 1, scales_over)
-            nc.vector.quantize_mx(out=codes[key][:, c0:c1].bitcast(FP8X4), scales=scales[key][:, c0:c1], in_=staged[(key, source or (c0, c1))][:, (c0 - (source or (c0, c1))[0]) * PACK : (c1 - (source or (c0, c1))[0]) * PACK])
+            into = source or (c0, c1)
+            nc.vector.quantize_mx(out=codes[key][:, c0:c1].bitcast(FP8X4), scales=scales[key][:, c0:c1], in_=staged[(key, into)][:, (c0 - into[0]) * PACK : (c1 - into[0]) * PACK])
 
-        def first_passes(e, order, start=False, stop=False, bank=None):
-            slots = slice(e % 2 * C, (e % 2 + 1) * C)
-            wave = e // 2
+        def first_passes(e, order, start=False, stop=False, bank=None, c0=0, c1=H, part=False):
             if start:
-                accs[e] = psum.tile([P, H], F32, name="acc%d" % e, offset=BANK * (e % 2 if bank is None else bank))
+                accs[(e, c0)] = psum.tile([P, c1 - c0], F32, name="acc%d_%d" % (e, c0), offset=BANK * (e % 2 if bank is None else bank))
             names = order.split()
             for n, name in enumerate(names):
                 s = int(name[1])
                 if name[0] == "o":
                     key = "%d%d" % (e, s)
-                    operands = (gathered[("tw", s, wave)][:, slots], gathered[("tb", s, wave)][:, slots], codes[key][:].bitcast(FP8X4), scales[key][:])
+                    operands = (gathered[("tw", s, e)], gathered[("tb", s, e)], codes[key][:, c0:c1].bitcast(FP8X4), scales[key][:, c0:c1])
                 else:
                     g = e * PASSES + s
-                    operands = (gathered[("pw", s, wave)][:, slots], gathered[("pb", s, wave)][:, slots], wpw[(e, s)].bitcast(FP4X4), wps[:, g * H : (g + 1) * H])
-                nc.tensor.matmul_mx(out=accs[e][:], lhsT=operands[0].bitcast(FP8X4), lhsT_scale=operands[1], rhs=operands[2], rhs_scale=operands[3], start=(start and n == 0), stop=(stop and n == len(names) - 1))
+                    operands = (gathered[("pw", s, e)], gathered[("pb", s, e)], wpw[(e, s)][:, 2 * c0 : 2 * c1].bitcast(FP4X4), wps[:, g * H + c0 : g * H + c1])
+                nc.tensor.matmul_mx(out=accs[(e, 0)][:, c0:c1] if part else accs[(e, c0)][:], lhsT=operands[0].bitcast(FP8X4), lhsT_scale=operands[1], rhs=operands[2], rhs_scale=operands[3], start=(start and n == 0), stop=(stop and n == len(names) - 1))
 
-        def keep_clock(key, wave, passes):
-            spare = psum.tile([P, H], F32, name="spare" + key, offset=BANK * 7)
+        def keep_clock(key, e, passes, width=H):
+            spare = psum.tile([P, width], F32, name="spare" + key, offset=BANK * 7)
             for n in range(passes):
-                nc.tensor.matmul_mx(out=spare[:], lhsT=gathered[("tw", 1, wave)][:, 0:C].bitcast(FP8X4), lhsT_scale=gathered[("tb", 1, wave)][:, 0:C], rhs=codes[key][:].bitcast(FP8X4), rhs_scale=scales[key][:], start=True, stop=True)
+                nc.tensor.matmul_mx(out=spare[:], lhsT=gathered[("tw", 1, e)].bitcast(FP8X4), lhsT_scale=gathered[("tb", 1, e)], rhs=codes[key][:, 0:width].bitcast(FP8X4), rhs_scale=scales[key][:, 0:width], start=True, stop=True)
 
-        def deal_partner_words(e, over=None):
-            tile = placed("wpd%d" % e, PASSES * H, U16, 2, over)
-            nc.vector.tensor_copy(
-                out=tile[:].rearrange("p (s t m) -> p s t m", s=PASSES, t=PACK),
-                in_=wpw[e].bitcast(U16).rearrange("p (s m t) -> p s t m", s=PASSES, t=PACK),
-            )
-            dealt["words"] = tile
+        def silu(e, over=None, room=0, c0=0, c1=H, inside=None):
+            if inside is not None:
+                hrows[e] = flat[inside[0]][:, inside[1] : inside[1] + H // 2].bitcast(BF16)
+            elif e not in hrows:
+                hrows[e] = placed("hrows%d" % e, H, BF16, 2, over, room)[:]
+            target = hrows[e].rearrange("c (u p d) -> c u p d", u=2, d=2)[:, :, c0 // PACK : c1 // PACK, :]
+            nc.scalar.activation(out=target, in_=accs[(e, c0)][:].rearrange("c (p u d) -> c u p d", u=2, d=2), func=SILU)
 
-        def deal_partner_scales(e, over=None):
-            tile = placed("wsd%d" % e, PASSES * H, U8, 1, over)
-            nc.vector.tensor_copy(
-                out=tile[:].rearrange("p (s t m) -> p s t m", s=PASSES, t=PACK),
-                in_=wps[:, e * PASSES * H : (e + 1) * PASSES * H].rearrange("p (s m t) -> p s t m", s=PASSES, t=PACK),
-            )
-            dealt["scales"] = tile
+        def silu_half(e, u, over=None, room=0):
+            if e not in hrows:
+                hrows[e] = placed("hrows%d" % e, H, BF16, 2, over, room)[:]
+            target = hrows[e].rearrange("c (u p d) -> c u p d", u=2, d=2)[:, u, :, :]
+            nc.scalar.activation(out=target, in_=accs[(e, 0)][:].rearrange("c (p u d) -> c u p d", u=2, d=2)[:, u, :, :], func=SILU)
 
-        def cast_dealt(key, engine, c0, c1, over=None):
-            source = raw[key][0][2]
-            if key not in staged:
-                staged[key] = placed("st" + key, H * PACK, BF16, 2, over)
-                staged[(key, (0, H))] = staged[key]
+        def turn(e, halves=(0, 1)):
+            if e not in turns:
+                turns[e] = psum.tile([P, 2, C], F32, name="turned%d" % e, offset=BANK * (2 + e % 2))
+            pairs = hrows[e].bitcast(F32)
+            for u in halves:
+                nc.tensor.transpose(turns[e][:, u, :], pairs[:, u * P : (u + 1) * P], ident[:])
+
+        def regroup(e, over=None, room=0, engine="S", inside=None):
+            if inside is not None:
+                grouped = flat[inside[0]][:, inside[1] : inside[1] + C * PACK // 2].bitcast(BF16)
+            else:
+                grouped = placed("hg%d" % e, C * PACK, BF16, 2, over, room)[:]
             copy = nc.vector.tensor_copy if engine == "V" else nc.scalar.copy
-            copy(
-                out=staged[key][:].rearrange("p (t m j) -> p m j t", t=PACK, j=PACK)[:, c0 // PACK : c1 // PACK, :, :],
-                in_=source[:, :, c0:c1].rearrange("p j (m t) -> p m j t", t=PACK),
-            )
-
-        def turned_passes(e, name, blocks, start=False, stop=False):
-            slots = slice(e % 2 * C, (e % 2 + 1) * C)
-            wave = e // 2
-            s = int(name[1])
-            if start:
-                accs[e] = psum.tile([P, PACK, C], F32, name="acc%d" % e, offset=BANK * (e % 2))
-            for t in blocks:
-                if name[0] == "o":
-                    key = "%d%d" % (e, s)
-                    cols = slice(t * P, (t + 1) * P)
-                    operands = (codes[key][:, cols].bitcast(FP8X4), scales[key][:, cols], gathered[("tw", s, wave)][:, slots], gathered[("tb", 1, wave)][4 * (1 - s) : P, slots])
-                else:
-                    cols = slice(s * H + t * P, s * H + (t + 1) * P)
-                    operands = (dealt["words"][:, cols].bitcast(FP4X4), dealt["scales"][:, cols], gathered[("pw", s, wave)][:, slots], gathered[("pb", s, wave)][:, slots])
-                nc.tensor.matmul_mx(out=accs[e][:, t, :], lhsT=operands[0], lhsT_scale=operands[1], rhs=operands[2].bitcast(FP8X4), rhs_scale=operands[3], start=(start and t == blocks[0]), stop=(stop and t == blocks[-1]))
-
-        def silu_grouped(e):
-            grouped = placed("hg%d" % e, C * PACK, BF16, 2)
-            nc.scalar.activation(out=grouped[:].rearrange("p (c t) -> p c t", t=PACK), in_=accs[e][:].rearrange("p t c -> p c t"), func=SILU)
-            staged[("h%d" % e, (0, C))] = grouped
-
-        def silu(e, over=None, halves=False, room=0):
-            rows = placed("hrows%d" % e, H, BF16, 2, over, room)
-            turned = psum.tile([P, 2, C], F32, name="turned%d" % e, offset=BANK * (2 + e % 2))
-            pairs = rows[:].bitcast(F32)
-            target = rows[:].rearrange("c (u p d) -> c u p d", u=2, d=2)
-            source = accs[e][:].rearrange("c (p u d) -> c u p d", u=2, d=2)
-            if not halves:
-                nc.scalar.activation(out=target, in_=source, func=SILU)
-            for u in range(2):
-                if halves:
-                    nc.scalar.activation(out=target[:, u, :, :], in_=source[:, u, :, :], func=SILU)
-                nc.tensor.transpose(turned[:, u, :], pairs[:, u * P : (u + 1) * P], ident[:])
-            turns[e] = turned
-
-        def regroup(e, over=None, room=0):
-            grouped = placed("hg%d" % e, C * PACK, BF16, 2, over, room)
-            nc.scalar.copy(out=grouped[:].bitcast(F32).rearrange("p (c u) -> p c u", u=2), in_=turns[e][:].rearrange("p u c -> p c u"))
+            copy(out=grouped.bitcast(F32).rearrange("p (c u) -> p c u", u=2), in_=turns[e][:].rearrange("p u c -> p c u"))
             staged[("h%d" % e, (0, C))] = grouped
 
         def second_product(e, bank, blocks=(0, 1)):
@@ -263,23 +225,45 @@ def tile_moe_duo_silu_kernel(
                 ys[(e, b)] = y[:, n, :]
             ys[e] = y
 
-        def copy_y(e, b=None, over=None, room=0):
+        def pair_y(e, over=None):
+            both = placed("ysb%d" % e, N // P * C, F32, 4, over)
+            y_sb[(e, 0)] = both[:, 0:C]
+            y_sb[(e, 1)] = both[:, C : 2 * C]
+
+        def copy_y(e, b, over=None, room=0, inside=None):
+            if inside is not None:
+                y_sb[(e, b)] = flat[inside[0]][:, inside[1] : inside[1] + C]
+            elif (e, b) not in y_sb:
+                y_sb[(e, b)] = placed("ysb%d_%d" % (e, b), C, F32, 4, over, room)[:]
+            nc.scalar.copy(out=y_sb[(e, b)], in_=ys[(e, b)])
+
+        def gate_y(e, b=None, over=None, room=0, inside=None):
             if b is None:
-                both = placed("ysb%d" % e, N // P * C, F32, 4, over)
-                nc.scalar.copy(out=both[:].rearrange("p (b c) -> p b c", b=N // P), in_=ys[e][:])
+                if inside is not None:
+                    both = flat[inside[0]][:, inside[1] : inside[1] + N // P * C]
+                else:
+                    both = placed("ysb%d" % e, N // P * C, F32, 4, over, room)[:]
+                nc.vector.tensor_tensor(both.rearrange("p (b c) -> p b c", b=N // P), ys[e][:], gates[e][:].unsqueeze(1).to_broadcast([P, N // P, C]), MULT)
                 y_sb[(e, 0)] = both[:, 0:C]
                 y_sb[(e, 1)] = both[:, C : 2 * C]
             else:
-                one = placed("ysb%d_%d" % (e, b), C, F32, 4, over, room)
-                nc.scalar.copy(out=one[:], in_=ys[(e, b)])
-                y_sb[(e, b)] = one[:]
+                if inside is not None:
+                    y_sb[(e, b)] = flat[inside[0]][:, inside[1] : inside[1] + C]
+                elif (e, b) not in y_sb:
+                    y_sb[(e, b)] = placed("ysb%d_%d" % (e, b), C, F32, 4, over, room)[:]
+                nc.vector.tensor_tensor(y_sb[(e, b)], ys[(e, b)], gates[e][:], MULT)
 
-        def scatter(e, b):
-            cols = slice(e * C // 16, (e + 1) * C // 16)
-            nc.vector.tensor_tensor(result[b][:].indirect(tok_list[:, cols]), y_sb[(e, b)], gate_all[:, e * C : (e + 1) * C], MULT)
+        def scatter(e, b, engine):
+            window = result[b][:].indirect(tok_list[:, e * C // 16 : (e + 1) * C // 16])
+            if engine == "S":
+                nc.scalar.activation(window, y_sb[(e, b)], COPY)
+            elif engine == "V":
+                nc.vector.tensor_copy(window, y_sb[(e, b)])
+            else:
+                nc.vector.tensor_tensor(window, y_sb[(e, b)], gates[e][:], MULT)
 
-        def store(b):
-            nc.sync.dma_start(out=out[b * P : (b + 1) * P, :], in_=result[b][:])
+        def store(b, queue=nc.sync):
+            queue.dma_start(out=out[b * P : (b + 1) * P, :], in_=result[b][:])
 
         nc.scalar.activation(out=warm[:], in_=warm[:], func=SILU)
         load_partner_scales(nc.gpsimd, (0, 1))
@@ -312,17 +296,18 @@ def tile_moe_duo_silu_kernel(
         gather("tb", 0)
         gather("pb", 1)
         gather("tb", 1)
-        gather("tw", 1, 0)
-        gather("pw", 1, 0)
+        gather("tw", 1, 0, 256)
+        gather("pw", 1, 0, 256)
         cast("00", "S", 0, 512)
-        spread_gate()
-        quant("00", 0, 512, scales_over="xs0")
+        spread_gate(None)
+        quant("00", 0, 512, scales_over="xs")
         cast("01", "S", 0, 512)
         quant("01", 0, 512)
         first_passes(0, "p0 p1 o0 o1", start=True, stop=True)
         cast("10", "S", 256, 512, into=(0, 512))
         cast("10", "V", 0, 256, into=(0, 512))
         silu(0, over="raw10_0")
+        turn(0)
         quant("10", 0, 512)
         first_passes(1, "o0", start=True)
         cast("11", "V", 0, 256, into=(0, 512))
@@ -331,10 +316,11 @@ def tile_moe_duo_silu_kernel(
         regroup(0, over="raw11_0")
         first_passes(1, "p0 p1 o1", stop=True)
         quant("h0", 0, C)
-        gather("pw", 1, 1, over="hg0")
-        gather("tw", 1, 1, over=("raw11_0", 4096))
+        gather("pw", 1, 256, 256, over="hg0")
+        gather("tw", 1, 256, 256, over=("raw11_0", 4096))
         cast("v0", "S", 0, 256, over=("raw11_0", 2048))
         silu(1, room=4096)
+        turn(1)
         cast("v1", "S", 0, 256, over="codes11")
         quant("v0", 0, 256, room=2048)
         second_product(0, 4)
@@ -345,23 +331,24 @@ def tile_moe_duo_silu_kernel(
         copy_y(0, 1, over=("hrows1", 2048))
         quant("h1", 0, C)
         second_product(1, 5)
-        scatter(0, 0)
-        scatter(0, 1)
+        scatter(0, 0, "VG")
+        scatter(0, 1, "VG")
         cast("20", "S", 256, 512, over="codesv0")
         copy_y(1, 0, over="raw20_256")
         copy_y(1, 1, over=("raw20_256", 2048))
         quant("20", 0, 256, codes_over="ysb0_0")
         quant("20", 256, 512)
-        scatter(1, 0)
+        scatter(1, 0, "VG")
         first_passes(2, "p0 p1 o0", start=True)
-        scatter(1, 1)
+        scatter(1, 1, "VG")
         cast("21", "S", 0, 512, over="codesv1")
         quant("21", 0, 512, codes_over="ysb1_0")
         first_passes(2, "o1", stop=True)
-        keep_clock("21", 1, 2)
+        keep_clock("21", 2, 1)
         cast("30", "S", 256, 512, into=(0, 512))
-        cast("30", "V", 0, 256, into=(0, 512), over=None)
+        cast("30", "V", 0, 256, into=(0, 512))
         silu(2, over="raw30_0")
+        turn(2)
         quant("30", 0, 512)
         first_passes(3, "o0", start=True)
         cast("31", "V", 0, 256)
@@ -372,27 +359,29 @@ def tile_moe_duo_silu_kernel(
         quant("31", 256, 384)
         quant("31", 384, 512)
         first_passes(3, "p0 p1 o1", stop=True)
-        keep_clock("31", 1, 1)
         cast("v2", "S", 128, 256, into=(0, 256))
         cast("v2", "V", 0, 128, into=(0, 256))
         quant("h2", 0, C)
-        silu(3, halves=True)
+        silu_half(3, 0)
+        turn(3, (0,))
+        silu_half(3, 1)
+        turn(3, (1,))
         quant("v2", 0, 256)
         cast("v3", "V", 0, 256)
         regroup(3)
         second_product(2, 4, (0,))
         second_product(2, 5, (1,))
         quant("v3", 0, 256)
+        gate_y(2, 1, over="rawv3_0")
         quant("h3", 0, C)
         copy_y(2, 0, over="hrows3")
-        copy_y(2, 1, over=("hrows3", 512))
         second_product(3, 6, (0,))
         second_product(3, 7, (1,))
-        scatter(2, 0)
-        scatter(2, 1)
+        scatter(2, 0, "VG")
+        scatter(2, 1, "S")
         copy_y(3, 0)
-        copy_y(3, 1)
-        scatter(3, 0)
+        gate_y(3, 1)
+        scatter(3, 0, "VG")
         store(0)
-        scatter(3, 1)
+        scatter(3, 1, "S")
         store(1)

@@ -46,7 +46,7 @@ def tile_moe_duo_silu_kernel(
             else:
                 tenant, skip = over if isinstance(over, tuple) else (over, 0)
                 at, room = places[tenant][0] + skip, places[tenant][1] - skip
-                assert columns * size <= room
+                assert skip < 0 or columns * size <= room
             places[name] = (at, room)
             return stage.tile([P, columns], dtype, name=name, offset=at, align_bytes=64)
 
@@ -95,17 +95,21 @@ def tile_moe_duo_silu_kernel(
             for r in rows:
                 queue.dma_start(out=wps[r:P:32, :].bitcast(I32).rearrange("q (g n) -> q g n", g=E * PASSES), in_=wps_rows[r])
 
-        def load_rows(key, rows, c0, c1, room, pad):
-            flat[key] = placed("raw%s_%d" % (key, c0), PACK * (c1 - c0) + pad, F32, 4, None, room)
-            tile = flat[key][:, 0 : PACK * (c1 - c0)].rearrange("p (j w) -> p j w", j=PACK)
+        def gap(count):
+            places["top"] = (places["top"][0] + count, 0)
+
+        def load_rows(key, rows, c0, c1, room, pad, over, lead):
+            flat[key] = placed("raw%s_%d" % (key, c0), lead + PACK * (c1 - c0) + pad, F32, 4, over, room)
+            flat["%s_%d" % (key, c0)] = flat[key]
+            tile = flat[key][:, lead : lead + PACK * (c1 - c0)].rearrange("p (j w) -> p j w", j=PACK)
             nc.sync.dma_start(out=tile, in_=rows[:, c0:c1].rearrange("(p j) w -> p j w", j=PACK))
             raw.setdefault(key, []).append((c0, c1, tile))
 
-        def load_w1(e, s, c0=0, c1=H, room=0, pad=0):
-            load_rows("%d%d" % (e, s), w1[e, s * K_PASS : (s + 1) * K_PASS, :], c0, c1, room, pad)
+        def load_w1(e, s, c0=0, c1=H, room=0, pad=0, over=None, lead=0):
+            load_rows("%d%d" % (e, s), w1[e, s * K_PASS : (s + 1) * K_PASS, :], c0, c1, room, pad, over, lead)
 
-        def load_w2(e, c0=0, c1=N, room=0, pad=0):
-            load_rows("v%d" % e, w2[e], c0, c1, room, pad)
+        def load_w2(e, c0=0, c1=N, room=0, pad=0, over=None, lead=0):
+            load_rows("v%d" % e, w2[e], c0, c1, room, pad, over, lead)
 
         def load_wp(e0, e1):
             tile = placed("wpw%d" % e0, (e1 - e0) * PASSES * 2 * H, U8, 1)
@@ -181,10 +185,10 @@ def tile_moe_duo_silu_kernel(
                     operands = (gathered[("pw", s, e)], gathered[("pb", s, e)], wpw[(e, s)][:, 2 * c0 : 2 * c1].bitcast(FP4X4), wps[:, g * H + c0 : g * H + c1])
                 nc.tensor.matmul_mx(out=accs[(e, 0)][:, c0:c1] if part else accs[(e, c0)][:], lhsT=operands[0].bitcast(FP8X4), lhsT_scale=operands[1], rhs=operands[2], rhs_scale=operands[3], start=(start and n == 0), stop=(stop and n == len(names) - 1))
 
-        def keep_clock(key, e, passes, width=H):
-            spare = psum.tile([P, width], F32, name="spare" + key, offset=BANK * 7)
+        def keep_clock(key, e, passes, width=H, bank=7):
+            spare = psum.tile([P, width], F32, name="spare" + key, offset=BANK * bank)
             for n in range(passes):
-                nc.tensor.matmul_mx(out=spare[:], lhsT=gathered[("tw", 1, e)].bitcast(FP8X4), lhsT_scale=gathered[("tb", 1, e)], rhs=codes[key][:, 0:width].bitcast(FP8X4), rhs_scale=scales[key][:, 0:width], start=True, stop=True)
+                nc.tensor.matmul_mx(out=spare[:], lhsT=gathered[("tw", 1, e)].bitcast(FP8X4), lhsT_scale=gathered[("tb", 1, e)], rhs=codes[key[0:2]][:, 0:width].bitcast(FP8X4), rhs_scale=scales[key[0:2]][:, 0:width], start=True, stop=True)
 
         def silu(e, over=None, room=0, c0=0, c1=H, inside=None):
             if inside is not None:
@@ -194,8 +198,10 @@ def tile_moe_duo_silu_kernel(
             target = hrows[e].rearrange("c (u p d) -> c u p d", u=2, d=2)[:, :, c0 // PACK : c1 // PACK, :]
             nc.scalar.activation(out=target, in_=accs[(e, c0)][:].rearrange("c (p u d) -> c u p d", u=2, d=2), func=SILU)
 
-        def silu_half(e, u, over=None, room=0):
-            if e not in hrows:
+        def silu_half(e, u, over=None, room=0, inside=None):
+            if inside is not None:
+                hrows[e] = flat[inside[0]][:, inside[1] : inside[1] + H // 2].bitcast(BF16)
+            elif e not in hrows:
                 hrows[e] = placed("hrows%d" % e, H, BF16, 2, over, room)[:]
             target = hrows[e].rearrange("c (u p d) -> c u p d", u=2, d=2)[:, u, :, :]
             nc.scalar.activation(out=target, in_=accs[(e, 0)][:].rearrange("c (p u d) -> c u p d", u=2, d=2)[:, u, :, :], func=SILU)
@@ -276,19 +282,19 @@ def tile_moe_duo_silu_kernel(
         load_gate_row(nc.sync)
         load_w1(0, 1)
         load_partner_scales(nc.sync, (2, 3))
-        load_wp(0, 2)
-        load_w1(1, 0)
+        load_wp(0, 1)
+        load_w1(1, 0, lead=128)
         load_w1(1, 1)
-        load_w2(0)
+        load_wp(1, 2)
+        load_w2(0, lead=128)
+        load_w1(2, 0, lead=240)
         load_w2(1)
-        load_w1(2, 0, 0, 256)
-        load_w1(2, 0, 256, 512)
-        load_w1(2, 1)
+        load_w1(2, 1, pad=128)
         load_wp(2, 3)
         load_w1(3, 0)
         load_w1(3, 1)
         load_wp(3, 4)
-        load_w2(2)
+        load_w2(2, lead=128)
         load_w2(3)
         gather("tw", 0)
         gather("pw", 0)
@@ -304,65 +310,64 @@ def tile_moe_duo_silu_kernel(
         cast("01", "S", 0, 512)
         quant("01", 0, 512)
         first_passes(0, "p0 p1 o0 o1", start=True, stop=True)
-        cast("10", "S", 256, 512, into=(0, 512))
-        cast("10", "V", 0, 256, into=(0, 512))
-        silu(0, over="raw10_0")
+        cast("10", "S", 128, 512, into=(0, 512))
+        cast("10", "V", 0, 128, into=(0, 512))
+        silu(0, inside=("10", 0))
         turn(0)
+        gather("tw", 1, 256, 256, over="st01_0")
         quant("10", 0, 512)
         first_passes(1, "o0", start=True)
+        gather("pw", 1, 256, 256, over="st10_0")
         cast("11", "V", 0, 256, into=(0, 512))
         cast("11", "S", 256, 512, into=(0, 512))
         quant("11", 0, 512)
-        regroup(0, over="raw11_0")
+        regroup(0, inside=("11", 0))
         first_passes(1, "p0 p1 o1", stop=True)
         quant("h0", 0, C)
-        gather("pw", 1, 256, 256, over="hg0")
-        gather("tw", 1, 256, 256, over=("raw11_0", 4096))
-        cast("v0", "S", 0, 256, over=("raw11_0", 2048))
-        silu(1, room=4096)
-        turn(1)
-        cast("v1", "S", 0, 256, over="codes11")
-        quant("v0", 0, 256, room=2048)
+        cast("v0", "S", 128, 256, into=(0, 256))
+        cast("v0", "V", 0, 128, into=(0, 256))
+        silu(1, inside=("v0", 0))
+        quant("v0", 0, 256)
         second_product(0, 4)
-        cast("20", "V", 0, 256)
-        quant("v1", 0, 256, room=4096)
-        regroup(1)
-        copy_y(0, 0, over="hrows1")
-        copy_y(0, 1, over=("hrows1", 2048))
+        turn(1)
+        cast("20", "S", 320, 512, into=(0, 512))
+        cast("20", "V", 0, 320, into=(0, 512))
+        gate_y(0, inside=("20", 0))
+        regroup(1, inside=("20", 256))
+        quant("20", 0, 512)
+        first_passes(2, "o0", start=True)
+        scatter(0, 0, "S")
+        scatter(0, 1, "S")
+        cast("v1", "V", 0, 256)
         quant("h1", 0, C)
+        quant("v1", 0, 256)
         second_product(1, 5)
-        scatter(0, 0, "VG")
-        scatter(0, 1, "VG")
-        cast("20", "S", 256, 512, over="codesv0")
-        copy_y(1, 0, over="raw20_256")
-        copy_y(1, 1, over=("raw20_256", 2048))
-        quant("20", 0, 256, codes_over="ysb0_0")
-        quant("20", 256, 512)
-        scatter(1, 0, "VG")
-        first_passes(2, "p0 p1 o0", start=True)
-        scatter(1, 1, "VG")
-        cast("21", "S", 0, 512, over="codesv1")
-        quant("21", 0, 512, codes_over="ysb1_0")
-        first_passes(2, "o1", stop=True)
+        cast("21", "S", 384, 512, into=(0, 512))
+        cast("21", "V", 0, 384, into=(0, 512))
+        gate_y(1, inside=("21", 2048 - 128))
+        quant("21", 0, 512)
+        first_passes(2, "p0 o1 p1", stop=True)
         keep_clock("21", 2, 1)
-        cast("30", "S", 256, 512, into=(0, 512))
-        cast("30", "V", 0, 256, into=(0, 512))
-        silu(2, over="raw30_0")
+        scatter(1, 0, "S")
+        scatter(1, 1, "V")
+        cast("30", "S", 320, 512, into=(0, 512))
+        cast("30", "V", 0, 320, into=(0, 512))
+        silu(2, inside=("30", 0))
         turn(2)
         quant("30", 0, 512)
         first_passes(3, "o0", start=True)
         cast("31", "V", 0, 256)
-        cast("31", "S", 384, 512)
-        cast("31", "V", 256, 384)
-        regroup(2, over="raw31_0")
+        cast("31", "S", 256, 512)
+        regroup(2, inside=("31", 0))
+        first_passes(3, "p0 p1")
         quant("31", 0, 256)
-        quant("31", 256, 384)
-        quant("31", 384, 512)
-        first_passes(3, "p0 p1 o1", stop=True)
+        first_passes(3, "o1", c0=0, c1=256, part=True)
+        quant("31", 256, 512)
+        first_passes(3, "o1", c0=256, c1=512, part=True, stop=True)
+        quant("h2", 0, C)
         cast("v2", "S", 128, 256, into=(0, 256))
         cast("v2", "V", 0, 128, into=(0, 256))
-        quant("h2", 0, C)
-        silu_half(3, 0)
+        silu_half(3, 0, inside=("v2", 0))
         turn(3, (0,))
         silu_half(3, 1)
         turn(3, (1,))
@@ -374,7 +379,7 @@ def tile_moe_duo_silu_kernel(
         quant("v3", 0, 256)
         gate_y(2, 1, over="rawv3_0")
         quant("h3", 0, C)
-        copy_y(2, 0, over="hrows3")
+        copy_y(2, 0, over=("rawv2_0", 0))
         second_product(3, 6, (0,))
         second_product(3, 7, (1,))
         scatter(2, 0, "VG")

@@ -125,8 +125,8 @@ def tile_moe_duo_silu_kernel(
         def load_gate_row(queue):
             queue.dma_start(out=gate_cols[:], in_=gate[0].rearrange("(p j) -> p j", j=PACK))
 
-        def spread_gate(rooms):
-            spread = psum.tile([P, PACK, P], F32, name="spread", offset=BANK * 6)
+        def spread_gate(rooms, bank=6):
+            spread = psum.tile([P, PACK, P], F32, name="spread", offset=BANK * bank)
             for j in range(PACK):
                 nc.tensor.transpose(spread[:, j, :], gate_cols[:, j : j + 1].to_broadcast([P, P]), ident[:])
             if rooms is None:
@@ -294,7 +294,7 @@ def tile_moe_duo_silu_kernel(
         load_w1(3, 0)
         load_w1(3, 1)
         load_wp(3, 4)
-        load_w2(2, lead=128)
+        load_w2(2)
         load_w2(3)
         gather("tw", 0)
         gather("pw", 0)
@@ -357,7 +357,8 @@ def tile_moe_duo_silu_kernel(
         quant("30", 0, 512)
         first_passes(3, "o0", start=True)
         cast("31", "V", 0, 256)
-        cast("31", "S", 256, 512)
+        cast("31", "S", 320, 512, into=(256, 512))
+        cast("31", "V", 256, 320, into=(256, 512))
         regroup(2, inside=("31", 0))
         first_passes(3, "p0 p1")
         quant("31", 0, 256)
@@ -365,21 +366,22 @@ def tile_moe_duo_silu_kernel(
         quant("31", 256, 512)
         first_passes(3, "o1", c0=256, c1=512, part=True, stop=True)
         quant("h2", 0, C)
-        cast("v2", "S", 128, 256, into=(0, 256))
-        cast("v2", "V", 0, 128, into=(0, 256))
-        silu_half(3, 0, inside=("v2", 0))
+        cast("v2", "V", 0, 128)
+        cast("v2", "V", 128, 256)
+        silu_half(3, 0)
         turn(3, (0,))
         silu_half(3, 1)
         turn(3, (1,))
-        quant("v2", 0, 256)
+        quant("v2", 0, 128)
+        quant("v2", 128, 256)
         cast("v3", "V", 0, 256)
         regroup(3)
         second_product(2, 4, (0,))
         second_product(2, 5, (1,))
         quant("v3", 0, 256)
         gate_y(2, 1, over="rawv3_0")
-        quant("h3", 0, C)
-        copy_y(2, 0, over=("rawv2_0", 0))
+        quant("h3", 0, C, codes_over=("rawv3_0", 2048))
+        copy_y(2, 0, over=("rawv3_0", 1024))
         second_product(3, 6, (0,))
         second_product(3, 7, (1,))
         scatter(2, 0, "VG")

@@ -91,9 +91,9 @@ def tile_moe_duo_silu_kernel(
                 rows = xs[r:P:32, :].bitcast(I32).rearrange("q (s n) -> q s n", s=PASSES)
                 queue.dma_start(out=rows[:, :, 0 : T // 4], in_=xs_rows[r])
 
-        def load_partner_scales(queue, rows):
+        def load_partner_scales(queue, rows, g0=0, g1=E * PASSES):
             for r in rows:
-                queue.dma_start(out=wps[r:P:32, :].bitcast(I32).rearrange("q (g n) -> q g n", g=E * PASSES), in_=wps_rows[r])
+                queue.dma_start(out=wps[r:P:32, g0 * H : g1 * H].bitcast(I32).rearrange("q (g n) -> q g n", g=g1 - g0), in_=wps_rows[r][:, g0:g1, :])
 
         def gap(count):
             places["top"] = (places["top"][0] + count, 0)
@@ -347,7 +347,6 @@ def tile_moe_duo_silu_kernel(
         gate_y(1, inside=("21", 2048 - 128))
         quant("21", 0, 512)
         first_passes(2, "p0 o1 p1", stop=True)
-        keep_clock("21", 2, 1)
         scatter(1, 0, "S")
         scatter(1, 1, "V")
         cast("30", "S", 320, 512, into=(0, 512))

from contextlib import ExitStack

import concourse.mybir as mybir
from concourse.masks import make_identity

K, T, E, C, H, N = 1024, 512, 4, 128, 512, 256
FLOPS = 2 * E * C * (2 * K * H + H * N)

F32 = mybir.dt.float32
BF16 = mybir.dt.bfloat16
I32 = mybir.dt.int32
U32 = mybir.dt.uint32
U16 = mybir.dt.uint16
U8 = mybir.dt.uint8
FP8X4 = mybir.dt.float8_e4m3fn_x4
FP4X4 = mybir.dt.float4_e2m1fn_x4
COPY = mybir.ActivationFunctionType.Copy
SILU = mybir.ActivationFunctionType.Silu
MULT = mybir.AluOpType.mult

P = 128
PACK = 4
K_PASS = P * PACK
PASSES = K // K_PASS
WINDOW = 704
BANK = 2048
TAILS = 1


def tile_moe_duo_silu_kernel(
    tc, x_words, x_scales, w1, wp_words, wp_scales, w2, gate, offs, offs2, out
):
    nc = tc.nc
    with ExitStack() as ctx:
        keep = ctx.enter_context(tc.tile_pool(name="keep", bufs=1))
        stage = ctx.enter_context(tc.tile_pool(name="stage", bufs=1))
        psum = ctx.enter_context(tc.psum_pool(name="psum", bufs=1))

        places = {"top": (0, 0)}

        def placed(name, columns, dtype, size, over=None, room=0):
            if over is None:
                at = places["top"][0]
                room = max(room, (columns * size + 63) // 64 * 64)
                places["top"] = (at + room, 0)
            else:
                tenant, skip = over if isinstance(over, tuple) else (over, 0)
                at, room = places[tenant][0] + skip, places[tenant][1] - skip
                assert skip < 0 or columns * size <= room
            places[name] = (at, room)
            return stage.tile([P, columns], dtype, name=name, offset=at, align_bytes=64)

        xs = placed("xs", PASSES * WINDOW, U8, 1)
        wps = keep.tile([P, E * PASSES * H], U8, name="wps", align_bytes=64)
        nc.vector.memset(wps[:].bitcast(I32), 0)
        nc.vector.memset(xs[:].bitcast(I32), 0)
        warm = keep.tile([P, 1], F32, name="warm")
        nc.vector.memset(warm[:], 0.0)
        ident = keep.tile([P, P], F32, name="ident")
        make_identity(nc, ident[:])

        tok_list = keep.tile([P, T // 16], U16, name="tok_list")
        par_list = keep.tile([P, T // 16], U16, name="par_list")
        xw = [placed("xw%d" % s, WINDOW, I32, 4) for s in range(PASSES)]
        for s in range(TAILS):
            nc.vector.memset(xw[s][:, T:WINDOW], 0)
        result = [keep.tile([P, T], F32, name="result%d" % b) for b in range(N // P)]
        xs_rows = x_scales.bitcast(I32).rearrange("s (q r) n -> r q s n", r=4)
        wps_rows = wp_scales.bitcast(I32).rearrange("e s (q r) n -> r q (e s) n", r=4)
        gate_cols = keep.tile([P, PACK], F32, name="gate_cols")

        raw = {}
        flat = {}
        wpw = {}
        gates = {}
        gathered = {}
        staged = {}
        codes = {}
        scales = {}
        accs = {}
        hrows = {}
        turns = {}
        ys = {}
        y_sb = {}

        def load_x(s):
            nc.sync.dma_start(out=xw[s][:, 0:T], in_=x_words[s].rearrange("p t d -> p (t d)").bitcast(I32))

        def load_token_scales(queue):
            for r in range(4):
                rows = xs[r:P:32, :].bitcast(I32).rearrange("q (s n) -> q s n", s=PASSES)
                queue.dma_start(out=rows[:, :, 0 : T // 4], in_=xs_rows[r])

        def load_partner_scales(queue, rows, g0=0, g1=E * PASSES):
            for r in rows:
                queue.dma_start(out=wps[r:P:32, g0 * H : g1 * H].bitcast(I32).rearrange("q (g n) -> q g n", g=g1 - g0), in_=wps_rows[r][:, g0:g1, :])

        def gap(count):
            places["top"] = (places["top"][0] + count, 0)

        def load_rows(key, rows, c0, c1, room, pad, over, lead):
            flat[key] = placed("raw%s_%d" % (key, c0), lead + PACK * (c1 - c0) + pad, F32, 4, over, room)
            flat["%s_%d" % (key, c0)] = flat[key]
            tile = flat[key][:, lead : lead + PACK * (c1 - c0)].rearrange("p (j w) -> p j w", j=PACK)
            nc.sync.dma_start(out=tile, in_=rows[:, c0:c1].rearrange("(p j) w -> p j w", j=PACK))
            raw.setdefault(key, []).append((c0, c1, tile))

        def load_w1(e, s, c0=0, c1=H, room=0, pad=0, over=None, lead=0):
            load_rows("%d%d" % (e, s), w1[e, s * K_PASS : (s + 1) * K_PASS, :], c0, c1, room, pad, over, lead)

        def load_w2(e, c0=0, c1=N, room=0, pad=0, over=None, lead=0):
            load_rows("v%d" % e, w2[e], c0, c1, room, pad, over, lead)

        def load_wp(e0, e1):
            tile = placed("wpw%d" % e0, (e1 - e0) * PASSES * 2 * H, U8, 1)
            nc.sync.dma_start(
                out=tile[:].bitcast(I32).rearrange("p (g n) -> p g n", g=(e1 - e0) * PASSES),
                in_=wp_words[e0:e1].bitcast(I32).rearrange("e s p n -> p (e s) n"),
            )
            for e in range(e0, e1):
                for s in range(PASSES):
                    g = (e - e0) * PASSES + s
                    wpw[(e, s)] = tile[:, g * 2 * H : (g + 1) * 2 * H]

        def load_gate_row(queue):
            queue.dma_start(out=gate_cols[:], in_=gate[0].rearrange("(p j) -> p j", j=PACK))

        def spread_gate(rooms, bank=6):
            spread = psum.tile([P, PACK, P], F32, name="spread", offset=BANK * bank)
            for j in range(PACK):
                nc.tensor.transpose(spread[:, j, :], gate_cols[:, j : j + 1].to_broadcast([P, P]), ident[:])
            if rooms is None:
                whole = placed("gate_all", E * C, F32, 4)
                nc.scalar.copy(out=whole[:].rearrange("p (n j) -> p n j", j=PACK), in_=spread[:].rearrange("p j n -> p n j"))
                for e in range(E):
                    gates[e] = whole[:, e * C : (e + 1) * C]
                return
            for e in range(E):
                gates[e] = placed("gate%d" % e, C, F32, 4, None, rooms[e])
                quarter = slice(e * C // PACK, (e + 1) * C // PACK)
                nc.scalar.copy(out=gates[e][:].rearrange("p (n j) -> p n j", j=PACK), in_=spread[:, :, quarter].rearrange("p j n -> p n j"))

        def gather(kind, s, first=0, count=E * C, over=None):
            dtype = U32 if kind[1] == "w" else U8
            width = WINDOW if count == E * C else T
            tile = placed("%s%d_%d" % (kind, s, first), count, dtype, 4 if kind[1] == "w" else 1, over)
            offsets = (tok_list if kind[0] == "t" else par_list)[:, first // 16 : (first + count) // 16]
            window = xw[s][:, 0:width].bitcast(U32) if kind[1] == "w" else xs[:, s * WINDOW : s * WINDOW + width]
            nc.vector.tensor_copy(tile[:], window.indirect(offsets))
            for n in range(count // C):
                gathered[(kind, s, first // C + n)] = tile[:, n * C : (n + 1) * C]

        def cast(key, engine, c0, c1, over=None, into=None, room=0):
            r0, r1, source = [piece for piece in raw[key] if piece[0] <= c0 and c1 <= piece[1]][0]
            if into is None:
                into = (c0, c1)
            if (key, into) not in staged:
                staged[(key, into)] = placed("st%s_%d" % (key, into[0]), (into[1] - into[0]) * PACK, BF16, 2, over, room)
            target = staged[(key, into)][:, (c0 - into[0]) * PACK : (c1 - into[0]) * PACK]
            copy, walk = (nc.vector.tensor_copy, 4) if engine == "V" else (nc.scalar.copy, 2)
            copy(
                out=target.rearrange("p (c i j) -> p c j i", i=walk, j=PACK),
                in_=source[:, :, c0 - r0 : c1 - r0].rearrange("p j (c i) -> p c j i", i=walk),
            )

        def quant(key, c0, c1, codes_over=None, scales_over=None, room=0, source=None):
            width = C if key[0] == "h" else N if key[0] == "v" else H
            if key not in codes:
                codes[key] = placed("codes" + key, width, U32, 4, codes_over, room)
                scales[key] = placed("scales" + key, width, U8, 1, scales_over)
            into = source or (c0, c1)
            nc.vector.quantize_mx(out=codes[key][:, c0:c1].bitcast(FP8X4), scales=scales[key][:, c0:c1], in_=staged[(key, into)][:, (c0 - into[0]) * PACK : (c1 - into[0]) * PACK])

        def first_passes(e, order, start=False, stop=False, bank=None, c0=0, c1=H, part=False):
            if start:
                accs[(e, c0)] = psum.tile([P, c1 - c0], F32, name="acc%d_%d" % (e, c0), offset=BANK * (e % 2 if bank is None else bank))
            names = order.split()
            for n, name in enumerate(names):
                s = int(name[1])
                if name[0] == "o":
                    key = "%d%d" % (e, s)
                    operands = (gathered[("tw", s, e)], gathered[("tb", s, e)], codes[key][:, c0:c1].bitcast(FP8X4), scales[key][:, c0:c1])
                else:
                    g = e * PASSES + s
                    operands = (gathered[("pw", s, e)], gathered[("pb", s, e)], wpw[(e, s)][:, 2 * c0 : 2 * c1].bitcast(FP4X4), wps[:, g * H + c0 : g * H + c1])
                nc.tensor.matmul_mx(out=accs[(e, 0)][:, c0:c1] if part else accs[(e, c0)][:], lhsT=operands[0].bitcast(FP8X4), lhsT_scale=operands[1], rhs=operands[2], rhs_scale=operands[3], start=(start and n == 0), stop=(stop and n == len(names) - 1))

        def keep_clock(key, e, passes, width=H, bank=7):
            spare = psum.tile([P, width], F32, name="spare" + key, offset=BANK * bank)
            for n in range(passes):
                nc.tensor.matmul_mx(out=spare[:], lhsT=gathered[("tw", 1, e)].bitcast(FP8X4), lhsT_scale=gathered[("tb", 1, e)], rhs=codes[key[0:2]][:, 0:width].bitcast(FP8X4), rhs_scale=scales[key[0:2]][:, 0:width], start=True, stop=True)

        def silu(e, over=None, room=0, c0=0, c1=H, inside=None):
            if inside is not None:
                hrows[e] = flat[inside[0]][:, inside[1] : inside[1] + H // 2].bitcast(BF16)
            elif e not in hrows:
                hrows[e] = placed("hrows%d" % e, H, BF16, 2, over, room)[:]
            target = hrows[e].rearrange("c (u p d) -> c u p d", u=2, d=2)[:, :, c0 // PACK : c1 // PACK, :]
            nc.scalar.activation(out=target, in_=accs[(e, c0)][:].rearrange("c (p u d) -> c u p d", u=2, d=2), func=SILU)

        def silu_half(e, u, over=None, room=0, inside=None):
            if inside is not None:
                hrows[e] = flat[inside[0]][:, inside[1] : inside[1] + H // 2].bitcast(BF16)
            elif e not in hrows:
                hrows[e] = placed("hrows%d" % e, H, BF16, 2, over, room)[:]
            target = hrows[e].rearrange("c (u p d) -> c u p d", u=2, d=2)[:, u, :, :]
            nc.scalar.activation(out=target, in_=accs[(e, 0)][:].rearrange("c (p u d) -> c u p d", u=2, d=2)[:, u, :, :], func=SILU)

        def turn(e, halves=(0, 1)):
            if e not in turns:
                turns[e] = psum.tile([P, 2, C], F32, name="turned%d" % e, offset=BANK * (2 + e % 2))
            pairs = hrows[e].bitcast(F32)
            for u in halves:
                nc.tensor.transpose(turns[e][:, u, :], pairs[:, u * P : (u + 1) * P], ident[:])

        def regroup(e, over=None, room=0, engine="S", inside=None):
            if inside is not None:
                grouped = flat[inside[0]][:, inside[1] : inside[1] + C * PACK // 2].bitcast(BF16)
            else:
                grouped = placed("hg%d" % e, C * PACK, BF16, 2, over, room)[:]
            copy = nc.vector.tensor_copy if engine == "V" else nc.scalar.copy
            copy(out=grouped.bitcast(F32).rearrange("p (c u) -> p c u", u=2), in_=turns[e][:].rearrange("p u c -> p c u"))
            staged[("h%d" % e, (0, C))] = grouped

        def second_product(e, bank, blocks=(0, 1)):
            y = psum.tile([P, len(blocks), C], F32, name="y%d_%d" % (e, blocks[0]), offset=BANK * bank)
            v, h = "v%d" % e, "h%d" % e
            for n, b in enumerate(blocks):
                cols = slice(b * P, (b + 1) * P)
                nc.tensor.matmul_mx(out=y[:, n, :], lhsT=codes[v][:, cols].bitcast(FP8X4), lhsT_scale=scales[v][:, cols], rhs=codes[h][:].bitcast(FP8X4), rhs_scale=scales[h][:], start=True, stop=True)
                ys[(e, b)] = y[:, n, :]
            ys[e] = y

        def pair_y(e, over=None):
            both = placed("ysb%d" % e, N // P * C, F32, 4, over)
            y_sb[(e, 0)] = both[:, 0:C]
            y_sb[(e, 1)] = both[:, C : 2 * C]

        def copy_y(e, b, over=None, room=0, inside=None):
            if inside is not None:
                y_sb[(e, b)] = flat[inside[0]][:, inside[1] : inside[1] + C]
            elif (e, b) not in y_sb:
                y_sb[(e, b)] = placed("ysb%d_%d" % (e, b), C, F32, 4, over, room)[:]
            nc.scalar.copy(out=y_sb[(e, b)], in_=ys[(e, b)])

        def gate_y(e, b=None, over=None, room=0, inside=None):
            if b is None:
                if inside is not None:
                    both = flat[inside[0]][:, inside[1] : inside[1] + N // P * C]
                else:
                    both = placed("ysb%d" % e, N // P * C, F32, 4, over, room)[:]
                nc.vector.tensor_tensor(both.rearrange("p (b c) -> p b c", b=N // P), ys[e][:], gates[e][:].unsqueeze(1).to_broadcast([P, N // P, C]), MULT)
                y_sb[(e, 0)] = both[:, 0:C]
                y_sb[(e, 1)] = both[:, C : 2 * C]
            else:
                if inside is not None:
                    y_sb[(e, b)] = flat[inside[0]][:, inside[1] : inside[1] + C]
                elif (e, b) not in y_sb:
                    y_sb[(e, b)] = placed("ysb%d_%d" % (e, b), C, F32, 4, over, room)[:]
                nc.vector.tensor_tensor(y_sb[(e, b)], ys[(e, b)], gates[e][:], MULT)

        def scatter(e, b, engine):
            window = result[b][:].indirect(tok_list[:, e * C // 16 : (e + 1) * C // 16])
            if engine == "S":
                nc.scalar.activation(window, y_sb[(e, b)], COPY)
            elif engine == "V":
                nc.vector.tensor_copy(window, y_sb[(e, b)])
            else:
                nc.vector.tensor_tensor(window, y_sb[(e, b)], gates[e][:], MULT)

        def store(b, queue=nc.sync):
            queue.dma_start(out=out[b * P : (b + 1) * P, :], in_=result[b][:])

        nc.scalar.activation(out=warm[:], in_=warm[:], func=SILU)
        load_partner_scales(nc.gpsimd, (0, 1))
        nc.sync.dma_start(tok_list[:], offs)
        load_x(0)
        nc.sync.dma_start(par_list[:], offs2)
        load_w1(0, 0)
        load_token_scales(nc.sync)
        load_x(1)
        load_gate_row(nc.sync)
        load_w1(0, 1)
        load_partner_scales(nc.sync, (2, 3))
        load_wp(0, 1)
        load_w1(1, 0, lead=128)
        load_w1(1, 1)
        load_wp(1, 2)
        load_w2(0, lead=128)
        load_w1(2, 0, lead=240)
        load_w2(1)
        load_w1(2, 1, pad=128)
        load_wp(2, 3)
        load_w1(3, 0)
        load_w1(3, 1)
        load_wp(3, 4)
        load_w2(2)
        load_w2(3)
        gather("tw", 0)
        gather("pw", 0)
        gather("pb", 0)
        gather("tb", 0)
        gather("pb", 1)
        gather("tb", 1)
        gather("tw", 1, 0, 256)
        gather("pw", 1, 0, 256)
        cast("00", "S", 0, 512)
        spread_gate(None)
        quant("00", 0, 512, scales_over="xs")
        cast("01", "S", 0, 512)
        quant("01", 0, 512)
        first_passes(0, "p0 p1 o0 o1", start=True, stop=True)
        cast("10", "S", 128, 512, into=(0, 512))
        cast("10", "V", 0, 128, into=(0, 512))
        silu(0, inside=("10", 0))
        turn(0)
        gather("tw", 1, 256, 256, over="st01_0")
        quant("10", 0, 512)
        first_passes(1, "o0", start=True)
        gather("pw", 1, 256, 256, over="st10_0")
        cast("11", "V", 0, 256, into=(0, 512))
        cast("11", "S", 256, 512, into=(0, 512))
        quant("11", 0, 512)
        regroup(0, inside=("11", 0))
        first_passes(1, "p0 p1 o1", stop=True)
        quant("h0", 0, C)
        cast("v0", "S", 128, 256, into=(0, 256))
        cast("v0", "V", 0, 128, into=(0, 256))
        silu(1, inside=("v0", 0))
        quant("v0", 0, 256)
        second_product(0, 4)
        turn(1)
        cast("20", "S", 320, 512, into=(0, 512))
        cast("20", "V", 0, 320, into=(0, 512))
        gate_y(0, inside=("20", 0))
        regroup(1, inside=("20", 256))
        quant("20", 0, 512)
        first_passes(2, "o0", start=True)
        scatter(0, 0, "S")
        scatter(0, 1, "S")
        cast("v1", "V", 0, 256)
        quant("h1", 0, C)
        quant("v1", 0, 256)
        second_product(1, 5)
        cast("21", "S", 384, 512, into=(0, 512))
        cast("21", "V", 0, 384, into=(0, 512))
        gate_y(1, inside=("21", 2048 - 128))
        quant("21", 0, 512)
        first_passes(2, "p0 o1 p1", stop=True)
        scatter(1, 0, "S")
        scatter(1, 1, "V")
        cast("30", "S", 320, 512, into=(0, 512))
        cast("30", "V", 0, 320, into=(0, 512))
        silu(2, inside=("30", 0))
        turn(2)
        quant("30", 0, 512)
        first_passes(3, "o0", start=True)
        cast("31", "V", 0, 256)
        cast("31", "S", 320, 512, into=(256, 512))
        cast("31", "V", 256, 320, into=(256, 512))
        regroup(2, inside=("31", 0))
        first_passes(3, "p0 p1")
        quant("31", 0, 256)
        first_passes(3, "o1", c0=0, c1=256, part=True)
        quant("31", 256, 512)
        first_passes(3, "o1", c0=256, c1=512, part=True, stop=True)
        quant("h2", 0, C)
        cast("v2", "V", 0, 128)
        cast("v2", "V", 128, 256)
        silu_half(3, 0)
        turn(3, (0,))
        silu_half(3, 1)
        turn(3, (1,))
        quant("v2", 0, 128)
        quant("v2", 128, 256)
        cast("v3", "V", 0, 256)
        regroup(3)
        second_product(2, 4, (0,))
        second_product(2, 5, (1,))
        quant("v3", 0, 256)
        gate_y(2, 1, over="rawv3_0")
        quant("h3", 0, C, codes_over=("rawv3_0", 2048))
        copy_y(2, 0, over=("rawv3_0", 1024))
        second_product(3, 6, (0,))
        second_product(3, 7, (1,))
        scatter(2, 0, "VG")
        scatter(2, 1, "S")
        copy_y(3, 0)
        gate_y(3, 1)
        scatter(3, 0, "VG")
        store(0)
        scatter(3, 1, "S")
        store(1)
